import numpy as np, ml_dtypes
CORES = [10,34,74,98]
N = 4
BF = ml_dtypes.bfloat16
def gentries(a):
    return np.ascontiguousarray(a.reshape(8, 16, -1).transpose(0, 2, 1)).reshape(8, -1)
def gtable(e):
    e = np.asarray(e); return np.ascontiguousarray(e.reshape(8, -1, 16).transpose(0, 2, 1)).reshape(128, -1).astype(np.int32)
H, W, P, F, S, R, CAP = 32, 32, 1024, 5, 5, 6, 256
def near(rng, e):
    c = 2 + np.arange(F) + np.add.accumulate(e, axis=-1); n = np.concatenate([np.zeros((N, 8, 1), np.int64), np.ones((N, 8, 1), np.int64), c], axis=-1)
    j = np.maximum(np.arange(F) + 1 - rng.integers(0, 3, e.shape), 0)
    return np.minimum(c - np.take_along_axis(n, j, -1), R)
def near3(rng, e):
    return np.stack([near(rng, e) for k in range(3)], axis=-1)
def parts(rng):
    e = rng.choice(np.array([0, 0, 0, 1, 1, 2]), (N, 8, F)); op = rng.choice(np.array([0, 0, 1, 1, 2]), (N, 8, F))
    rel = np.where(rng.random((N, 8, F, 3)) < 0.6, near3(rng, e), rng.integers(1, R + 1, (N, 8, F, 3)))
    sh = rng.choice(np.array([0.0, 0.1, 0.45]), (N, 8, F, 1)); sd = rng.choice(np.array([0.2, 0.35, 0.5]), (N, 8, F, 1)); z = (N, 8, F, P)
    ia = np.where(rng.random(z) < sh, S, rng.integers(0, S, z)); ib = np.where(rng.random(z) < sh, S, rng.integers(0, S, z))
    ia = np.where(rng.random(z) < sd, S + 1, ia); z = (N, 8, F, 2, P); b = np.arange(P)
    vy = np.where(rng.random(z) < 0.15, rng.integers(-H, H + 1, z), rng.integers(0, H, z) - b // W)
    vx = np.where(rng.random(z) < 0.15, rng.integers(-W, W + 1, z), rng.integers(0, W, z) - b % W)
    z = (N, 8, 16, F, P); res = np.where(rng.random(z) < 0.05, rng.integers(-255, 256, z), rng.integers(-48, 49, z))
    return e, op, rel, ia, ib, vy, vx, res, rng.integers(0, 256, (N, 8, 16, 2, P))
def keep(rng, ia, ib, top):
    w = np.concatenate([ia == S, (ib == S) & (ia <= S)], axis=-1); o = np.argsort(rng.random(w.shape), axis=-1)
    s = np.take_along_axis(w, o, -1); over = s & (np.add.accumulate(s.astype(np.int64), axis=-1) > CAP)
    cut = np.zeros(w.shape, bool); np.put_along_axis(cut, o, over, -1); new = rng.integers(0, top, w.shape)
    return np.where(cut[..., :P], new[..., :P], ia), np.where(cut[..., P:], new[..., P:], ib)
def gts(a):
    return np.stack([gtable(np.ascontiguousarray(v).reshape(8, -1)) for v in a])
def pack(rng, e, op, rel, ia, ib, vy, vx, res, pic, top=S):
    ia, ib = keep(rng, ia, ib, top)
    return {"res": np.ascontiguousarray(res).reshape(N, 128, F * P).astype(np.float32).astype(BF), "pic0": np.ascontiguousarray(pic).reshape(N, 128, 2 * P).astype(np.float32).astype(BF),
            "ia": gts(ia), "ib": gts(ib), "vy": gts(vy), "vx": gts(vx), "gaps": e.astype(np.int32), "cmd": op.astype(np.int32), "rel": np.ascontiguousarray(rel).reshape(N, 8, 3 * F).astype(np.int32)}
def setup_inputs(rng):
    return pack(rng, *parts(rng))
def setup_inputs_spread(rng):
    e, op, rel, ia, ib, vy, vx, res, pic = parts(rng)
    res = np.clip(np.rint((2 * rng.random(res.shape) - 1) * np.exp2(8 * rng.random((N, 8, 1, F, P)))), -255, 255).astype(np.int64)
    pic = np.minimum((rng.random(pic.shape) * np.exp2(8 * rng.random((N, 8, 1, 2, P)))).astype(np.int64), 255); pic = np.where(rng.random((N, 8, 16, 1, P)) < 0.5, pic, 255 - pic)
    big = rng.random((N, 8, F, 2, P))
    vy = np.where(big < 0.5, vy, np.rint((2 * rng.random(vy.shape) - 1) * H * np.exp2(-6 * rng.random(vy.shape))).astype(np.int64))
    vx = np.where(big < 0.5, vx, np.rint((2 * rng.random(vx.shape) - 1) * W * np.exp2(-6 * rng.random(vx.shape))).astype(np.int64))
    return pack(rng, e, op, rel, ia, ib, vy, vx, res, pic)
def setup_inputs_ends(rng):
    e, op, rel, ia, ib, vy, vx, res, pic = parts(rng); z = ia.shape
    e = np.where(rng.random(e.shape) < 0.35, 2, 0); op = rng.choice(np.array([0, 0, 2, 2, 1]), e.shape); rel = np.where(rng.random(rel.shape) < 0.5, 1, R)
    e[:, 0, 1] = 2; e[:, 0, 2] = 0; op[:, 0, 2] = 2; op[:, 0, 1] = 0
    ia = np.where(rng.random(z) < 0.15, rng.integers(0, S + 1, z), np.where(rng.random(z) < 0.5, S + 1, 0)); ib = np.where(rng.random(z) < 0.5, S, 0)
    vy = np.where(rng.random(vy.shape) < 0.2, vy, np.where(rng.random(vy.shape) < 0.5, H, -H)); vx = np.where(rng.random(vx.shape) < 0.2, vx, np.where(rng.random(vx.shape) < 0.5, W, -W))
    res = np.where(rng.random(res.shape) < 0.65, np.where(rng.random(res.shape) < 0.5, 255, -255), rng.integers(-64, 65, res.shape)); pic = np.where(rng.random(pic.shape) < 0.5, 255, 0)
    e[:, 6:] = 0; op[:, 6:] = 0; rel[:, 6:, :, 1:] = 1
    ia[:, 6:, :, P - 1] = 0; ib[:, 6:, :, P - 1] = 0; vy[:, 6:, :, :, P - 1] = H; vx[:, 6:, :, :, P - 1] = W
    pic[:, 6, :, :, P - 1] = 0; pic[:, 7, :, :, P - 1] = 255
    res[:, 6, :, :, P - 1] = np.tile(np.array([0, 1, 255, -255]), 4)[:, None]; res[:, 7, :, :, P - 1] = np.tile(np.array([0, -1, -255, 255]), 4)[:, None]
    return pack(rng, e, op, rel, ia, ib, vy, vx, res, pic, 1)
def roles():
    return (np.arange(8)[None, :] + np.arange(N)[:, None]) % 8
def setup_inputs_corners(rng):
    e, op, rel, ia, ib, vy, vx, res, pic = parts(rng); k = roles(); b = np.arange(P)
    e[k == 0] = 0; op[k == 0] = 0; e[k == 1] = 2; op[k == 2] = 1; e[k == 3] = 0; op[k == 3] = 2
    nr = near3(rng, e); m = (k == 1) | (k == 2) | (k == 4); rel[m] = nr[m]
    rel[..., 2] = np.where(rng.random((N, 8, F)) < 0.3, rel[..., 1], rel[..., 2]); rel[..., 0] = np.where(rng.random((N, 8, F)) < 0.3, rel[..., 1], rel[..., 0])
    x = rel[..., 0]; x = np.where((k == 3)[..., None], rng.integers(1, 3, x.shape), x); rel[..., 0] = x
    m = (k == 0)[..., None, None]; ia = np.where(m & (ia > S), rng.integers(0, S, ia.shape), ia)
    m = (k == 4)[..., None, None]; late = np.arange(F)[:, None] >= 1
    ia = np.where(m & late, S + 1, np.where(m, rng.integers(0, S, ia.shape), ia))
    m = (k == 5)[..., None, None, None]; z = (N, 8, F, 2, 1)
    vy = np.where(m, rng.choice(np.array([0, H - 1]), z) - b // W, vy); vx = np.where(m, rng.choice(np.array([0, W - 1]), z) - b % W, vx)
    m = (k == 5)[..., None, None]; ib = np.where(m, S, ib); ia = np.where(m, rng.integers(0, S, ia.shape), ia)
    m = (k == 6)[..., None, None, None]; vy = np.where(m, np.where(rng.random(vy.shape) < 0.5, H, -H), vy); vx = np.where(m, np.where(rng.random(vx.shape) < 0.5, W, -W), vx)
    m = (k == 6)[..., None, None]; ia = np.where(m & (ia == S), 0, ia); ib = np.where(m & (ib == S), S - 1, ib)
    m = (k == 7)[..., None, None]; n = CAP - (np.arange(F)[:, None] & 1)
    ia = np.where(m, np.where(b < n, S, rng.integers(0, S, ia.shape)), ia); ib = np.where(m, rng.integers(0, S, ib.shape), ib)
    return pack(rng, e, op, rel, ia, ib, vy, vx, res, pic)
def setup_inputs_calm(rng):
    e, op, rel, ia, ib, vy, vx, res, pic = parts(rng); k = roles(); e0, op0 = e, op; odd = (np.arange(N)[:, None] & 1) == 1
    e = np.zeros(e.shape, np.int64); op = np.zeros(op.shape, np.int64); x = rng.integers(1, 4, e.shape)
    op[k < 2] = 2; x[k == 0] = 1; x[k == 1] = 2
    e[k == 3, 0] = 1; op[k == 3, 0] = 1; x[k == 3, 0] = 4; op[k == 3, F - 1] = 2; e[k == 4, 0] = 2
    e[k == 5, 0] = 2; e[k == 5, 1] = 2; op[k == 5, 2:] = 2
    op[k == 6] = 1; x[k == 6] = 1; e[k == 6, 1] = 1
    m = (k == 6) & odd; e[m] = 0; e[m, 0] = min(S - F, 2); x[m, :F - 1] = 2; e[m, F - 1] = 2
    for t, (o, v) in enumerate(((1, 1), (1, 2), (2, 3))):
        op[k == 2, t] = o; x[k == 2, t] = v
    m = (k == 2) & odd
    for t, (o, v) in enumerate(((1, 1), (2, 2), (0, 3))):
        op[m, t] = o; x[m, t] = v
    e[k == 7] = e0[k == 7]; op[k == 7] = op0[k == 7]
    rel = np.where(rng.random(rel.shape) < 0.7, near3(rng, e), rng.integers(1, 4, rel.shape)); rel[..., 0] = x
    rel[k == 3, 1, 1:] = 2; rel[k == 6, F - 1, 1:] = rng.integers(2, R + 1, (N, 2))
    vy = rng.integers(-3, 4, vy.shape); vx = rng.integers(-3, 4, vx.shape)
    return pack(rng, e, op, rel, ia, ib, vy, vx, res, pic)
def check_inputs(d):
    bad = []
    for k, lo, hi in (("res", -255, 255), ("pic0", 0, 255), ("ia", 0, S + 1), ("ib", 0, S), ("vy", -H, H), ("vx", -W, W), ("gaps", 0, 2), ("cmd", 0, 2), ("rel", 1, R)):
        v = np.asarray(d[k]).astype(np.float64)
        if not (np.min(v) >= lo and np.max(v) <= hi): bad.append("range of " + k)
        if np.any(v != np.rint(v)): bad.append("whole numbers in " + k)
    a, b = [np.stack([gentries(v) for v in np.asarray(d[k])]).reshape(N, 8, F, P) for k in ("ia", "ib")]
    if np.max(np.sum((a == S).astype(np.int64) + ((b == S) & (a <= S)), axis=-1)) > CAP: bad.append("view blocks of a frame and group")
    return bad
def insert(h, n):
    if len(h) == S: del h[min(k for k in h if not h[k])]
    h[n] = False
def step(h, nxt, cur, first, e, op, x, m0, m1):
    if not first: insert(h, cur)
    for k in range(e): insert(h, nxt + k)
    cur = nxt + e
    if op == 1 and cur - x in h: h[cur - x] = True
    if op == 2 and cur - x in h and len(h) > 2: del h[cur - x]
    key = {n: (63 - n if h[n] else 64 + n) + 128 * (n == cur - m0) + 256 * (n == cur - m1) for n in h}
    return sorted(h, key=lambda n: -key[n]), cur + 1, cur
def reference(res, pic0, ia, ib, vy, vx, gaps, cmd, rel):
    M = 3 * F + 2
    rs = res.astype(np.float32).astype(np.int64).reshape(N, 8, 16, F, P); st = pic0.astype(np.float32).astype(np.int64).reshape(N, 8, 16, 2, P)
    la, lb = [np.stack([gentries(v) for v in a]).astype(np.int64).reshape(N, 8, F, P) for a in (ia, ib)]
    ly, lx = [np.stack([gentries(v) for v in a]).astype(np.int64).reshape(N, 8, F, 2, P) for a in (vy, vx)]
    by = np.arange(P) // W; bx = np.arange(P) % W; g8 = np.arange(8); y = np.zeros((N, 8, 16, F, P), np.int64)
    pics = np.full((N, 8, 16, M + 2, P), 128, np.int32); pics[:, :, :, 0:2] = st
    mq = np.full((N, 8, M, P), -1, np.int64); my = np.zeros((N, 8, M, P), np.int64); mx = np.zeros((N, 8, M, P), np.int64)
    held = [[{0: False, 1: False} for g in range(8)] for r in range(N)]; nxt = np.full((N, 8), 2); cur = np.zeros((N, 8), np.int64)
    for f in range(F):
        for r in range(N):
            q = (r - 1) % N; src = (g8 + f) % 8
            pics[r, :, :, M + 1] = st[q, src, :, 1] if f == 0 else y[q, src, :, f - 1]
            A = np.full((8, S + 1), M, np.int64); A[:, S] = M + 1; here = np.zeros((8, M), bool)
            for g in range(8):
                lst, a, b = step(held[r][g], int(nxt[r, g]), int(cur[r, g]), f == 0, int(gaps[r, g, f]), int(cmd[r, g, f]), int(rel[r, g, 3 * f]), int(rel[r, g, 3 * f + 1]), int(rel[r, g, 3 * f + 2]))
                nxt[r, g] = a; cur[r, g] = b; A[g, :len(lst)] = lst; here[g, lst] = True
            B = np.array(A); B[:, 0] = A[:, 1]; B[:, 1] = A[:, 0]; c = B[:, 0]
            ja = la[r, :, f]; direct = ja == S + 1
            na = np.take_along_axis(A, np.where(direct, 0, ja), 1); nb = np.take_along_axis(B, lb[r, :, f], 1)
            n = mq[r, g8, c]; wy = my[r, g8, c]; wx = mx[r, g8, c]; ay = wy >> 1; ax = wx >> 1
            ok = (n >= 0) & np.take_along_axis(here, np.maximum(n, 0), 1)
            na = np.where(direct, np.where(ok, n, A[:, :1]), na); nb = np.where(direct, c[:, None], nb)
            uy = np.where(direct, ay, ly[r, :, f, 0]); ux = np.where(direct, ax, lx[r, :, f, 0])
            ty = np.where(direct, ay - wy, ly[r, :, f, 1]); tx = np.where(direct, ax - wx, lx[r, :, f, 1])
            flat = pics[r].reshape(8, 16, (M + 2) * P)
            i = na * P + np.clip(by + uy, 0, H - 1) * W + np.clip(bx + ux, 0, W - 1); j = nb * P + np.clip(by + ty, 0, H - 1) * W + np.clip(bx + tx, 0, W - 1)
            s = np.take_along_axis(flat, i[:, None, :], 2) + np.take_along_axis(flat, j[:, None, :], 2) + 1
            v = np.clip((s >> 1) + rs[r, :, :, f], 0, 255)
            y[r, :, :, f] = v
            for g in range(8):
                k = cur[r, g]; pics[r, g, :, k] = v[g]; mq[r, g, k] = np.where(na[g] < M, na[g], -1); my[r, g, k] = uy[g]; mx[r, g, k] = ux[g]
    return {"y": y.reshape(N, 128, F * P).astype(np.float32).astype(BF)}

@@ -1,0 +1,510 @@
+import math
+from concourse.mybir import AluOpType as OP, ActivationFunctionType as AF
+
+F, P = 5, 1024
+BF, F32, I32, U16 = "bfloat16", "float32", "int32", "uint16"
+CH = [0, 256, 448, 800, 1024]
+SENDS = {1: (0, 448), 3: (448, 1024)}
+VUNITS = [(0, 0, 256), (0, 256, 448), (0, 448, 544)]
+SUNITS = [(1, 0, 256), (1, 256, 448), (0, 544, 800), (1, 448, 800), (0, 800, 1024), (1, 800, 1024)]
+PQ = [(0, 1), (0, 1), (0, 1), (0, 1)]
+MAGIC = 12582912.0
+LN16 = math.log(16.0)
+
+
+def _sb(n, d):
+    return ("sbuf", [128, n] if isinstance(n, int) else [128] + n, d)
+
+
+SCRATCH = {
+    "win": _sb(12 * P, BF), "rs": _sb(F * P, BF), "sb": _sb(F * P, BF), "pq": _sb(2 * P, BF), "cr": _sb(P, BF),
+    "ctl": _sb(26, I32), "ctlb": _sb(26, BF),
+    "ja": _sb([F, 64], I32), "jb": _sb([F, 64], I32), "wy": _sb(640, I32), "wx": _sb(640, I32),
+    "jaf": _sb([F, 64], BF), "kq": _sb([F, 64], BF), "d16": _sb([F, 64], BF), "d3": _sb([F, 192], BF), "nd2": _sb([F, 128], BF),
+    "rawp": _sb([F, 64], BF), "rawq": _sb([F, 64], BF), "pw": _sb(640, BF),
+    "pcol": _sb(4, I32), "ncol": _sb(4, I32), "col": _sb(16, F32), "ci": _sb(8, F32), "one": _sb(8, BF), "arow": _sb(20, F32),
+    "repi": _sb(128, BF), "rep": _sb(128, BF), "blk": _sb(128, BF), "alls": _sb(128, BF), "ge": _sb(128, BF), "le": _sb(128, BF),
+    "a15": _sb(128, BF), "an15": _sb(128, BF), "dif": _sb(256, BF), "wide": _sb(256, BF), "half": _sb(256, BF),
+    "i32": _sb(128, BF), "i1k": _sb(128, BF), "in16k": _sb(128, BF), "i16th": _sb(128, BF), "quar": _sb(128, BF),
+    "base": _sb(256, BF), "mio": _sb(12, F32), "moff": _sb(48, U16), "mst": _sb(7 * 256, BF),
+    "c": _sb(128, F32), "cq": _sb(24, BF), "st": _sb(16, BF), "sm": _sb(32, F32), "rk": _sb(32, BF), "pb": _sb(40, F32),
+    "tv": _sb(32, BF), "tt": _sb(20, F32),
+    "ti": _sb(192, I32), "ta": _sb(192, I32), "dg": _sb(256, BF), "de": _sb(64, BF), "cs": _sb(128, BF), "ev": _sb(512, BF),
+    "xb": _sb(192, BF), "hv": _sb(256, BF), "zz": _sb(64, BF), "nok": _sb(64, BF), "mm": _sb(64, BF), "cn": _sb(64, BF), "ef": _sb(64, BF),
+    "cb": _sb(256, BF), "off": _sb(F * 128, U16),
+}
+for _k in ("u0", "u1", "u2", "u3", "rb0", "rb1", "ix0", "ix1"):
+    SCRATCH[_k] = ("psum", [128, 512], F32)
+LOADS = ["ls1", "ls0", "lg", "lc", "lr", "lja", "ljb", "lwy0", "lwx0", "lwy1", "lwx1", "lwy2", "lwx2"] + ["lrs%d" % f for f in range(F)]
+SEMAPHORES = (["cv", "cs", "ct", "cg", "stored", "va0"] + LOADS + ["sent%d" % f for f in range(F)]
+              + ["va%d_%d" % (f, k) for f in range(1, F) for k in range(4)])
+
+
+def rank_program(g, core, T, topo):
+    rank = T.rank_of(core)
+    if rank is None:
+        return
+    nxt = T.cores[(rank + 1) % len(T.cores)]
+    rid, pid = topo.addr(nxt)[0], topo.addr(nxt)[1]
+    emask = topo.mask(core, nxt)
+    neng = len(topo.engines(core, nxt))
+    prv = T.cores[(rank - 1) % len(T.cores)]
+    narr = len(topo.engines(prv, core))
+    Q = {"v": g.vector, "s": g.scalar, "t": g.tensor, "g": g, "y": g.sync}
+    cnt = {"cv": 0, "cs": 0, "ct": 0, "cg": 0}
+    known = {e: {} for e in Q}
+    hist = {}
+
+    def need(e, tok):
+        sem, val, snap = tok
+        if known[e].get(sem, 0) >= val:
+            return
+        Q[e].wait_ge(T.sem[sem], val)
+        known[e][sem] = val
+        for k, v in snap.items():
+            if known[e].get(k, 0) < v:
+                known[e][k] = v
+
+    def order(e, outs, ins):
+        toks = {}
+        for wr, group in ((True, outs), (False, ins)):
+            for x in group:
+                for name, lo, hi in x[1]:
+                    ps = SCRATCH[name][0] == "psum"
+                    for l2, h2, w2, e2, tok in hist.get(name, []):
+                        if ps and e2 == e == "t":
+                            continue
+                        if (ps and e2 != e) or ((wr or w2) and lo < h2 and l2 < hi):
+                            if tok[0] not in toks or toks[tok[0]][1] < tok[1]:
+                                toks[tok[0]] = tok
+        for tok in sorted(toks.values(), key=lambda t: -len(t[2])):
+            need(e, tok)
+
+    def note(e, outs, ins, tok):
+        for wr, group in ((True, outs), (False, ins)):
+            for x in group:
+                for name, lo, hi in x[1]:
+                    hist.setdefault(name, []).append((lo, hi, wr, e, tok))
+
+    def run(e, outs, ins, call):
+        ins = [x for x in ins if isinstance(x, tuple)]
+        order(e, outs, ins)
+        sem = "c" + e
+        cnt[sem] += 1
+        call().then_inc(T.sem[sem], 1)
+        note(e, outs, ins, (sem, cnt[sem], dict(known[e])))
+
+    def a(name, lo, hi, step=1, parts=128):
+        ap = T[name][0:parts, lo:hi] if step == 1 else T[name][0:parts, lo:hi:step]
+        return (ap, [(name, lo, hi)])
+
+    def a3(name, lo=None, hi=None):
+        w = SCRATCH[name][1][2]
+        return (T[name][:] if lo is None else T[name][:, :, lo:hi], [(name, 0, F * w)])
+
+    def af(name, f, lo, hi):
+        w = SCRATCH[name][1][2]
+        return (T[name][:, f, lo:hi], [(name, f * w + lo, f * w + hi)])
+
+    def gi(w, o):
+        return (w[0].indirect(o[0]), w[1] + o[1])
+
+    def u(x):
+        return x[0] if isinstance(x, tuple) else x
+
+    def ts(o, i, s1, s2, op0, op1=None):
+        if op1 is None:
+            run("v", [o], [i, s1], lambda: g.vector.tensor_scalar(o[0], i[0], u(s1), None, op0))
+        else:
+            run("v", [o], [i, s1, s2], lambda: g.vector.tensor_scalar(o[0], i[0], u(s1), u(s2), op0, op1))
+
+    def tt(o, x, y, op):
+        run("v", [o], [x, y], lambda: g.vector.tensor_tensor(o[0], x[0], y[0], op))
+
+    def cp(o, i):
+        run("v", [o], [i], lambda: g.vector.tensor_copy(o[0], i[0]))
+
+    def ms(o, c):
+        run("v", [o], [], lambda: g.vector.memset(o[0], c))
+
+    def scan(o, d0, d1, init, op0, op1):
+        run("v", [o], [d0, d1, init], lambda: g.vector.tensor_tensor_scan(o[0], d0[0], d1[0], u(init), op0, op1))
+
+    def act(o, i, func=AF.Identity, bias=0.0, scale=1.0):
+        run("s", [o], [i, bias, scale], lambda: g.scalar.activation(o[0], i[0], func, bias=u(bias), scale=u(scale)))
+
+    def mm(o, l, r, start, stop):
+        run("t", [o], [l, r], lambda: g.tensor.matmul(o[0], l[0], r[0], start, stop))
+
+    def iota(o, pat, base, cm, small=True):
+        if small:
+            run("g", [o], [], lambda: g.iota(o[0], pat, base, cm, allow_small_or_imprecise_dtypes=True))
+        else:
+            run("g", [o], [], lambda: g.iota(o[0], pat, base, cm))
+
+    def load(e, o, src, sem):
+        order(e, [o], [])
+        Q[e].dma_start(o[0], src).then_inc(T.sem[sem], 16)
+        note(e, [o], [], (sem, 16, dict(known[e])))
+
+    stores = [0]
+
+    def store(lo, hi, src):
+        order("y", [], [src])
+        g.sync.dma_start(T.y[:, lo:hi], src[0]).then_inc(T.sem.stored, 16)
+        stores[0] += 16
+
+    def send(dst, src, rsem, lsem):
+        order("g", [], [src])
+        g.remote_dma(out_ap=dst[0], in_ap=src[0], remote_sem=T.sem[rsem], local_sem=T.sem[lsem], pid=pid, routing_id=rid, dma_engine_mask=emask)
+
+    def view(f, lo=0, hi=P):
+        return a("win", (4 - f) * P + lo, (4 - f) * P + hi)
+
+    note("r", [view(0)], [], ("va0", narr, {}))
+    for f in range(1, F):
+        for k, (lo, hi) in SENDS.items():
+            note("r", [view(f, lo, hi)], [], ("va%d_%d" % (f, k), narr, {}))
+
+    load("y", a("win", 7 * P, 8 * P), T.pic0[:, P:2 * P], "ls1")
+    load("s", a("ctl", 0, 5, parts=8), T.gaps[:], "lg")
+    load("s", a("ctl", 5, 10, parts=8), T.cmd[:], "lc")
+    load("s", a("ctl", 10, 25, parts=8), T.rel[:], "lr")
+    load("y", a3("ja"), T.ia[:], "lja")
+    load("y", a3("jb"), T.ib[:], "ljb")
+    load("y", a("wy", 0, 128), T.vy[:, 0:128], "lwy0")
+    load("y", a("wx", 0, 128), T.vx[:, 0:128], "lwx0")
+    load("y", a("rs", 0, P), T.res[:, 0:P], "lrs0")
+    load("y", a("win", 6 * P, 7 * P), T.pic0[:, 0:P], "ls0")
+
+    nf, n1, np1, c01 = a("col", 0, 1), a("col", 1, 2), a("col", 2, 3), a("col", 3, 4)
+    alls, ge, le, wide = a("alls", 0, 128), a("ge", 0, 128), a("le", 0, 128), a("wide", 0, 256)
+    ident = a("wide", 0, 128)
+    iota(a("pcol", 0, 1), [[0, 1]], 0, 1, False)
+    iota(a("repi", 0, 128, parts=8), [[1, 8], [0, 16]], 0, -1)
+    iota(a("blk", 0, 128), [[16, 8], [0, 16]], 0, -1)
+    iota(a("ci", 0, 6), [[1, 6]], 1, 0)
+    iota(a("dif", 0, 256), [[0, 2], [1, 128]], 0, -1)
+    ms(a("c", 0, 128), 0.0)
+    act(a("one", 0, 8), a("c", 120, 128), AF.Exp)
+    ms(a("arow", 5, 10), 0.5)
+    ms(a("arow", 10, 15), 0.0)
+    ts(a("ncol", 0, 1), a("pcol", 0, 1), 15, None, OP.bitwise_and)
+    cp(nf, a("ncol", 0, 1))
+    ms(a("quar", 0, 128), 2.0 ** -16)
+    ts(n1, nf, -1.0, 1.0, OP.mult, OP.add)
+    ts(np1, nf, 1.0, None, OP.add)
+    ts(a("rep", 0, 128, parts=8), a("repi", 0, 128, parts=8), 0.0, None, OP.is_equal)
+    ts(alls, a("blk", 0, 128), nf, 0.0, OP.add, OP.is_equal)
+    ts(c01, nf, 2.0, np1, OP.is_lt, OP.mult)
+    ms(a("win", 5 * P, 6 * P), 128.0)
+    run("g", [ge], [alls], lambda: g.affine_select(ge[0], alls[0], [[-1, 128]], OP.is_ge, 0.0, 0, 1))
+    send(view(0), a("win", 7 * P, 8 * P), "va0", "sent0")
+    run("g", [le], [alls], lambda: g.affine_select(le[0], alls[0], [[1, 128]], OP.is_ge, 0.0, 0, -1))
+    iota(a("base", 0, 128), [[0, 2], [1, 32], [0, 2]], -192, 0)
+    iota(a("base", 128, 256), [[0, 64], [16, 2]], -192, 0)
+    iota(a("mio", 0, 12), [[16, 12]], 0, 0)
+    ms(a("mst", 0, 768), 0.0)
+    ts(wide, a("dif", 0, 256), 0.0, None, OP.is_equal)
+    ms(a("mst", 768 + 192, 7 * 256), 0.0)
+    act(a("arow", 0, 5), a("ci", 0, 5), bias=0.5, scale=69905.0)
+    act(a("arow", 15, 20), a("ci", 0, 5), bias=0.5, scale=69905.0)
+    act(a("a15", 0, 128), alls, scale=15.0)
+    act(a("an15", 0, 128), alls, scale=-15.0)
+    act(a("half", 0, 256), wide, scale=0.5)
+    act(a("i16th", 0, 128), ident, scale=1.0 / 16)
+    act(a("i32", 0, 128), ident, scale=32.0)
+    act(a("i1k", 0, 128), ident, scale=1024.0)
+    act(a("in16k", 0, 128), ident, scale=-16384.0)
+
+    def later_loads(f):
+        need("y", ("sent%d" % f, neng * (len(SENDS) if f else 1), {}))
+        if f < 2:
+            lo, hi = 128 + 256 * f, 384 + 256 * f
+            load("y", a("wy", lo, hi), T.vy[:, lo:hi], "lwy%d" % (f + 1))
+            load("y", a("wx", lo, hi), T.vx[:, lo:hi], "lwx%d" % (f + 1))
+        if f < F - 1:
+            load("y", a("rs", (f + 1) * P, (f + 2) * P), T.res[:, (f + 1) * P:(f + 2) * P], "lrs%d" % (f + 1))
+    later_loads(0)
+
+    def explicit(f, k):
+        tt(ev(f, 128 * k, 128 * k + 128), a(("wy", "wx")[k], 128 * f, 128 * f + 128), af("nd2", f, 0, 128), OP.mult)
+
+    def ev(f, lo, hi):
+        return a("ev", 256 * (f & 1) + lo, 256 * (f & 1) + hi)
+
+    def coords0(f):
+        mm(a("ix0", 0, 256), ident, a("base", 0, 256), True, False)
+        mm(a("ix0", 0, 256), ident, ev(f, 0, 256), False, f == 0)
+
+    def coords(f):
+        for k, (o, i) in enumerate(((0, 0), (128, 64), (64, 128), (192, 192))):
+            mm(a("ix0", o, o + 64), ident, a("hv", i, i + 64), False, k == 3)
+        if f < F - 1:
+            mm(a("ix0", 256, 384), ident, a("hv", 0, 128), True, False)
+            mm(a("ix0", 256, 320), ident, ev(f, 0, 64), False, False)
+            mm(a("ix0", 320, 384), ident, ev(f, 128, 192), False, True)
+
+    def clamp(lo=0.0):
+        ts(a("cb", 0, 256), a("ix0", 0, 256), lo, lo + 31.0, OP.max, OP.min)
+
+    def places():
+        mm(a("ix1", 128, 256), a("i32", 0, 128), a("cb", 0, 128), True, False)
+        mm(a("ix1", 128, 256), ident, a("cb", 128, 256), False, False)
+
+    def keepw(f):
+        act(a("mst", 256 * (3 + f) + 64, 256 * (3 + f) + 192), a("ix0", 256, 384), bias=-192.0)
+
+    def preacc(f, ks):
+        s = (f + 1) % F
+        for k in ks:
+            n = CH[k + 1] - CH[k]
+            mm(a("u%d" % k, 0, n), a("wide", 16 * s, 16 * s + 128), a("rs", f * P + CH[k], f * P + CH[k + 1]), True, False)
+            mm(a("u%d" % k, 0, n), a("quar", 0, 128), a("win", 5 * P, 5 * P + n), False, False)
+
+    def look(f, k):
+        pw = a("pw", 320 * (k & 1) + 64 * f, 320 * (k & 1) + 64 * f + 64)
+        col = (0, 15, 5)[k] + f
+        ts(a("ti", 64 * k, 64 * k + 64), pw, a("tt", col, col + 1), -0.5, OP.mult, OP.add)
+
+    def c5(k, lo=0, hi=5):
+        return a("c", 8 * k + lo, 8 * k + hi)
+    cn_, tx, tc, lt, new, m0, m1, isb, nb, nm1, m64, isf, sl_, e_ = [k for k in range(14)]
+    gaps, cmd = a("rb0", 0, 5), a("rb0", 5, 10)
+    cp(a("ctlb", 0, 25, parts=8), a("ctl", 0, 25, parts=8))
+    mm(a("rb0", 0, 25), a("rep", 0, 128, parts=8), a("ctlb", 0, 25, parts=8), True, True)
+    scan(c5(cn_), gaps, a("one", 0, 5), n1, OP.add, OP.add)
+    tot0 = a("col", 4, 5)
+    ts(tot0, a("rb0", 0, 1), 2.0, None, OP.add)
+    tt(c5(tx), c5(cn_), a("rb0", 10, 25, 3), OP.is_equal)
+    ts(c5(lt), c5(cn_), 0.0, None, OP.is_gt)
+    tt(c5(tc), c5(tx), cmd, OP.mult)
+    tt(c5(new, 0, 4), c5(lt, 1, 5), c5(lt, 0, 4), OP.subtract)
+    ts(a("cq", 0, 5), c5(tc), -6.0, 14.5, OP.mult, OP.add)
+    ts(a("cq", 8, 13), c5(tc), 1.0, None, OP.is_equal)
+
+    def powers(k):
+        bank = a(("ix0", "u3")[k], 0, 320)
+        mm(bank, a("i16th", 0, 128), a3("d16"), True, False)
+        mm(bank, ident, a3(("rawp", "rawq")[k]), False, True)
+        act(a("pw", 320 * k, 320 * k + 320), bank)
+
+    def st_s(f):
+        return a("st", 2 * f, 2 * f + 1)
+
+    def st_l(f):
+        return a("st", 2 * f + 1, 2 * f + 2)
+
+    def thr_(f):
+        return a("cq", f, f + 1)
+
+    def t1_(f):
+        return a("cq", 8 + f, 9 + f)
+    ks0 = a("sm", 0, 1)
+    ts(ks0, tot0, thr_(0), t1_(0), OP.is_le, OP.subtract)
+    ts(st_l(1), c5(lt, 0, 1), t1_(0), None, OP.mult)
+    ts(st_s(1), c5(lt, 0, 1), ks0, c5(new, 0, 1), OP.mult, OP.add)
+
+    def fill1():
+        tt(c5(m0), c5(cn_), a("rb0", 11, 25, 3), OP.is_equal)
+        tt(c5(m1), c5(cn_), a("rb0", 12, 25, 3), OP.is_equal)
+        ts(c5(isf, 0, 4), c5(cn_, 0, 4), 0.0, None, OP.is_equal)
+
+    def fill2():
+        cp(a3("jaf"), a3("ja"))
+        act(a3("d16"), a3("jaf"), AF.Relu, bias=-80.0, scale=16.0)
+        act(a3("rawp"), a3("jaf"), AF.Exp, scale=-LN16)
+
+    def fill3():
+        tt(c5(isb), c5(m0), c5(m1), OP.max)
+        tt(c5(isf, 4, 8), c5(isf, 0, 4), a("ci", 2, 6), OP.mult)
+        ts(c5(nm1), c5(m1), -1.0, 1.0, OP.mult, OP.add)
+        ts(c5(nb), c5(isb), -1.0, 1.0, OP.mult, OP.add)
+        scan(c5(sl_, 0, 4), c5(isf, 4, 8), c5(isf, 4, 8), c01, OP.max, OP.max)
+        act(a3("nd2", 0, 64), a3("d16"), bias=1.0, scale=-1.0 / 16)
+        act(c5(m64), c5(m1), bias=64.0)
+
+    def fill4():
+        tt(a3("kq"), a3("jb"), a3("d16"), OP.add)
+        powers(0)
+        act(a3("rawq"), a3("kq"), AF.Exp, scale=-LN16)
+        act(a3("nd2", 64, 128), a3("d16"), bias=1.0, scale=-1.0 / 16)
+    fills = [fill1, fill2, fill3, fill4]
+    for f in range(1, F):
+        tot, cum = a("rb1", 2 * f, 2 * f + 1), a("rb1", 2 * f + 1, 2 * f + 2)
+        mm(a("rb1", 2 * f, 2 * f + 2), alls, a("st", 2 * f, 2 * f + 2), True, False)
+        mm(tot, alls, st_l(f), False, False)
+        mm(cum, ge, st_s(f), False, True)
+        fills[f - 1]()
+        s2, ks, lk = a("sm", 4 * f, 4 * f + 1), a("sm", 4 * f + 1, 4 * f + 2), a("cq", 16 + f, 17 + f)
+        ts(s2, cum, 5.0, st_s(f), OP.is_le, OP.mult)
+        ts(ks, tot, thr_(f), t1_(f), OP.is_le, OP.subtract)
+        ts(lk, tot, thr_(f), st_l(f), OP.is_le, OP.mult)
+        ts(st_s(f + 1), s2, ks, c5(new, f, f + 1), OP.mult, OP.add)
+        ts(st_l(f + 1), s2, t1_(f), lk, OP.mult, OP.add)
+
+    s3, hh = a("sm", 20, 25), a("sm", 26, 31)
+    lg = a("st", 3, 13, 2)
+    rs_, hb, rl, bb = a("rk", 0, 5), a("rk", 5, 10), a("rk", 10, 15), a("rk", 16, 21)
+    tt(s3, a("st", 2, 12, 2), c5(new), OP.subtract)
+    tt(rl, lg, c5(nb), OP.mult)
+    tt(hh, s3, lg, OP.add)
+    tt(rs_, s3, c5(nb), OP.mult)
+    tt(bb, hh, c5(isb), OP.mult)
+    mm(a("ix1", 0, 5), ge, rs_, True, True)
+    mm(a("ix1", 10, 15), alls, rs_, True, False)
+    mm(a("ix1", 10, 15), le, rl, False, True)
+    mm(a("ix1", 5, 10), alls, bb, True, True)
+    tt(hb, hh, c5(nm1), OP.mult)
+    tt(a("pb", 15, 20), hh, c5(m64), OP.mult)
+    scan(c5(e_), hh, c5(lt), 4.0, OP.add, OP.subtract)
+    powers(1)
+    tt(a("pb", 0, 15), a("rk", 0, 15), a("ix1", 0, 15), OP.mult)
+    tt(a("pb", 20, 30), a("pb", 0, 10), a("pb", 10, 20), OP.add)
+    r1 = a("pb", 32, 37)
+    tt(r1, a("pb", 20, 25), a("pb", 25, 30), OP.add)
+    sl, ee = c5(sl_, 3, 4), c5(e_, 4, 5)
+    ex, vs, ve, v1, v0 = a("tv", 24, 29), a("tv", 0, 5), a("tv", 5, 10), a("tv", 10, 15), a("tv", 16, 21)
+    act(ex, r1, AF.Exp, bias=-65.0 * LN16, scale=LN16)
+    ts(v1, r1, 66.0, sl, OP.is_equal, OP.mult)
+    ts(v0, r1, 65.0, sl, OP.is_equal, OP.mult)
+    act(a("base", 128, 256), a("base", 128, 256), bias=nf)
+    preacc(0, [0])
+    explicit(0, 0)
+    ts(vs, ex, sl, None, OP.mult)
+    ts(ve, ex, ee, None, OP.mult)
+    mm(a("rb1", 47, 52), a("a15", 0, 128), v0, True, False)
+    mm(a("rb1", 47, 52), a("an15", 0, 128), v1, False, False)
+    mm(a("rb1", 47, 52), alls, vs, False, True)
+    mm(a("rb1", 32, 47), alls, a("tv", 0, 15), True, True)
+    explicit(0, 1)
+    coords0(0)
+    tt(a("tt", 0, 20), a("rb1", 32, 52), a("arow", 0, 20), OP.add)
+    look(0, 0)
+    look(0, 1)
+    clamp(-192.0)
+    preacc(0, [1])
+    places()
+    ts(a("ta", 0, 128), a("ti", 0, 128), 15, None, OP.bitwise_and)
+    cp(a("dg", 0, 128), a("ta", 0, 128))
+    mm(a("ix1", 128, 256), a("i1k", 0, 128), a("dg", 0, 128), False, True)
+    preacc(0, [2, 3])
+    look(0, 2)
+    ts(a("mio", 0, 12), a("mio", 0, 12), nf, 1.0 / 256, OP.add, OP.mult)
+    ts(a("off", 0, 128), a("ix1", 128, 256), 33.0 * 192, None, OP.add)
+    act(a("mst", 768 + 64, 768 + 128), ev(0, 0, 64))
+    act(a("mst", 768 + 128, 768 + 192), ev(0, 128, 192))
+    act(a3("d3", 0, 64), a3("d16"), scale=1.0 / 16)
+
+    def code0():
+        ts(a("ta", 128, 192), a("ti", 128, 192), 15, None, OP.bitwise_and)
+        ts(a("de", 0, 64), a("ta", 128, 192), 16.0, 4.0, OP.mult, OP.add)
+        tt(a("mst", 256 * 3, 256 * 3 + 64), a("dg", 0, 64), a("de", 0, 64), OP.add)
+
+    def sigma(f):
+        return 16.0 * f - 0.5
+
+    def fixed1(f):
+        for k in range(3):
+            look(f, k)
+        ts(a("ta", 0, 192), a("ti", 0, 192), 15, None, OP.bitwise_and)
+
+    def fixed2(f):
+        p = f & 1
+        ts(a("de", 0, 64), a("ta", 128, 192), 16.0, 4.0 - f - sigma(f), OP.mult, OP.add)
+        cp(a("dg", 128 * p + 64, 128 * p + 128), a("ta", 64, 128))
+        tt(a("cs", 64 * p, 64 * p + 64), a("ta", 0, 64), a("de", 0, 64), OP.add)
+
+    def mplace(f):
+        ts(a("moff", 12 * (f - 1), 12 * f), a("mio", 0, 12), a("tt", 10 + f, 11 + f), 256.0, OP.add, OP.mult)
+
+    def index(f):
+        sg, p, more = sigma(f), f & 1, f < F - 1
+        tt(a("xb", 0, 192), gi(a("mst", 0, 256 * (3 + f)), a("moff", 12 * (f - 1), 12 * f)), af("d3", f, 0, 192), OP.mult)
+        act(a("hv", 0, 128), a("xb", 64, 192), bias=191.75, scale=0.5)
+        act(a("hv", 128, 256), a("xb", 64, 192), bias=191.75, scale=-0.5)
+        turn_back(f - 1, 0)
+        if f == 1:
+            explicit(f, 0)
+            explicit(f, 1)
+        coords0(f)
+        coords(f)
+        turn_back(f - 1, 1)
+        if f == 1:
+            fixed1(f)
+            fixed2(f)
+        ts(a("zz", 0, 64), a("xb", 0, 64), sg, sg, OP.max, OP.subtract)
+        ts(a("nok", 0, 64), a("xb", 0, 64), sg, None, OP.is_lt)
+        if more:
+            mplace(f + 1)
+        tt(a("mm", 0, 64), a("cs", 64 * p, 64 * p + 64), a("nok", 0, 64), OP.mult)
+        tt(a("cn", 0, 64), a("zz", 0, 64), a("mm", 0, 64), OP.add)
+        act(a("ef", 0, 64), a("cn", 0, 64), bias=sg / 16 - 15.0 / 32 + 192.0, scale=1.0 / 16)
+        if more and f > 1:
+            fixed1(f + 1)
+        clamp()
+        places()
+        mm(a("ix1", 192, 256), a("i1k", 0, 128), a("dg", 128 * p + 64, 128 * p + 128), False, False)
+        mm(a("ix1", 128, 192), a("i1k", 0, 128), a("cn", 0, 64), False, False)
+        mm(a("ix1", 128, 192), a("in16k", 0, 128), a("ef", 0, 64), False, True)
+        preacc(f, range(4))
+        if more:
+            if f == 1:
+                fixed1(f + 1)
+            fixed2(f + 1)
+        ts(a("off", 128 * f, 128 * f + 64), a("ix1", 128, 192), 1024.0 * (sg + 3068 + f), None, OP.add)
+        cp(a("off", 128 * f + 64, 128 * f + 128), a("ix1", 192, 256))
+        if more:
+            keepw(f)
+            act(a("mst", 256 * (3 + f), 256 * (3 + f) + 64), a("cn", 0, 64), bias=sg)
+            explicit(f + 1, 0)
+            explicit(f + 1, 1)
+
+    def turn_back(f, h):
+        s = f + 1
+        mm(a("rb%d" % h, 0, 512), a("wide", 128 - 16 * s, 256 - 16 * s), a("sb", f * P + 512 * h, f * P + 512 * h + 512), True, True)
+        act(a("win", (8 + f) * P + 512 * h, (8 + f) * P + 512 * h + 512), a("rb%d" % h, 0, 512))
+        if h == 1:
+            later_loads(f + 1)
+            store(f * P, (f + 1) * P, a("win", (8 + f) * P, (9 + f) * P))
+
+    def pixels(f):
+        s = (f + 1) % F
+        win = a("win", (4 - f) * P, (8 + f) * P)
+
+        def unit(i, lo, hi):
+            o = 128 * f + 64 * i
+            return a("pq", P * i + lo, P * i + hi), gi(win, a("off", o + lo // 16, o + hi // 16))
+        for x in VUNITS:
+            cp(*unit(*x))
+        for x in SUNITS:
+            act(*unit(*x))
+        for k in range(4):
+            n = CH[k + 1] - CH[k]
+            if f == 0 and k == 2:
+                code0()
+                mplace(1)
+            for i in PQ[k]:
+                mm(a("u%d" % k, 0, n), a("half", 16 * s, 16 * s + 128), a("pq", P * i + CH[k], P * i + CH[k + 1]), False, i == PQ[k][1])
+            ts(a("cr", CH[k], CH[k + 1]), a("u%d" % k, 0, n), MAGIC, MAGIC, OP.add, OP.subtract)
+            ts(a("sb", f * P + CH[k], f * P + CH[k + 1]), a("cr", CH[k], CH[k + 1]), 0.0, 255.0, OP.max, OP.min)
+            if f < F - 1 and k in SENDS:
+                lo, hi = SENDS[k]
+                send(view(f + 1, lo, hi), a("sb", f * P + lo, f * P + hi), "va%d_%d" % (f + 1, k), "sent%d" % (f + 1))
+            if f == F - 1 and k > 0:
+                lo, hi = f * P + CH[k if k > 1 else 0], f * P + CH[k + 1]
+                store(lo, hi, a("sb", lo, hi))
+
+    for f in range(F):
+        pixels(f)
+        if f == 0:
+            for j in range(1, 3):
+                act(a3("d3", 64 * j, 64 * j + 64), a3("d16"), scale=1.0 / 16)
+        if f < F - 1:
+            index(f + 1)
+
+    for sem in cnt:
+        need("y", (sem, cnt[sem], {}))
+    for sem in LOADS:
+        need("y", (sem, 16, {}))
+    need("y", ("stored", stores[0], {}))

@@ -1,43 +1,60 @@
 import math
-from concourse.mybir import AluOpType as OP, ActivationFunctionType as AF
+from concourse.mybir import AluOpType as OP, ActivationFunctionType as AF, AxisListType as AX
 
 F, P = 5, 1024
 BF, F32, I32, U16 = "bfloat16", "float32", "int32", "uint16"
-CH = [0, 256, 448, 800, 1024]
+CW, CA = [0, 192, 448, 832, 1024], [0, 192, 576, 832, 1024]
 SENDS = {1: (0, 448), 3: (448, 1024)}
-VUNITS = [(0, 0, 256), (0, 256, 448), (0, 448, 544)]
-SUNITS = [(1, 0, 256), (1, 256, 448), (0, 544, 800), (1, 448, 800), (0, 800, 1024), (1, 800, 1024)]
-PQ = [(0, 1), (0, 1), (0, 1), (0, 1)]
-MAGIC = 12582912.0
-LN16 = math.log(16.0)
+STORES = {1: (0, 448), 2: (448, 832), 3: (832, 1024)}
+FIRSTV = [(0, 1024)]
+L0 = 5
+NL = F - L0
+ASK = L0 - 2
+B = min(NL, 1)
+N, U, SB = 64 * NL, 256 * NL, P + 16
+VWORK = [(0, 0, 192), (0, 192, 448), (0, 448, 832), 0, 1, 2, 3]
+SWORK = [(1, 0, 192), (1, 192, 448), (1, 448, 832), (0, 832, 1024), (1, 832, 1024)]
+VPRE, SPRE = [(0, 0, 576)], [(0, 576, 1024)]
+VPOST, SPOST = [(1, 192, 576), 0, 1, 2, 3], [(1, 0, 192), (1, 576, 832), (1, 832, 1024)]
+LAG = 3
+WAKE, GATHER, START, ROW, LOCAL, FAR, REMOTE, ONCE, CALL = 130.0, 1.7, 1300.0, 30.0, 0.03, 6.0, 0.06, 2500.0, 1200.0
+ROUNDS, FIRST = 2, 0.0
+EARLY = 0.0
+LN8 = math.log(8.0)
+K = 1024.0
 
 
 def _sb(n, d):
-    return ("sbuf", [128, n] if isinstance(n, int) else [128] + n, d)
+    return ("sbuf", [128, max(n, 16)] if isinstance(n, int) else [128] + n, d)
 
 
 SCRATCH = {
-    "win": _sb(12 * P, BF), "rs": _sb(F * P, BF), "sb": _sb(F * P, BF), "pq": _sb(2 * P, BF), "cr": _sb(P, BF),
+    "win": _sb(U + 8 * P, BF), "rs": _sb(F * P, BF), "sb": _sb(F * SB, BF), "pq": _sb(2 * P, BF),
+    "e4": _sb(256, F32), "eq": _sb(6 * 128, BF), "w1": _sb(512, F32), "be": _sb(256, BF), "lcol": _sb(4, I32),
+    "fab": _sb(2 * N, BF), "vf": _sb(N, BF), "fm": _sb(N, BF), "inc": _sb(N, BF), "qq": _sb(3 * N, BF), "k0": _sb(N, BF), "sx": _sb(N, BF), "kp": _sb(N, BF),
+    "zq": _sb(N, F32), "sgn": _sb(6 * N, BF), "cbe": _sb(4 * N, BF), "pa": _sb(N, F32), "pf": _sb(N, F32), "pv": _sb(3 * N, F32), "xs": _sb(N, F32), "ys": _sb(N, F32),
+    "ec": _sb(16, F32), "eo": _sb(4, U16), "thr": _sb(32 * NL, F32), "wm": _sb(32 * NL, F32), "hs": _sb(16 * NL + 8, F32), "y1": _sb(32 * NL, F32),
+    "ri": _sb(48 * NL, I32), "rqo": _sb(32 * NL, U16), "rq": _sb(32 * NL, U16), "ob": _sb(256, BF), "uo": _sb(U, BF), "of": _sb(192, F32),
     "ctl": _sb(26, I32), "ctlb": _sb(26, BF),
-    "ja": _sb([F, 64], I32), "jb": _sb([F, 64], I32), "wy": _sb(640, I32), "wx": _sb(640, I32),
-    "jaf": _sb([F, 64], BF), "kq": _sb([F, 64], BF), "d16": _sb([F, 64], BF), "d3": _sb([F, 192], BF), "nd2": _sb([F, 128], BF),
-    "rawp": _sb([F, 64], BF), "rawq": _sb([F, 64], BF), "pw": _sb(640, BF),
-    "pcol": _sb(4, I32), "ncol": _sb(4, I32), "col": _sb(16, F32), "ci": _sb(8, F32), "one": _sb(8, BF), "arow": _sb(20, F32),
-    "repi": _sb(128, BF), "rep": _sb(128, BF), "blk": _sb(128, BF), "alls": _sb(128, BF), "ge": _sb(128, BF), "le": _sb(128, BF),
-    "a15": _sb(128, BF), "an15": _sb(128, BF), "dif": _sb(256, BF), "wide": _sb(256, BF), "half": _sb(256, BF),
-    "i32": _sb(128, BF), "i1k": _sb(128, BF), "in16k": _sb(128, BF), "i16th": _sb(128, BF), "quar": _sb(128, BF),
-    "base": _sb(256, BF), "mio": _sb(12, F32), "moff": _sb(48, U16), "mst": _sb(7 * 256, BF),
-    "c": _sb(128, F32), "cq": _sb(24, BF), "st": _sb(16, BF), "sm": _sb(32, F32), "rk": _sb(32, BF), "pb": _sb(40, F32),
-    "tv": _sb(32, BF), "tt": _sb(20, F32),
-    "ti": _sb(192, I32), "ta": _sb(192, I32), "dg": _sb(256, BF), "de": _sb(64, BF), "cs": _sb(128, BF), "ev": _sb(512, BF),
-    "xb": _sb(192, BF), "hv": _sb(256, BF), "zz": _sb(64, BF), "nok": _sb(64, BF), "mm": _sb(64, BF), "cn": _sb(64, BF), "ef": _sb(64, BF),
-    "cb": _sb(256, BF), "off": _sb(F * 128, U16),
+    "ja": _sb(320, I32), "jb": _sb(320, I32), "wy": _sb(640, I32), "wx": _sb(640, I32),
+    "jf": _sb([2 * F, 64], BF), "r6": _sb(320, BF), "d3": _sb([F, 192], BF), "pw": _sb(640, BF), "ev": _sb(F * 256, BF),
+    "pcol": _sb(4, I32), "ncol": _sb(4, I32), "col": _sb(24, F32), "f0": _sb(16, BF), "t0": _sb(16, F32), "o0": _sb(128, F32), "ta0": _sb(192, I32), "ci": _sb(16, F32), "one": _sb(8, BF), "arow": _sb(25, F32),
+    "repi": _sb(128, BF), "rep": _sb(128, BF), "i16": _sb(16, BF), "dif": _sb(128, BF), "wide": _sb(256, BF), "half": _sb(256, BF),
+    "base": _sb(256, BF), "mio": _sb(12, F32), "moff": _sb(48, U16), "mst": _sb(6 * 192, BF),
+    "c": _sb(128, F32), "cq": _sb(8, BF), "st": _sb(16, BF), "sm": _sb(8, F32), "key": _sb(8, F32), "sg": _sb(8, F32),
+    "dd": _sb(80, BF), "junk": _sb(80, BF), "tv": _sb(64, BF), "tt": _sb(25, F32),
+    "ti": _sb(192, I32), "ta": _sb(192, I32), "dg": _sb(F * 192, BF),
+    "xb": _sb(192, BF), "hv": _sb(128, BF), "zz": _sb(128, BF), "ef": _sb(64, BF), "cb": _sb(256, BF), "off": _sb(F * 128, U16),
 }
+MATS = ("alls", "ge", "a18", "a7", "an7", "a8", "i32", "i8", "ni", "n8k", "n16", "quar", "unit", "mup", "mdn",
+        "nalls", "nge", "nge4", "n4", "nbig", "i64k", "i2k", "n32")
+for _k in MATS:
+    SCRATCH[_k] = _sb(128, BF)
 for _k in ("u0", "u1", "u2", "u3", "rb0", "rb1", "ix0", "ix1"):
     SCRATCH[_k] = ("psum", [128, 512], F32)
-LOADS = ["ls1", "ls0", "lg", "lc", "lr", "lja", "ljb", "lwy0", "lwx0", "lwy1", "lwx1", "lwy2", "lwx2"] + ["lrs%d" % f for f in range(F)]
-SEMAPHORES = (["cv", "cs", "ct", "cg", "stored", "va0"] + LOADS + ["sent%d" % f for f in range(F)]
-              + ["va%d_%d" % (f, k) for f in range(1, F) for k in range(4)])
+LOADS = (["ls1_%d" % k for k in range(len(FIRSTV))] + ["ls0", "lg", "lc", "lr", "lja", "ljb"] + ["l%s%d" % (n, k) for n in ("wy", "wx") for k in range(2)] + ["lrs%d" % f for f in range(F)])
+SEMAPHORES = (["cv", "cs", "ct", "cg", "stored", "asked", "ask"] + LOADS
+              + ["%s%d_%d" % (n, f, k) for n in ("va", "sent") for f in range(F) for k in range(4)])
 
 
 def rank_program(g, core, T, topo):
@@ -45,11 +62,10 @@ def rank_program(g, core, T, topo):
     if rank is None:
         return
     nxt = T.cores[(rank + 1) % len(T.cores)]
-    rid, pid = topo.addr(nxt)[0], topo.addr(nxt)[1]
-    emask = topo.mask(core, nxt)
-    neng = len(topo.engines(core, nxt))
     prv = T.cores[(rank - 1) % len(T.cores)]
-    narr = len(topo.engines(prv, core))
+
+    def engines(src, dst):
+        return len(topo.engines(src, dst))
     Q = {"v": g.vector, "s": g.scalar, "t": g.tensor, "g": g, "y": g.sync}
     cnt = {"cv": 0, "cs": 0, "ct": 0, "cg": 0}
     known = {e: {} for e in Q}
@@ -86,28 +102,103 @@ def rank_program(g, core, T, topo):
                 for name, lo, hi in x[1]:
                     hist.setdefault(name, []).append((lo, hi, wr, e, tok))
 
-    def run(e, outs, ins, call):
+    calls, seen, line, soft, early = [], {}, {}, set(), [0.0]
+
+    def width(x):
+        return sum(hi - lo for _, lo, hi in x[1])
+
+    def add(e, outs, ins, cost, emit, flight=0.0, after=()):
+        before = set(after)
+        for wr, group in ((True, outs), (False, ins)):
+            for x in group:
+                for name, lo, hi in x[1]:
+                    ps = SCRATCH[name][0] == "psum"
+                    for l2, h2, w2, k in seen.get(name, []):
+                        if (ps and (calls[k][0] != e or e == "t")) or ((wr or w2) and lo < h2 and l2 < hi):
+                            before.add(k)
+        if e in "gy":
+            before.update([k for k, c in enumerate(calls) if c[0] == e][-1:])
+        in_line = set(line.get(e, [])[-1:]) - before
+        before |= in_line
+        if e in line:
+            line[e].append(len(calls))
+        soft.update((j, len(calls)) for j in in_line)
+        for wr, group in ((True, outs), (False, ins)):
+            for x in group:
+                for name, lo, hi in x[1]:
+                    seen.setdefault(name, []).append((lo, hi, wr, len(calls)))
+        calls.append((e, cost, flight, before, emit, FIRST if line else early[0]))
+        return len(calls) - 1
+
+    def issue():
+        def gap(j, k):
+            e, cost, flight = calls[j][:3]
+            if (j, k) in soft or (e == calls[k][0] and e in "tgy"):
+                return max(cost, flight if calls[k][2] else 0.0)
+            return WAKE + (START + flight if flight else cost)
+
+        def plan(users, at, rank_):
+            left = [0] * n
+            for row_ in users:
+                for k, lag in row_:
+                    left[k] += 1
+            ready, free, done = {e: [k for k in range(n) if not left[k] and calls[k][0] == e] for e in Q}, {e: 0.0 for e in Q}, []
+            while len(done) < n:
+                end, e = min((max(at[k], free[e]) + calls[k][1], e) for e in Q for k in ready[e])
+                k = max((j for j in ready[e] if max(at[j], free[e]) < end), key=lambda j: (rank_[j], -j))
+                ready[e].remove(k)
+                at[k] = max(at[k], free[e])
+                free[e] = at[k] + calls[k][1]
+                done.append(k)
+                for j, lag in users[k]:
+                    at[j] = max(at[j], at[k] + lag)
+                    left[j] -= 1
+                    if not left[j]:
+                        ready[calls[j][0]].append(j)
+            return done, [at[k] + calls[k][1] for k in range(n)]
+        n = len(calls)
+        on, back = [[] for _ in calls], [[] for _ in calls]
+        for k, c in enumerate(calls):
+            for j in c[3]:
+                on[j].append((k, gap(j, k)))
+                back[k].append((j, gap(j, k) + c[1] - calls[j][1]))
+        tail = [START + c[2] - c[1] if c[2] else 0.0 for c in calls]
+        chain = [0.0] * n
+        for j in reversed(range(n)):
+            chain[j] = max([tail[j] + calls[j][1]] + [lag + chain[k] for k, lag in on[j]])
+        for _ in range(ROUNDS):
+            chain = plan(back, list(tail), plan(on, [0.0] * n, [x + c[5] for x, c in zip(chain, calls)])[1])[1]
+        for k in plan(on, [0.0] * n, [x + c[5] for x, c in zip(chain, calls)])[0]:
+            calls[k][4]()
+
+    def run(e, outs, ins, call, rate=1.0, fixed=0.0):
         ins = [x for x in ins if isinstance(x, tuple)]
-        order(e, outs, ins)
-        sem = "c" + e
-        cnt[sem] += 1
-        call().then_inc(T.sem[sem], 1)
-        note(e, outs, ins, (sem, cnt[sem], dict(known[e])))
+
+        def emit():
+            order(e, outs, ins)
+            sem = "c" + e
+            cnt[sem] += 1
+            call().then_inc(T.sem[sem], 1)
+            note(e, outs, ins, (sem, cnt[sem], dict(known[e])))
+        if any(len(x) > 2 for x in ins):
+            rate, fixed = GATHER, 70.0
+        elif e == "v" and rate == 1.0 and all(SCRATCH[x[1][0][0]][2] in (BF, U16) for x in outs + ins[:1]):
+            rate = 0.5
+        add(e, outs, ins, fixed + max(64.0 * min(rate, 1.0) if e == "t" else 64.0, rate * width(outs[0])), emit)
 
     def a(name, lo, hi, step=1, parts=128):
         ap = T[name][0:parts, lo:hi] if step == 1 else T[name][0:parts, lo:hi:step]
         return (ap, [(name, lo, hi)])
 
-    def a3(name, lo=None, hi=None):
+    def a3(name, r0, r1, lo, hi):
         w = SCRATCH[name][1][2]
-        return (T[name][:] if lo is None else T[name][:, :, lo:hi], [(name, 0, F * w)])
+        return (T[name][:, r0, lo:hi] if r1 == r0 + 1 else T[name][:, r0:r1, lo:hi], [(name, r * w + lo, r * w + hi) for r in range(r0, r1)])
 
-    def af(name, f, lo, hi):
-        w = SCRATCH[name][1][2]
-        return (T[name][:, f, lo:hi], [(name, f * w + lo, f * w + hi)])
+    def one(name, k):
+        return a(name, k, k + 1)
 
     def gi(w, o):
-        return (w[0].indirect(o[0]), w[1] + o[1])
+        return (w[0].indirect(o[0]), w[1] + o[1], "gather")
 
     def u(x):
         return x[0] if isinstance(x, tuple) else x
@@ -119,7 +210,8 @@ def rank_program(g, core, T, topo):
             run("v", [o], [i, s1, s2], lambda: g.vector.tensor_scalar(o[0], i[0], u(s1), u(s2), op0, op1))
 
     def tt(o, x, y, op):
-        run("v", [o], [x, y], lambda: g.vector.tensor_tensor(o[0], x[0], y[0], op))
+        both = all(SCRATCH[z[1][0][0]][0] == "sbuf" for z in (x, y))
+        run("v", [o], [x, y], lambda: g.vector.tensor_tensor(o[0], x[0], y[0], op), 2.0 if both else 1.0)
 
     def cp(o, i):
         run("v", [o], [i], lambda: g.vector.tensor_copy(o[0], i[0]))
@@ -130,381 +222,596 @@ def rank_program(g, core, T, topo):
     def scan(o, d0, d1, init, op0, op1):
         run("v", [o], [d0, d1, init], lambda: g.vector.tensor_tensor_scan(o[0], d0[0], d1[0], u(init), op0, op1))
 
-    def act(o, i, func=AF.Identity, bias=0.0, scale=1.0):
-        run("s", [o], [i, bias, scale], lambda: g.scalar.activation(o[0], i[0], func, bias=u(bias), scale=u(scale)))
+    def total(o, i):
+        run("v", [o], [i], lambda: g.vector.tensor_reduce(o[0], i[0], AX.X, OP.add))
 
-    def mm(o, l, r, start, stop):
-        run("t", [o], [l, r], lambda: g.tensor.matmul(o[0], l[0], r[0], start, stop))
+    def act(o, i, func=AF.Identity, bias=0.0, scale=1.0, acc=None, fixed=0.0):
+        if acc is None:
+            run("s", [o], [i, bias, scale], lambda: g.scalar.activation(o[0], i[0], func, bias=u(bias), scale=u(scale)), 1.0, fixed)
+        else:
+            run("s", [o, acc], [i, bias, scale], lambda: g.scalar.activation(o[0], i[0], func, bias=u(bias), scale=u(scale), accum_out=acc[0]))
+
+    def mm(o, l, r, start=False, stop=False):
+        run("t", [o], [l, r], lambda: g.tensor.matmul(o[0], l[0], r[0], start, stop), 2.0 if SCRATCH[l[1][0][0]][2] == F32 else 0.5)
+
+    def mms(terms):
+        for k, (o, l, r) in enumerate(terms):
+            mm(o, l, r, k == 0, k == len(terms) - 1)
 
     def iota(o, pat, base, cm, small=True):
         if small:
-            run("g", [o], [], lambda: g.iota(o[0], pat, base, cm, allow_small_or_imprecise_dtypes=True))
+            run("g", [o], [], lambda: g.iota(o[0], pat, base, cm, allow_small_or_imprecise_dtypes=True), 2.0, 160.0)
         else:
-            run("g", [o], [], lambda: g.iota(o[0], pat, base, cm))
+            run("g", [o], [], lambda: g.iota(o[0], pat, base, cm), 2.0, 160.0)
+
+    def row(x):
+        return width(x) * (4 if SCRATCH[x[1][0][0]][2] == I32 else 2)
+
+    gate = []
+
+    def local(e, outs, ins, start):
+        waits, after = [tok for tok, k in gate], [k for tok, k in gate]
+        del gate[:]
+
+        def emit():
+            for tok in waits:
+                need(e, tok)
+            order(e, outs, ins)
+            start()
+        x = (outs + ins)[0]
+        add(e, outs, ins, 64.0, emit, (8 if row(x) > 64 else 1) * (ROW + LOCAL * row(x)), after)
 
     def load(e, o, src, sem):
-        order(e, [o], [])
-        Q[e].dma_start(o[0], src).then_inc(T.sem[sem], 16)
-        note(e, [o], [], (sem, 16, dict(known[e])))
+        def start():
+            Q[e].dma_start(o[0], src).then_inc(T.sem[sem], 16)
+            note(e, [o], [], (sem, 16, dict(known[e])))
+        local(e, [o], [], start)
 
     stores = [0]
 
     def store(lo, hi, src):
-        order("y", [], [src])
-        g.sync.dma_start(T.y[:, lo:hi], src[0]).then_inc(T.sem.stored, 16)
+        local("y", [], [src], lambda: g.sync.dma_start(T.y[:, lo:hi], src[0]).then_inc(T.sem.stored, 16))
         stores[0] += 16
 
-    def send(dst, src, rsem, lsem):
-        order("g", [], [src])
-        g.remote_dma(out_ap=dst[0], in_ap=src[0], remote_sem=T.sem[rsem], local_sem=T.sem[lsem], pid=pid, routing_id=rid, dma_engine_mask=emask)
+    sends = {}
 
-    def view(f, lo=0, hi=P):
-        return a("win", (4 - f) * P + lo, (4 - f) * P + hi)
+    def send(dst, src, rsem, lsem, to=nxt, frm=prv):
+        def emit():
+            order("g", [], [src])
+            g.remote_dma(out_ap=dst[0], in_ap=src[0], remote_sem=T.sem[rsem], local_sem=T.sem[lsem], pid=topo.addr(to)[1], routing_id=topo.addr(to)[0],
+                         dma_engine_mask=topo.mask(core, to))
+        n = engines(core, to)
+        note("r", [dst], [], (rsem, engines(frm, core), {}))
+        sends[lsem] = (n, add("g", [dst], [src], CALL, emit, 128 // n * (FAR + REMOTE * row(src)) + (0.0 if sends else ONCE)))
 
-    note("r", [view(0)], [], ("va0", narr, {}))
-    for f in range(1, F):
-        for k, (lo, hi) in SENDS.items():
-            note("r", [view(f, lo, hi)], [], ("va%d_%d" % (f, k), narr, {}))
+    def slot(k, lo=0, hi=P):
+        return a("win", U + (k - 1 + B) * P + lo, U + (k - 1 + B) * P + hi)
 
-    load("y", a("win", 7 * P, 8 * P), T.pic0[:, P:2 * P], "ls1")
+    def blank(n):
+        return slot(1, 0, n)
+
+    def made(f, lo, hi):
+        return a("sb", f * SB + 16 + lo, f * SB + 16 + hi)
+
+    def vectors(k, lo, hi):
+        load("y", a("wy", lo, hi), T.vy[:, lo:hi], "lwy%d" % k)
+        load("y", a("wx", lo, hi), T.vx[:, lo:hi], "lwx%d" % k)
+
+    def residual(f):
+        load("y", a("rs", f * P, (f + 1) * P), T.res[:, f * P:(f + 1) * P], "lrs%d" % f)
+
     load("s", a("ctl", 0, 5, parts=8), T.gaps[:], "lg")
+    load("y", a("ctl", 10, 25, parts=8), T.rel[:], "lr")
     load("s", a("ctl", 5, 10, parts=8), T.cmd[:], "lc")
-    load("s", a("ctl", 10, 25, parts=8), T.rel[:], "lr")
-    load("y", a3("ja"), T.ia[:], "lja")
-    load("y", a3("jb"), T.ib[:], "ljb")
-    load("y", a("wy", 0, 128), T.vy[:, 0:128], "lwy0")
-    load("y", a("wx", 0, 128), T.vx[:, 0:128], "lwx0")
-    load("y", a("rs", 0, P), T.res[:, 0:P], "lrs0")
-    load("y", a("win", 6 * P, 7 * P), T.pic0[:, 0:P], "ls0")
+    for k, (lo, hi) in enumerate(FIRSTV):
+        load("y", slot(3, lo, hi), T.pic0[:, P + lo:P + hi], "ls1_%d" % k)
+    load("y", a("ja", 0, 320), T.ia[:], "lja")
+    load("y", a("jb", 0, 320), T.ib[:], "ljb")
+    vectors(0, 0, 128)
+    load("y", slot(2), T.pic0[:, 0:P], "ls0")
+    residual(0)
+    vectors(1, 128, 640)
 
-    nf, n1, np1, c01 = a("col", 0, 1), a("col", 1, 2), a("col", 2, 3), a("col", 3, 4)
-    alls, ge, le, wide = a("alls", 0, 128), a("ge", 0, 128), a("le", 0, 128), a("wide", 0, 256)
-    ident = a("wide", 0, 128)
-    iota(a("pcol", 0, 1), [[0, 1]], 0, 1, False)
-    iota(a("repi", 0, 128, parts=8), [[1, 8], [0, 16]], 0, -1)
-    iota(a("blk", 0, 128), [[16, 8], [0, 16]], 0, -1)
-    iota(a("ci", 0, 6), [[1, 6]], 1, 0)
-    iota(a("dif", 0, 256), [[0, 2], [1, 128]], 0, -1)
-    ms(a("c", 0, 128), 0.0)
-    act(a("one", 0, 8), a("c", 120, 128), AF.Exp)
-    ms(a("arow", 5, 10), 0.5)
-    ms(a("arow", 10, 15), 0.0)
-    ts(a("ncol", 0, 1), a("pcol", 0, 1), 15, None, OP.bitwise_and)
-    cp(nf, a("ncol", 0, 1))
-    ms(a("quar", 0, 128), 2.0 ** -16)
-    ts(n1, nf, -1.0, 1.0, OP.mult, OP.add)
-    ts(np1, nf, 1.0, None, OP.add)
-    ts(a("rep", 0, 128, parts=8), a("repi", 0, 128, parts=8), 0.0, None, OP.is_equal)
-    ts(alls, a("blk", 0, 128), nf, 0.0, OP.add, OP.is_equal)
-    ts(c01, nf, 2.0, np1, OP.is_lt, OP.mult)
-    ms(a("win", 5 * P, 6 * P), 128.0)
-    run("g", [ge], [alls], lambda: g.affine_select(ge[0], alls[0], [[-1, 128]], OP.is_ge, 0.0, 0, 1))
-    send(view(0), a("win", 7 * P, 8 * P), "va0", "sent0")
-    run("g", [le], [alls], lambda: g.affine_select(le[0], alls[0], [[1, 128]], OP.is_ge, 0.0, 0, -1))
-    iota(a("base", 0, 128), [[0, 2], [1, 32], [0, 2]], -192, 0)
-    iota(a("base", 128, 256), [[0, 64], [16, 2]], -192, 0)
-    iota(a("mio", 0, 12), [[16, 12]], 0, 0)
-    ms(a("mst", 0, 768), 0.0)
-    ts(wide, a("dif", 0, 256), 0.0, None, OP.is_equal)
-    ms(a("mst", 768 + 192, 7 * 256), 0.0)
-    act(a("arow", 0, 5), a("ci", 0, 5), bias=0.5, scale=69905.0)
-    act(a("arow", 15, 20), a("ci", 0, 5), bias=0.5, scale=69905.0)
-    act(a("a15", 0, 128), alls, scale=15.0)
-    act(a("an15", 0, 128), alls, scale=-15.0)
-    act(a("half", 0, 256), wide, scale=0.5)
-    act(a("i16th", 0, 128), ident, scale=1.0 / 16)
-    act(a("i32", 0, 128), ident, scale=32.0)
-    act(a("i1k", 0, 128), ident, scale=1024.0)
-    act(a("in16k", 0, 128), ident, scale=-16384.0)
-
-    def later_loads(f):
-        need("y", ("sent%d" % f, neng * (len(SENDS) if f else 1), {}))
-        if f < 2:
-            lo, hi = 128 + 256 * f, 384 + 256 * f
-            load("y", a("wy", lo, hi), T.vy[:, lo:hi], "lwy%d" % (f + 1))
-            load("y", a("wx", lo, hi), T.vx[:, lo:hi], "lwx%d" % (f + 1))
+    def later(f):
+        n, k = sends["sent%d_3" % f]
+        gate.append((("sent%d_3" % f, n, {}), k))
         if f < F - 1:
-            load("y", a("rs", (f + 1) * P, (f + 2) * P), T.res[:, (f + 1) * P:(f + 2) * P], "lrs%d" % (f + 1))
-    later_loads(0)
+            residual(f + 1)
+        if f > 0:
+            store((f - 1) * P, f * P, slot(3 + f))
 
-    def explicit(f, k):
-        tt(ev(f, 128 * k, 128 * k + 128), a(("wy", "wx")[k], 128 * f, 128 * f + 128), af("nd2", f, 0, 128), OP.mult)
+    nf, n1, nb0, nb1, cl, c01, gz, cz, ee, sm, ek, lf, b4, b16, et, hn, h0 = [one("col", k) for k in range(17)]
+    alls, ge, a18, a7, an7, a8, i32, i8, ni, n8k, n16, quar, unit, mup, mdn, nalls, nge, nge4, n4, nbig, i64k, i2k, n32 = [a(n, 0, 128) for n in MATS]
+    wide, ident, i16 = a("wide", 0, 256), a("wide", 0, 128), a("i16", 0, 16)
+    iota(one("pcol", 0), [[0, 1]], 0, 1, False)
+    iota(a("repi", 0, 128, parts=8), [[1, 8], [0, 16]], 0, -1)
+    iota(a("ci", 0, 16), [[1, 16]], 0, 0)
+    iota(a("dif", 0, 128), [[1, 128]], 0, -1)
+    rep = a("rep", 0, 128, parts=8)
+    ms(a("c", 120, 128), 0.0)
+    act(a("one", 0, 8), a("c", 120, 128), AF.Exp, fixed=1600.0)
+    ts(one("ncol", 0), one("pcol", 0), 15, None, OP.bitwise_and)
+    ms(quar, 2.0 ** -16)
+    cp(nf, one("ncol", 0))
+    ms(unit, 2.0 ** -14)
+    ms(mup, 768.0)
+    ms(mdn, -768.0)
+    ts(rep, a("repi", 0, 128, parts=8), 0.0, None, OP.is_equal)
+    mm(a("u1", 0, 128), rep, rep, True, True)
+    ts(n1, nf, -1.0, 1.0, OP.mult, OP.add)
+    ts(nb0, nf, K, K, OP.mult, OP.add)
+    ts(nb1, nf, -239.0, None, OP.add)
+    cp(alls, a("u1", 0, 128))
+    ts(cl, nf, -2.0, 255.0, OP.mult, OP.add)
+    ts(i16, a("ci", 0, 16), nf, None, OP.is_equal)
+    ts(c01, nf, 2.0, nb0, OP.is_lt, OP.mult)
+    ts(ident, a("dif", 0, 128), 0.0, None, OP.is_equal)
+    ms(a("arow", 0, 25), 0.0)
+    ms(blank(128), 128.0)
+    cp(a("ctlb", 0, 25, parts=8), a("ctl", 0, 25, parts=8))
+    mm(a("u3", 0, 25), rep, a("ctlb", 0, 25, parts=8), True, True)
+    ts(a("wide", 128, 256), a("dif", 0, 128), 0.0, None, OP.is_equal)
+
+    def select(o, i, pat):
+        run("g", [o], [i], lambda: g.affine_select(o[0], i[0], pat, OP.is_ge, 0.0, 0, 1), 2.0, 200.0)
+    ts(hn, nf, 0.5, None, OP.mult)
+    act(ge, a("dif", 0, 128), AF.Abs, bias=hn)
+    ts(ge, ge, hn, None, OP.is_le)
+    iota(a("base", 0, 128), [[0, 2], [1, 32], [0, 2]], -192, 0)
+    for k, (lo, hi) in enumerate(FIRSTV):
+        send(slot(4, lo, hi), slot(3, lo, hi), "va0_%d" % k, "sent0_%d" % (3 if hi == P else k))
+    for k in range(2):
+        act((T.base[:, 128 + k:256:2], [("base", 128 + 64 * k, 192 + 64 * k)]), blank(64), bias=nf, scale=(16.0 * k - 192.0) / 128)
+    act(a("mio", 0, 12), a("ci", 0, 12), bias=nf, scale=16.0)
+    ms(a("mst", 0, 192), 0.0)
+    if NL:
+        act(nalls, alls, scale=-1.0)
+        select(nge, nalls, [[-1, 128]])
+        select(nge4, nalls, [[-16, 8], [0, 4], [-4, 4]])
+        iota(a("e4", 0, 128, parts=32), [[1, 32], [0, 4]], 0, -1)
+        iota(a("e4", 128, 256, parts=32), [[16, 8], [1, 4], [4, 4]], 0, -4)
+        iota(a("thr", 0, 16 * NL), [[0, NL], [16, 16]], 16, 0)
+        iota(slot(0), [[0, P]], 255, 0)
+        ms(slot(1, 128, P), 128.0)
+    else:
+        iota(slot(1, 128, P), [[0, P - 128]], 128, 0)
+    act(a18, alls, scale=2.0 ** 18)
+    act(a7, alls, scale=7.0)
+    act(an7, alls, scale=-7.0)
+    act(n16, ident, scale=-16.0)
+    act(ni, ident, scale=-1.0)
+    act(i32, ident, scale=32.0)
 
     def ev(f, lo, hi):
-        return a("ev", 256 * (f & 1) + lo, 256 * (f & 1) + hi)
+        return a("ev", 256 * f + lo, 256 * f + hi)
 
-    def coords0(f):
-        mm(a("ix0", 0, 256), ident, a("base", 0, 256), True, False)
-        mm(a("ix0", 0, 256), ident, ev(f, 0, 256), False, f == 0)
+    def dg(f, k):
+        return a("dg", 192 * f + 64 * k, 192 * f + 64 * k + 64)
 
-    def coords(f):
-        for k, (o, i) in enumerate(((0, 0), (128, 64), (64, 128), (192, 192))):
-            mm(a("ix0", o, o + 64), ident, a("hv", i, i + 64), False, k == 3)
-        if f < F - 1:
-            mm(a("ix0", 256, 384), ident, a("hv", 0, 128), True, False)
-            mm(a("ix0", 256, 320), ident, ev(f, 0, 64), False, False)
-            mm(a("ix0", 320, 384), ident, ev(f, 128, 192), False, True)
+    def explicit(f, nd=a("ix0", 384, 512)):
+        mms([(nd, unit, blank(128)), (nd, ni, a3("d3", f, f + 1, 0, 128))])
+        for k in range(2):
+            tt(ev(f, 128 * k, 128 * k + 128), a(("wy", "wx")[k], 128 * f, 128 * f + 128), nd, OP.mult)
 
     def clamp(lo=0.0):
         ts(a("cb", 0, 256), a("ix0", 0, 256), lo, lo + 31.0, OP.max, OP.min)
 
-    def places():
-        mm(a("ix1", 128, 256), a("i32", 0, 128), a("cb", 0, 128), True, False)
-        mm(a("ix1", 128, 256), ident, a("cb", 128, 256), False, False)
-
-    def keepw(f):
-        act(a("mst", 256 * (3 + f) + 64, 256 * (3 + f) + 192), a("ix0", 256, 384), bias=-192.0)
-
-    def preacc(f, ks):
-        s = (f + 1) % F
-        for k in ks:
+    def preacc(f):
+        s, CH = (f + 1) % F, (CA if f >= L0 else CW)
+        for k in range(len(CH) - 1):
             n = CH[k + 1] - CH[k]
-            mm(a("u%d" % k, 0, n), a("wide", 16 * s, 16 * s + 128), a("rs", f * P + CH[k], f * P + CH[k + 1]), True, False)
-            mm(a("u%d" % k, 0, n), a("quar", 0, 128), a("win", 5 * P, 5 * P + n), False, False)
+            mm(a("u%d" % k, 0, n), a("wide", 16 * s, 16 * s + 128), a("rs", f * P + CH[k], f * P + CH[k + 1]), True)
+            mm(a("u%d" % k, 0, n), quar, blank(n))
 
-    def look(f, k):
-        pw = a("pw", 320 * (k & 1) + 64 * f, 320 * (k & 1) + 64 * f + 64)
-        col = (0, 15, 5)[k] + f
-        ts(a("ti", 64 * k, 64 * k + 64), pw, a("tt", col, col + 1), -0.5, OP.mult, OP.add)
+    def look(f):
+        for k in range(3 if f < F - 1 else 2):
+            p = 320 * (k & 1) + 64 * f
+            ts(a("ti", 64 * k, 64 * k + 64), a("pw", p, p + 64), one("tt", 5 * k + f), None, OP.mult)
+
+    def digits(f):
+        n = 192 if f < F - 1 else 128
+        ts(a("ta", 0, n), a("ti", 0, n), 7 * 1024, None, OP.bitwise_and)
+
+    def keep(f):
+        n = 192 if f < F - 1 else 128
+        cp(a("dg", 192 * f, 192 * f + n), a("ta", 0, n))
+
+    def mplace(f):
+        ts(a("moff", 12 * (f - 1), 12 * f), a("mio", 0, 12), one("tt", 20 + f), None, OP.add)
 
     def c5(k, lo=0, hi=5):
         return a("c", 8 * k + lo, 8 * k + hi)
-    cn_, tx, tc, lt, new, m0, m1, isb, nb, nm1, m64, isf, sl_, e_ = [k for k in range(14)]
-    gaps, cmd = a("rb0", 0, 5), a("rb0", 5, 10)
-    cp(a("ctlb", 0, 25, parts=8), a("ctl", 0, 25, parts=8))
-    mm(a("rb0", 0, 25), a("rep", 0, 128, parts=8), a("ctlb", 0, 25, parts=8), True, True)
-    scan(c5(cn_), gaps, a("one", 0, 5), n1, OP.add, OP.add)
-    tot0 = a("col", 4, 5)
-    ts(tot0, a("rb0", 0, 1), 2.0, None, OP.add)
-    tt(c5(tx), c5(cn_), a("rb0", 10, 25, 3), OP.is_equal)
-    ts(c5(lt), c5(cn_), 0.0, None, OP.is_gt)
-    tt(c5(tc), c5(tx), cmd, OP.mult)
-    tt(c5(new, 0, 4), c5(lt, 1, 5), c5(lt, 0, 4), OP.subtract)
-    ts(a("cq", 0, 5), c5(tc), -6.0, 14.5, OP.mult, OP.add)
-    ts(a("cq", 8, 13), c5(tc), 1.0, None, OP.is_equal)
+    cn_, tx, tc, lt, m0, m1, kb, isf, sl_, hs, he, ka, ths, thl, k2 = range(15)
 
-    def powers(k):
-        bank = a(("ix0", "u3")[k], 0, 320)
-        mm(bank, a("i16th", 0, 128), a3("d16"), True, False)
-        mm(bank, ident, a3(("rawp", "rawq")[k]), False, True)
-        act(a("pw", 320 * k, 320 * k + 320), bank)
+    def tv(k, lo=0, hi=5):
+        return a("tv", 8 * k + lo, 8 * k + hi)
+    ex, vs, v0, v1, ve, v0e, v1m = range(7)
 
-    def st_s(f):
-        return a("st", 2 * f, 2 * f + 1)
+    def short(f):
+        return one("st", f)
 
-    def st_l(f):
-        return a("st", 2 * f + 1, 2 * f + 2)
+    def long_(f):
+        return one("st", 5 + f)
 
-    def thr_(f):
-        return a("cq", f, f + 1)
+    def place(bank, lo, hi):
+        keys = a(bank, 64 + 16 * lo, 64 + 16 * hi)
+        mms([(keys, quar, blank(16 * (hi - lo))), (keys, alls, a("dd", 16 * lo, 16 * hi))])
+        for f in range(lo, hi):
+            act(a("junk", 16 * f, 16 * f + 16), a(bank, 64 + 16 * f, 80 + 16 * f), AF.Sign, bias=one("key", f), scale=-1.0, acc=one("sg", f))
 
-    def t1_(f):
-        return a("cq", 8 + f, 9 + f)
-    ks0 = a("sm", 0, 1)
-    ts(ks0, tot0, thr_(0), t1_(0), OP.is_le, OP.subtract)
-    ts(st_l(1), c5(lt, 0, 1), t1_(0), None, OP.mult)
-    ts(st_s(1), c5(lt, 0, 1), ks0, c5(new, 0, 1), OP.mult, OP.add)
+    def control():
+        tt(c5(tx), c5(cn_), a("u3", 10, 25, 3), OP.is_equal)
+        ts(c5(lt), c5(cn_), 0.0, None, OP.is_gt)
+        ts(cz, one("u3", 5), gz, one("u3", 5), OP.is_le, OP.mult)
+        yield
+        ts(c5(tc, 0, 1), c5(tx, 0, 1), cz, None, OP.mult)
+        tt(c5(tc, 1, 5), c5(tx, 1, 5), a("u3", 6, 10), OP.mult)
+        tt(a("cq", 1, 5), c5(lt, 1, 5), c5(lt, 0, 4), OP.subtract)
+        yield
+        ts(short(0), c5(tc, 0, 1), 0.0, c5(lt, 0, 1), OP.is_equal, OP.mult)
+        ts(long_(0), c5(tc, 0, 1), 1.0, None, OP.is_equal)
+        ts(c5(k2), c5(tc), 2.0, None, OP.not_equal)
+        act(c5(thl), c5(tc), AF.Abs, bias=-100.0, scale=100.0)
+        act(c5(ths), c5(tc), bias=-11.0, scale=-100.0)
+        act(c5(thl), c5(thl), bias=-11.0, scale=-1.0)
+        for f in range(1, F):
+            cum, lk = one("u1", f), one("sm", f)
+            mms([(cum, ge, one("cq", f)), (cum, n16, one("cq", f)), (cum, alls, long_(f - 1)), (cum, ge, short(f - 1)), (cum, n16, short(f - 1))])
+            ts(lk, long_(f - 1), c5(k2, f, f + 1), None, OP.mult)
+            yield
+            act(c5(ka, f - 1, f), long_(f - 1), bias=c5(kb, f - 1, f), scale=cl)
+            act(one("key", f - 1), short(f - 1), bias=c5(ka, f - 1, f), scale=256.0)
+            act(a("dd", 16 * f - 16, 16 * f), i16, scale=one("key", f - 1))
+            if f == 1:
+                place("u2", 0, 1)
+                act(tv(ex, 0, 1), one("sg", 0), AF.Exp, bias=7.0 * LN8, scale=-LN8 / 2)
+                f0, f1, fs = [one("f0", k) for k in range(3)]
+                ts(h0, one("key", 0), 0.0, c01, OP.is_gt, OP.mult)
+                ts(f0, one("sg", 0), 14.0, c01, OP.is_equal, OP.mult)
+                ts(f1, one("sg", 0), 12.0, c01, OP.is_equal, OP.mult)
+                act(fs, tv(ex, 0, 1), scale=h0)
+                mms([(one("u2", 0), a18, f0), (one("u2", 0), alls, fs)])
+                mms([(one("u2", 1), a7, f0), (one("u2", 1), a18, f1), (one("u2", 1), an7, f1), (one("u2", 1), alls, fs)])
+                act(a("t0", 0, 2), a("u2", 0, 2), bias=K * (B * (8 ** 6 + sum(8 ** k for k in range(5))) + (3 + B) * 8 ** 5))
+            yield
+            ts(short(f), cum, c5(ths, f, f + 1), None, OP.is_le)
+            ts(long_(f), cum, c5(thl, f, f + 1), lk, OP.is_le, OP.add)
+        place("ix1", 1, 4)
+        yield
+        ts(c5(ka, 4, 5), long_(4), cl, c5(kb, 4, 5), OP.mult, OP.add)
+        total(ee, a("st", 0, 11))
+        yield
+        ts(one("key", 4), short(4), 256.0, c5(ka, 4, 5), OP.mult, OP.add)
+        act(ek, ee, scale=K)
+        yield
+        ts(a("dd", 64, 80), i16, one("key", 4), None, OP.mult)
+        place("ix1", 4, 5)
+        act(tv(ex, 1, 5), a("sg", 1, 5), AF.Exp, bias=7.0 * LN8, scale=-LN8 / 2)
+        slc = c5(sl_, 3, 4)
+        ts(c5(hs), a("key", 0, 5), 0.0, slc, OP.is_gt, OP.mult)
+        ts(c5(he), a("key", 0, 5), 0.0, ek, OP.is_gt, OP.mult)
+        yield
+        yield
+        ts(tv(v0), a("sg", 0, 5), 14.0, slc, OP.is_equal, OP.mult)
+        ts(tv(v1), a("sg", 0, 5), 12.0, slc, OP.is_equal, OP.mult)
+        ts(tv(v0e), a("sg", 0, 5), 14.0, ek, OP.is_equal, OP.mult)
+        ts(tv(v1m), a("sg", 0, 5), 12.0, sm, OP.is_equal, OP.mult)
+        tt(tv(vs), tv(ex), c5(hs), OP.mult)
+        tt(tv(ve), tv(ex), c5(he), OP.mult)
+        b = [a("ix1", 192 + 5 * k, 197 + 5 * k) for k in range(5)]
+        mms([(b[3], alls, tv(v0)), (b[3], a8, tv(v0e))])
+        mms([(b[4], alls, tv(v1m))])
+        mms([(b[0], a18, tv(v0)), (b[0], alls, tv(vs))])
+        mms([(b[1], a7, tv(v0)), (b[1], a18, tv(v1)), (b[1], an7, tv(v1)), (b[1], alls, tv(vs))])
+        mms([(b[2], a18, tv(v0e)), (b[2], alls, tv(ve))])
+        yield
+        tt(a("tt", 0, 25), a("ix1", 192, 217), a("arow", 0, 25), OP.add)
 
-    def fill1():
-        tt(c5(m0), c5(cn_), a("rb0", 11, 25, 3), OP.is_equal)
-        tt(c5(m1), c5(cn_), a("rb0", 12, 25, 3), OP.is_equal)
-        ts(c5(isf, 0, 4), c5(cn_, 0, 4), 0.0, None, OP.is_equal)
+    def lists():
+        for _ in range(LAG):
+            yield
+        ja = a3("jf", 0, F, 0, 64)
+        cp(ja, a("ja", 0, 320))
+        act(a("r6", 0, 320), ja, AF.Relu, bias=-30.0, scale=6.0)
+        mm(a("u0", 0, 320), ident, a("r6", 0, 320), True, True)
+        for j in range(2):
+            act(a3("d3", 0, F, 64 * j, 64 * j + 64), ja, AF.Relu, bias=-5.0)
+        yield
+        yield
+        tt(a3("jf", F, 2 * F, 0, 64), a("jb", 0, 320), a("u0", 0, 320), OP.max)
+        yield
+        yield
+        explicit(0)
+        mms([(a("ix0", 0, 256), ident, a("base", 0, 256)), (a("ix0", 0, 256), ident, ev(0, 0, 256))])
+        yield
+        act(a8, alls, scale=8.0)
+        yield
+        clamp(-192.0)
+        ones = B * K * (8 ** 6 + sum(8 ** k for k in range(5)))
+        for k in (0, 5):
+            act(a("arow", k, k + L0), a("ci", 3 + B, 3 + B + L0), bias=ones, scale=2.0 ** 25)
+            if NL:
+                act(a("arow", k + L0, k + 5), a("ci", 0, NL), bias=ones, scale=0.0)
+        act(a("arow", 15, 20), a("ci", 0, 5), bias=B * K, scale=-8.0 * K)
+        yield
+        yield
+        yield
+        for k in range(2):
+            act(a("pw", 320 * k, 320 * k + 64), a3("jf", F * k, F * k + 1, 0, 64), AF.Exp, scale=-LN8)
+            act(a("pw", 320 * k + 64, 320 * k + 320), a3("jf", F * k + 1, F * k + F, 0, 64), AF.Exp, scale=-LN8)
 
-    def fill2():
-        cp(a3("jaf"), a3("ja"))
-        act(a3("d16"), a3("jaf"), AF.Relu, bias=-80.0, scale=16.0)
-        act(a3("rawp"), a3("jaf"), AF.Exp, scale=-LN16)
-
-    def fill3():
-        tt(c5(isb), c5(m0), c5(m1), OP.max)
-        tt(c5(isf, 4, 8), c5(isf, 0, 4), a("ci", 2, 6), OP.mult)
-        ts(c5(nm1), c5(m1), -1.0, 1.0, OP.mult, OP.add)
-        ts(c5(nb), c5(isb), -1.0, 1.0, OP.mult, OP.add)
+    def extras():
+        yield
+        tt(c5(m0), c5(cn_), a("u3", 11, 25, 3), OP.is_equal)
+        tt(c5(m1), c5(cn_), a("u3", 12, 25, 3), OP.is_equal)
+        act(c5(m0), c5(m0), bias=nb1, scale=32.0)
+        act(c5(m1), c5(m1), scale=64.0)
+        yield
+        tt(c5(kb), c5(m0), c5(m1), OP.add)
+        yield
+        ts(c5(isf, 0, 4), c5(cn_, 0, 4), 0.0, K, OP.is_equal, OP.mult)
+        act(c5(sl_), c5(lt), bias=1.0, scale=-1.0, acc=ee)
+        yield
+        tt(c5(isf, 4, 8), c5(isf, 0, 4), a("ci", 3, 7), OP.mult)
+        act(one("st", 10), ee, bias=-1.0)
+        yield
         scan(c5(sl_, 0, 4), c5(isf, 4, 8), c5(isf, 4, 8), c01, OP.max, OP.max)
-        act(a3("nd2", 0, 64), a3("d16"), bias=1.0, scale=-1.0 / 16)
-        act(c5(m64), c5(m1), bias=64.0)
+        yield
+        act(sm, c5(sl_, 3, 4), AF.Relu, bias=-384.0, scale=192.0 / K)
 
-    def fill4():
-        tt(a3("kq"), a3("jb"), a3("d16"), OP.add)
-        powers(0)
-        act(a3("rawq"), a3("kq"), AF.Exp, scale=-LN16)
-        act(a3("nd2", 64, 128), a3("d16"), bias=1.0, scale=-1.0 / 16)
-    fills = [fill1, fill2, fill3, fill4]
-    for f in range(1, F):
-        tot, cum = a("rb1", 2 * f, 2 * f + 1), a("rb1", 2 * f + 1, 2 * f + 2)
-        mm(a("rb1", 2 * f, 2 * f + 2), alls, a("st", 2 * f, 2 * f + 2), True, False)
-        mm(tot, alls, st_l(f), False, False)
-        mm(cum, ge, st_s(f), False, True)
-        fills[f - 1]()
-        s2, ks, lk = a("sm", 4 * f, 4 * f + 1), a("sm", 4 * f + 1, 4 * f + 2), a("cq", 16 + f, 17 + f)
-        ts(s2, cum, 5.0, st_s(f), OP.is_le, OP.mult)
-        ts(ks, tot, thr_(f), t1_(f), OP.is_le, OP.subtract)
-        ts(lk, tot, thr_(f), st_l(f), OP.is_le, OP.mult)
-        ts(st_s(f + 1), s2, ks, c5(new, f, f + 1), OP.mult, OP.add)
-        ts(st_l(f + 1), s2, t1_(f), lk, OP.mult, OP.add)
+    def weave(*threads):
+        live = list(threads)
+        while live:
+            live = [t for t in live if next(t, live) is not live]
 
-    s3, hh = a("sm", 20, 25), a("sm", 26, 31)
-    lg = a("st", 3, 13, 2)
-    rs_, hb, rl, bb = a("rk", 0, 5), a("rk", 5, 10), a("rk", 10, 15), a("rk", 16, 21)
-    tt(s3, a("st", 2, 12, 2), c5(new), OP.subtract)
-    tt(rl, lg, c5(nb), OP.mult)
-    tt(hh, s3, lg, OP.add)
-    tt(rs_, s3, c5(nb), OP.mult)
-    tt(bb, hh, c5(isb), OP.mult)
-    mm(a("ix1", 0, 5), ge, rs_, True, True)
-    mm(a("ix1", 10, 15), alls, rs_, True, False)
-    mm(a("ix1", 10, 15), le, rl, False, True)
-    mm(a("ix1", 5, 10), alls, bb, True, True)
-    tt(hb, hh, c5(nm1), OP.mult)
-    tt(a("pb", 15, 20), hh, c5(m64), OP.mult)
-    scan(c5(e_), hh, c5(lt), 4.0, OP.add, OP.subtract)
-    powers(1)
-    tt(a("pb", 0, 15), a("rk", 0, 15), a("ix1", 0, 15), OP.mult)
-    tt(a("pb", 20, 30), a("pb", 0, 10), a("pb", 10, 20), OP.add)
-    r1 = a("pb", 32, 37)
-    tt(r1, a("pb", 20, 25), a("pb", 25, 30), OP.add)
-    sl, ee = c5(sl_, 3, 4), c5(e_, 4, 5)
-    ex, vs, ve, v1, v0 = a("tv", 24, 29), a("tv", 0, 5), a("tv", 5, 10), a("tv", 10, 15), a("tv", 16, 21)
-    act(ex, r1, AF.Exp, bias=-65.0 * LN16, scale=LN16)
-    ts(v1, r1, 66.0, sl, OP.is_equal, OP.mult)
-    ts(v0, r1, 65.0, sl, OP.is_equal, OP.mult)
-    act(a("base", 128, 256), a("base", 128, 256), bias=nf)
-    preacc(0, [0])
-    explicit(0, 0)
-    ts(vs, ex, sl, None, OP.mult)
-    ts(ve, ex, ee, None, OP.mult)
-    mm(a("rb1", 47, 52), a("a15", 0, 128), v0, True, False)
-    mm(a("rb1", 47, 52), a("an15", 0, 128), v1, False, False)
-    mm(a("rb1", 47, 52), alls, vs, False, True)
-    mm(a("rb1", 32, 47), alls, a("tv", 0, 15), True, True)
-    explicit(0, 1)
-    coords0(0)
-    tt(a("tt", 0, 20), a("rb1", 32, 52), a("arow", 0, 20), OP.add)
-    look(0, 0)
-    look(0, 1)
-    clamp(-192.0)
-    preacc(0, [1])
-    places()
-    ts(a("ta", 0, 128), a("ti", 0, 128), 15, None, OP.bitwise_and)
-    cp(a("dg", 0, 128), a("ta", 0, 128))
-    mm(a("ix1", 128, 256), a("i1k", 0, 128), a("dg", 0, 128), False, True)
-    preacc(0, [2, 3])
-    look(0, 2)
-    ts(a("mio", 0, 12), a("mio", 0, 12), nf, 1.0 / 256, OP.add, OP.mult)
-    ts(a("off", 0, 128), a("ix1", 128, 256), 33.0 * 192, None, OP.add)
-    act(a("mst", 768 + 64, 768 + 128), ev(0, 0, 64))
-    act(a("mst", 768 + 128, 768 + 192), ev(0, 128, 192))
-    act(a3("d3", 0, 64), a3("d16"), scale=1.0 / 16)
+    def start(f):
+        m = 192 * (f + 1)
+        tt(a("xb", 0, 192), gi(a("mst", 0, m), a("moff", 12 * (f - 1), 12 * f)), a3("d3", f, f + 1, 0, 192), OP.mult)
+        act(a("hv", 0, 128), a("xb", 64, 192), bias=191.75, scale=0.5)
+        act(a("zz", 0, 64), a("xb", 0, 64), AF.Relu, bias=-8.0 * K * f)
+        ts(a("zz", 64, 128), a("xb", 0, 64), 8.0 * K * f, one("tt", 15 + f), OP.is_ge, OP.mult)
 
-    def code0():
-        ts(a("ta", 128, 192), a("ti", 128, 192), 15, None, OP.bitwise_and)
-        ts(a("de", 0, 64), a("ta", 128, 192), 16.0, 4.0, OP.mult, OP.add)
-        tt(a("mst", 256 * 3, 256 * 3 + 64), a("dg", 0, 64), a("de", 0, 64), OP.add)
+    def ask():
+        x0, x1, y0, y1 = a("rb0", 0, N), a("rb0", N, 2 * N), a("rb1", 0, N), a("rb1", N, 2 * N)
+        e = [a("eq", 128 * k, 128 * (k + 1), parts=32) for k in range(6)]
+        ts(e[4], a("e4", 0, 128, parts=32), 0.0, None, OP.is_equal)
+        ts(e[5], a("e4", 0, 128, parts=32), 0.0, -1.0, OP.is_equal, OP.mult)
+        for v in range(4):
+            ts(e[v], a("e4", 128, 256, parts=32), float(v), None, OP.is_equal)
+        for v in range(4):
+            o = a("rb1", 128 * v, 128 * v + 128)
+            mms([(o, e[4], e[v]), (o, e[5 if v else 4], e[v - 1 if v else 3])])
+        act(a("w1", 0, 512), a("rb1", 0, 512), scale=0.5)
+        fa, fb, vf, inc = a("fab", 0, N), a("fab", N, 2 * N), a("vf", 0, N), a("inc", 0, N)
+        q0, q1, q2 = [a("qq", k * N, k * N + N) for k in range(3)]
+        ts(fa, a3("jf", L0, F, 0, 64), 5.0, None, OP.is_equal)
+        ts(fb, a3("jf", F + L0, 2 * F, 0, 64), 5.0, None, OP.is_equal)
+        tt(vf, fa, fb, OP.max)
+        ms(a("fm", 0, N), 1.0)
+        ms(a("fm", 0, N, 64), 0.0)
+        ts(one("lcol", 0), one("pcol", 0), 2, 3, OP.arith_shift_right, OP.bitwise_and)
+        cp(lf, one("lcol", 0))
+        act(b4, lf, bias=160.375, scale=-0.25)
+        act(b16, lf, bias=160.0 + 3.0 / 16 - 15.0 / 32, scale=-1.0 / 16)
+        act(et, nf, bias=15.5, scale=16.0)
+        act(n4, ident, scale=-4.0)
+        act(nbig, ident, scale=-16384.0)
+        mm(x0, alls, vf, True, True)
+        scan(inc, a("fm", 0, N), x0, 0.0, OP.mult, OP.add)
+        mms([(x0, ident, inc), (x0, nge, vf)])
+        mms([(x1, ident, inc), (x1, nge4, vf)])
+        mms([(y0, ident, inc), (y0, nalls, vf)])
+        mms([(y1, ident, inc), (y1, nge, vf), (y1, nbig, vf)])
+        act(q0, x0, bias=159.625, scale=0.25)
+        act(q1, x1, bias=b4, scale=0.25)
+        act(q2, x1, bias=b16, scale=1.0 / 16)
+        mms([(x0, ident, inc), (x0, nge, vf), (x0, n4, q0)])
+        mms([(x1, ident, q1), (x1, n4, q2)])
+        for v in range(1, 4):
+            act(a("sgn", (v - 1) * N, v * N), x0, AF.Sign, bias=640.5 - v)
+        for v in range(1, 4):
+            act(a("sgn", (v + 2) * N, (v + 3) * N), x1, AF.Sign, bias=480.5 - v)
+        act(a("sx", 0, N), y0)
+        for j in range(NL):
+            part = a("rb1", 64 * j, 64 * j + 64)
+            act(a("k0", 64 * j, 64 * j + 64), part, bias=130.0 + 32 * j - 15.0 / 32, scale=1.0 / 16)
+            act(a("kp", 64 * j, 64 * j + 64), part, AF.Sign, bias=et, scale=-1.0, acc=one("ec", j))
+            act(a("zq", 64 * j, 64 * j + 64), a("rb1", N + 64 * j, N + 64 * j + 64), bias=16384.0 - 256 * (j + 1))
+        tt(a("kp", 1, N), a("k0", 1, N), a("k0", 0, N - 1), OP.is_equal)
+        act(a("ec", 8, 8 + NL), a("ci", 0, NL), bias=62.0, scale=128.0)
+        tt(a("ec", 4, 4 + NL), a("ec", 0, NL), a("ec", 8, 8 + NL), OP.add)
+        ts(a("eo", 0, NL), a("ec", 4, 4 + NL), 0.5, None, OP.mult)
+        act(a("be", 0, 128), a("base", 0, 128), bias=192.0)
+        act(a("be", 128, 256), a("base", 128, 256), bias=208.0)
+        act(i64k, ident, scale=65536.0)
+        act(i2k, ident, scale=2048.0)
+        for j in range(NL):
+            explicit(L0 + j, a("rb1", 128 * j, 128 * j + 128))
+        for k, bank in enumerate(("rb1", "rb0")):
+            for j in range(NL):
+                o = a(bank, 128 * j, 128 * j + 128)
+                mms([(o, ident, a("be", 128 * k, 128 * k + 128)), (o, ident, ev(L0 + j, 128 * k, 128 * k + 128))])
+            ts(a("cbe", 2 * N * k, 2 * N * (k + 1)), a(bank, 0, 2 * N), 16.0 * k, 16.0 * k + 31, OP.max, OP.min)
+        for i, (my, mx) in enumerate(((i32, ident), (i64k, i2k))):
+            for j in range(NL):
+                o, c = a("rb1", i * N + 64 * j, i * N + 64 * j + 64), 128 * j + 64 * i
+                mms([(o, my, a("cbe", c, c + 64)), (o, mx, a("cbe", 2 * N + c, 2 * N + c + 64))])
+        tt(a("pa", 0, N), fa, y0, OP.mult)
+        tt(x0, fb, y1, OP.mult)
+        tt(x0, a("pa", 0, N), x0, OP.add)
+        for s, (src, dst, w) in enumerate(((x0, y0, "w1"), (y0, x0, "w1"))):
+            for v in range(3):
+                tt(a("pv", v * N, v * N + N), a("sgn", (3 * s + v) * N, (3 * s + v + 1) * N), src, OP.mult)
+            act(a("pf", 0, N), src)
+            mms([(dst, a(w, 128 * v, 128 * v + 128), a("pv", (v - 1) * N, v * N)) for v in range(1, 4)] + [(dst, a(w, 0, 128), a("pf", 0, N))])
+        n, xs, ys, eo = 16 * NL, a("xs", 0, N), a("ys", 0, N), a("eo", 0, NL)
+        act(xs, x0)
+        scan(ys, a("kp", 0, N), xs, 0.0, OP.mult, OP.add)
+        act(a("thr", n, 2 * n), a("thr", 0, n), bias=-16.5)
+        act(a("thr", 0, n), a("thr", 0, n), bias=nf)
+        ms(a("hs", 0, 8), 0.0)
+        tt(a("wm", 0, n), gi(inc, eo), a("thr", 0, n), OP.is_gt)
+        tt(a("wm", n, 2 * n), gi(a("sx", 0, N), eo), a("thr", n, 2 * n), OP.is_gt)
+        tt(a("hs", 8, 8 + n), gi(xs, eo), a("wm", 0, n), OP.mult)
+        tt(a("y1", 0, n), gi(ys, eo), a("hs", 8, 8 + n), OP.subtract)
+        tt(a("y1", n, 2 * n), a("y1", 0, n), a("wm", n, 2 * n), OP.mult)
+        tt(a("ri", 2 * n, 3 * n), a("y1", n, 2 * n), a("hs", 7, 7 + n), OP.add)
+        ts(a("ri", 0, n), a("ri", 2 * n, 3 * n), 2047, None, OP.bitwise_and)
+        ts(a("ri", n, 2 * n), a("ri", 2 * n, 3 * n), 11, None, OP.arith_shift_right)
+        cp(a("rqo", 0, 2 * n), a("ri", 0, 2 * n))
+        for f in range(L0 - 1, F - 1):
+            ms(a("sb", f * SB, f * SB + 16), 255.0)
+        act(n32, ident, scale=-32.0)
 
-    def sigma(f):
-        return 16.0 * f - 0.5
-
-    def fixed1(f):
-        for k in range(3):
-            look(f, k)
-        ts(a("ta", 0, 192), a("ti", 0, 192), 15, None, OP.bitwise_and)
-
-    def fixed2(f):
-        p = f & 1
-        ts(a("de", 0, 64), a("ta", 128, 192), 16.0, 4.0 - f - sigma(f), OP.mult, OP.add)
-        cp(a("dg", 128 * p + 64, 128 * p + 128), a("ta", 64, 128))
-        tt(a("cs", 64 * p, 64 * p + 64), a("ta", 0, 64), a("de", 0, 64), OP.add)
-
-    def mplace(f):
-        ts(a("moff", 12 * (f - 1), 12 * f), a("mio", 0, 12), a("tt", 10 + f, 11 + f), 256.0, OP.add, OP.mult)
+    def answer(f):
+        j, win = f - L0, a("sb", (f - 1) * SB, f * SB)
+        for h in range(2):
+            c = 16 * j + 8 * h
+            act(a("ob", 128 * h, 128 * h + 128), gi(win, a("rq", c, c + 8)), bias=-255.0)
+        for h in range(2):
+            c = 16 * (NL + j) + 8 * h
+            tt(a("uo", 256 * j + 128 * h, 256 * j + 128 * h + 128), gi(win, a("rq", c, c + 8)), a("ob", 128 * h, 128 * h + 128), OP.add)
+        send(a("win", 256 * (F - 1 - f), 256 * (F - f)), a("uo", 256 * j, 256 * j + 256), "va%d_3" % f, "sent%d_3" % f)
 
     def index(f):
-        sg, p, more = sigma(f), f & 1, f < F - 1
-        tt(a("xb", 0, 192), gi(a("mst", 0, 256 * (3 + f)), a("moff", 12 * (f - 1), 12 * f)), af("d3", f, 0, 192), OP.mult)
-        act(a("hv", 0, 128), a("xb", 64, 192), bias=191.75, scale=0.5)
-        act(a("hv", 128, 256), a("xb", 64, 192), bias=191.75, scale=-0.5)
-        turn_back(f - 1, 0)
-        if f == 1:
-            explicit(f, 0)
-            explicit(f, 1)
-        coords0(f)
-        coords(f)
-        turn_back(f - 1, 1)
-        if f == 1:
-            fixed1(f)
-            fixed2(f)
-        ts(a("zz", 0, 64), a("xb", 0, 64), sg, sg, OP.max, OP.subtract)
-        ts(a("nok", 0, 64), a("xb", 0, 64), sg, None, OP.is_lt)
+        more, m = f < F - 1, 192 * (f + 1)
+        turn_back(f - 1)
+        code = a("ix1", 0, 64)
+        terms = [(code, ident, dg(f, 0)), (code, ident, a("zz", 0, 64)), (code, ni, a("zz", 64, 128))]
+        if more:
+            terms.insert(1, (code, i8, dg(f, 2)))
+        mms(terms)
+        y0, y1, x0, x1 = [a("ix0", 64 * k, 64 * k + 64) for k in range(4)]
+        hy, hx = a("hv", 0, 64), a("hv", 64, 128)
+        mms([(a("ix0", 0, 256), ident, a("base", 0, 256)), (y1, ni, a("xb", 64, 128)), (x1, ni, a("xb", 128, 192)),
+             (y0, ident, hy), (y1, ident, hy), (x0, ident, hx), (x1, ident, hx), (a("ix0", 0, 256), ident, ev(f, 0, 256))])
+        act(a("mst", m, m + 64), code)
+        act(a("ef", 0, 64), code, bias=192.0 - 7.0 / 16, scale=1.0 / (8 * K))
+        if more:
+            look(f + 1)
+        clamp()
+        if more:
+            digits(f + 1)
+        op, oq = a("ix0", 256, 320), a("ix0", 320, 384)
+        mms([(a("ix0", 256, 384), i32, a("cb", 0, 128)), (a("ix0", 256, 384), ident, a("cb", 128, 256)), (oq, ident, dg(f, 1)),
+             (op, ident, a("mst", m, m + 64)), (op, n8k, a("ef", 0, 64))])
+        if f >= L0:
+            j, od = f - L0, a("ix0", 384, 448)
+            y0, y1, x0, x1 = [a("cb", 64 * k, 64 * k + 64) for k in range(4)]
+            mms([(od, i32, y1), (od, n32, y0), (od, ident, x1), (od, ni, x0), (od, ident, dg(f, 1))])
+            tt(a("of", 0, 64), a("fab", 64 * j, 64 * j + 64), od, OP.mult)
+            tt(a("of", 128, 192), a("zq", 64 * j, 64 * j + 64), oq, OP.min)
+            tt(a("of", 64, 128), a("of", 0, 64), op, OP.add)
+            op, oq = a("of", 64, 128), a("of", 128, 192)
         if more:
             mplace(f + 1)
-        tt(a("mm", 0, 64), a("cs", 64 * p, 64 * p + 64), a("nok", 0, 64), OP.mult)
-        tt(a("cn", 0, 64), a("zz", 0, 64), a("mm", 0, 64), OP.add)
-        act(a("ef", 0, 64), a("cn", 0, 64), bias=sg / 16 - 15.0 / 32 + 192.0, scale=1.0 / 16)
-        if more and f > 1:
-            fixed1(f + 1)
-        clamp()
-        places()
-        mm(a("ix1", 192, 256), a("i1k", 0, 128), a("dg", 128 * p + 64, 128 * p + 128), False, False)
-        mm(a("ix1", 128, 192), a("i1k", 0, 128), a("cn", 0, 64), False, False)
-        mm(a("ix1", 128, 192), a("in16k", 0, 128), a("ef", 0, 64), False, True)
-        preacc(f, range(4))
+            mms([(a("ix1", 64, 192), ident, a("hv", 0, 128)), (a("ix1", 64, 128), ident, ev(f, 0, 64)), (a("ix1", 128, 192), ident, ev(f, 128, 192))])
+            act(a("mst", m + 64, m + 192), a("ix1", 64, 192), bias=-192.0)
+        ts(a("off", 128 * f, 128 * f + 64), op, 192.0 * 8 * K, None, OP.add)
+        ts(a("off", 128 * f + 64, 128 * f + 128), oq, 256.0 * max(0, f - L0 + 1), None, OP.add)
         if more:
-            if f == 1:
-                fixed1(f + 1)
-            fixed2(f + 1)
-        ts(a("off", 128 * f, 128 * f + 64), a("ix1", 128, 192), 1024.0 * (sg + 3068 + f), None, OP.add)
-        cp(a("off", 128 * f + 64, 128 * f + 128), a("ix1", 192, 256))
-        if more:
-            keepw(f)
-            act(a("mst", 256 * (3 + f), 256 * (3 + f) + 64), a("cn", 0, 64), bias=sg)
-            explicit(f + 1, 0)
-            explicit(f + 1, 1)
+            keep(f + 1)
+        preacc(f)
+        later(f)
 
-    def turn_back(f, h):
-        s = f + 1
-        mm(a("rb%d" % h, 0, 512), a("wide", 128 - 16 * s, 256 - 16 * s), a("sb", f * P + 512 * h, f * P + 512 * h + 512), True, True)
-        act(a("win", (8 + f) * P + 512 * h, (8 + f) * P + 512 * h + 512), a("rb%d" % h, 0, 512))
-        if h == 1:
-            later_loads(f + 1)
-            store(f * P, (f + 1) * P, a("win", (8 + f) * P, (9 + f) * P))
+    def turn_back(f):
+        s, CH = f + 1, (CA if f >= L0 else CW)
+        for k in range(len(CH) - 1):
+            bank = a("u%d" % k, 0, CH[k + 1] - CH[k])
+            mm(bank, a("wide", 128 - 16 * s, 256 - 16 * s), made(f, CH[k], CH[k + 1]), True, True)
+            act(slot(4 + f, CH[k], CH[k + 1]), bank)
 
     def pixels(f):
-        s = (f + 1) % F
-        win = a("win", (4 - f) * P, (8 + f) * P)
+        s, asked = (f + 1) % F, f >= L0
+        CH = CA if asked else CW
+        end = U + (4 + B + f - asked) * P
+        wins = [a("win", U, end), a("win", 256 * (F - 1 - f) if asked else U, end)]
 
-        def unit(i, lo, hi):
+        def gather(i, lo, hi):
             o = 128 * f + 64 * i
-            return a("pq", P * i + lo, P * i + hi), gi(win, a("off", o + lo // 16, o + hi // 16))
-        for x in VUNITS:
-            cp(*unit(*x))
-        for x in SUNITS:
-            act(*unit(*x))
-        for k in range(4):
-            n = CH[k + 1] - CH[k]
-            if f == 0 and k == 2:
-                code0()
-                mplace(1)
-            for i in PQ[k]:
-                mm(a("u%d" % k, 0, n), a("half", 16 * s, 16 * s + 128), a("pq", P * i + CH[k], P * i + CH[k + 1]), False, i == PQ[k][1])
-            ts(a("cr", CH[k], CH[k + 1]), a("u%d" % k, 0, n), MAGIC, MAGIC, OP.add, OP.subtract)
-            ts(a("sb", f * P + CH[k], f * P + CH[k + 1]), a("cr", CH[k], CH[k + 1]), 0.0, 255.0, OP.max, OP.min)
-            if f < F - 1 and k in SENDS:
-                lo, hi = SENDS[k]
-                send(view(f + 1, lo, hi), a("sb", f * P + lo, f * P + hi), "va%d_%d" % (f + 1, k), "sent%d" % (f + 1))
-            if f == F - 1 and k > 0:
-                lo, hi = f * P + CH[k if k > 1 else 0], f * P + CH[k + 1]
-                store(lo, hi, a("sb", lo, hi))
+            return a("pq", P * i + lo, P * i + hi), gi(wins[i], a("off", o + lo // 16, o + hi // 16))
 
+        def half(i, k):
+            mm(a("u%d" % k, 0, CH[k + 1] - CH[k]), a("half", 16 * s, 16 * s + 128), a("pq", P * i + CH[k], P * i + CH[k + 1]))
+
+        def finish(k):
+            n = CH[k + 1] - CH[k]
+            acc = a("u%d" % k, 0, n)
+            for i in range(asked, 2):
+                half(i, k)
+            mm(acc, mup, blank(n))
+            mm(acc, mdn, blank(n), False, True)
+            ts(made(f, CH[k], CH[k + 1]), acc, 0.0, 255.0, OP.max, OP.min)
+            if f < L0 - 1 and k in SENDS:
+                send(slot(5 + f, *SENDS[k]), made(f, *SENDS[k]), "va%d_%d" % (f + 1, k), "sent%d_%d" % (f + 1, k))
+            if f == F - 1 and k in STORES:
+                lo, hi = STORES[k]
+                store(f * P + lo, f * P + hi, made(f, lo, hi))
+        if asked:
+            for x in SPRE:
+                act(*gather(*x))
+            for x in VPRE:
+                cp(*gather(*x))
+            for k in range(len(CH) - 1):
+                half(0, k)
+        line.update(v=[], s=[], t=[])
+        for x in SPOST if asked else SWORK:
+            act(*gather(*x))
+        for x in VPOST if asked else VWORK:
+            if isinstance(x, tuple):
+                cp(*gather(*x))
+            else:
+                finish(x)
+        if L0 - 1 <= f < F - 1:
+            answer(f + 1)
+        line.clear()
+
+    scan(c5(cn_), a("u3", 0, 5), a("one", 0, 5), n1, OP.add, OP.add)
+    ts(gz, one("u3", 0), 1.0, 1.0, OP.min, OP.add)
+    weave(control(), lists(), extras())
+    later(0)
+    act(a("half", 0, 256), wide, scale=0.5)
+    act(i8, ident, scale=8.0)
+    preacc(0)
+    mms([(a("ix0", 256, 384), i32, a("cb", 0, 128)), (a("ix0", 256, 384), ident, a("cb", 128, 256))])
+    for k, table in enumerate((one("t0", 0), one("t0", 1), one("tt", 10))):
+        ts(a("ta0", 64 * k, 64 * k + 64), a("pw", 320 * (k & 1), 320 * (k & 1) + 64), table, None, OP.mult)
+    for lo, hi in ((0, 128), (128, 192)):
+        ts(a("ta0", lo, hi), a("ta0", lo, hi), 7 * 1024, None, OP.bitwise_and)
+    tt(a("o0", 0, 128), a("ta0", 0, 128), a("ix0", 256, 384), OP.add)
+    ts(a("off", 0, 128), a("o0", 0, 128), 33.0 * 192, None, OP.add)
+    ts(dg(0, 2), a("ta0", 128, 192), 8.0, None, OP.mult)
+    tt(a("mst", 192, 256), a("ta0", 0, 64), dg(0, 2), OP.add)
+    look(1)
+    for f in range(1, L0):
+        explicit(f)
+    early[0] = EARLY
+    if NL:
+        ask()
+    early[0] = 0.0
     for f in range(F):
         pixels(f)
+        if NL and f == ASK:
+            send(a("rq", 0, 32 * NL), a("rqo", 0, 32 * NL), "asked", "ask", prv, nxt)
         if f == 0:
-            for j in range(1, 3):
-                act(a3("d3", 64 * j, 64 * j + 64), a3("d16"), scale=1.0 / 16)
+            act(a("mst", 192 + 64, 192 + 128), ev(0, 0, 64))
+            act(a("mst", 192 + 128, 192 + 192), ev(0, 128, 192))
+            act(a3("d3", 1, F, 128, 192), a3("jf", 1, F, 0, 64), AF.Relu, bias=-5.0)
+            act(n8k, ident, scale=-8.0 * K)
+            mplace(1)
+            digits(1)
+            start(1)
+            keep(1)
         if f < F - 1:
+            if f > 0:
+                start(f + 1)
             index(f + 1)
 
+    issue()
     for sem in cnt:
         need("y", (sem, cnt[sem], {}))
     for sem in LOADS:
         need("y", (sem, 16, {}))
+    for sem in sends:
+        need("y", (sem, sends[sem][0], {}))
     need("y", ("stored", stores[0], {}))

@@ -3,58 +3,49 @@ from concourse.mybir import AluOpType as OP, ActivationFunctionType as AF, AxisL
 
 F, P = 5, 1024
 BF, F32, I32, U16 = "bfloat16", "float32", "int32", "uint16"
-CW, CA = [0, 192, 448, 832, 1024], [0, 192, 576, 832, 1024]
-SENDS = {1: (0, 448), 3: (448, 1024)}
-STORES = {1: (0, 448), 2: (448, 832), 3: (832, 1024)}
+HAND = dict(CH=[0, 160, 352, 448, 768, 928, 1024], V="p0 p1 p2 p3 c0 c1 c2 p5 c3 c4 c5", S="q0 q1 q2 q3 p4 q4 q5", OUT={"c2": (0, 448), "c5": (448, 1024)})
+LAST = dict(CH=[0, 128, 320, 544, 768, 960, 1024], V="p0 p1 p2 p3 c0 p4 c1 c2 c3 c4 c5", S="q0 q1 q2 q3 q4 p5 q5",
+            OUT={"c2": (0, 544), "c4": (544, 960), "c5": (960, 1024)})
+BACK = [(0, 0, 448), (3, 448, 768), (4, 768, 1024)]
+MAGIC = 1.5 * 2.0 ** 23
+ONV, PEFIX = 7, 10.0
+SPLIT = 2
 FIRSTV = [(0, 1024)]
-L0 = 5
-NL = F - L0
-ASK = L0 - 2
-B = min(NL, 1)
-N, U, SB = 64 * NL, 256 * NL, P + 16
-VWORK = [(0, 0, 192), (0, 192, 448), (0, 448, 832), 0, 1, 2, 3]
-SWORK = [(1, 0, 192), (1, 192, 448), (1, 448, 832), (0, 832, 1024), (1, 832, 1024)]
-VPRE, SPRE = [(0, 0, 576)], [(0, 576, 1024)]
-VPOST, SPOST = [(1, 192, 576), 0, 1, 2, 3], [(1, 0, 192), (1, 576, 832), (1, 832, 1024)]
-LAG = 3
-WAKE, GATHER, START, ROW, LOCAL, FAR, REMOTE, ONCE, CALL = 130.0, 1.7, 1300.0, 30.0, 0.03, 6.0, 0.06, 2500.0, 1200.0
-ROUNDS, FIRST = 2, 0.0
-EARLY = 0.0
+GROUPS = [(0, 3), (3, 5)]
+WAKE, GATHER, START, ROW, LOCAL, FAR, REMOTE, CALL = 230.0, 1.7, 1300.0, 30.0, 0.03, 6.0, 0.06, 1200.0
+CASES = [(0.0, 0.9), (300.0, 1.0)]
+ORDER = {}
+ROUNDS, SHORT = 4, {"v": 130.0, "s": 130.0, "t": 50.0}
 LN8 = math.log(8.0)
 K = 1024.0
 
 
 def _sb(n, d):
-    return ("sbuf", [128, max(n, 16)] if isinstance(n, int) else [128] + n, d)
+    return ("sbuf", [128, n] if isinstance(n, int) else [128] + n, d)
 
 
 SCRATCH = {
-    "win": _sb(U + 8 * P, BF), "rs": _sb(F * P, BF), "sb": _sb(F * SB, BF), "pq": _sb(2 * P, BF),
-    "e4": _sb(256, F32), "eq": _sb(6 * 128, BF), "w1": _sb(512, F32), "be": _sb(256, BF), "lcol": _sb(4, I32),
-    "fab": _sb(2 * N, BF), "vf": _sb(N, BF), "fm": _sb(N, BF), "inc": _sb(N, BF), "qq": _sb(3 * N, BF), "k0": _sb(N, BF), "sx": _sb(N, BF), "kp": _sb(N, BF),
-    "zq": _sb(N, F32), "sgn": _sb(6 * N, BF), "cbe": _sb(4 * N, BF), "pa": _sb(N, F32), "pf": _sb(N, F32), "pv": _sb(3 * N, F32), "xs": _sb(N, F32), "ys": _sb(N, F32),
-    "ec": _sb(16, F32), "eo": _sb(4, U16), "thr": _sb(32 * NL, F32), "wm": _sb(32 * NL, F32), "hs": _sb(16 * NL + 8, F32), "y1": _sb(32 * NL, F32),
-    "ri": _sb(48 * NL, I32), "rqo": _sb(32 * NL, U16), "rq": _sb(32 * NL, U16), "ob": _sb(256, BF), "uo": _sb(U, BF), "of": _sb(192, F32),
+    "win": _sb(8 * P, BF), "rs": _sb(F * P, BF), "sb": _sb(F * P, BF), "pq": _sb(2 * P, BF), "cr": _sb(P, BF),
     "ctl": _sb(26, I32), "ctlb": _sb(26, BF),
     "ja": _sb(320, I32), "jb": _sb(320, I32), "wy": _sb(640, I32), "wx": _sb(640, I32),
     "jf": _sb([2 * F, 64], BF), "r6": _sb(320, BF), "d3": _sb([F, 192], BF), "pw": _sb(640, BF), "ev": _sb(F * 256, BF),
-    "pcol": _sb(4, I32), "ncol": _sb(4, I32), "col": _sb(24, F32), "f0": _sb(16, BF), "t0": _sb(16, F32), "o0": _sb(128, F32), "ta0": _sb(192, I32), "ci": _sb(16, F32), "one": _sb(8, BF), "arow": _sb(25, F32),
+    "pcol": _sb(4, I32), "ncol": _sb(4, I32), "col": _sb(16, F32), "ci": _sb(16, F32), "one": _sb(8, BF),
     "repi": _sb(128, BF), "rep": _sb(128, BF), "i16": _sb(16, BF), "dif": _sb(128, BF), "wide": _sb(256, BF), "half": _sb(256, BF),
     "base": _sb(256, BF), "mio": _sb(12, F32), "moff": _sb(48, U16), "mst": _sb(6 * 192, BF),
     "c": _sb(128, F32), "cq": _sb(8, BF), "st": _sb(16, BF), "sm": _sb(8, F32), "key": _sb(8, F32), "sg": _sb(8, F32),
-    "dd": _sb(80, BF), "junk": _sb(80, BF), "tv": _sb(64, BF), "tt": _sb(25, F32),
+    "dd": _sb(80, BF), "junk": _sb(80, BF), "tv": _sb(80, BF), "arow": _sb([5, F], F32), "tt": _sb([5, F], F32),
+    "f0": _sb(6, BF), "o0": _sb(128, F32), "ta0": _sb(192, I32),
     "ti": _sb(192, I32), "ta": _sb(192, I32), "dg": _sb(F * 192, BF),
     "xb": _sb(192, BF), "hv": _sb(128, BF), "zz": _sb(128, BF), "ef": _sb(64, BF), "cb": _sb(256, BF), "off": _sb(F * 128, U16),
 }
-MATS = ("alls", "ge", "a18", "a7", "an7", "a8", "i32", "i8", "ni", "n8k", "n16", "quar", "unit", "mup", "mdn",
-        "nalls", "nge", "nge4", "n4", "nbig", "i64k", "i2k", "n32")
+MATS = ("alls", "ge", "a18", "a7", "an7", "a8", "i32", "i8", "ni", "n8k", "n16", "quar", "unit", "mup", "mdn", "i6")
 for _k in MATS:
     SCRATCH[_k] = _sb(128, BF)
-for _k in ("u0", "u1", "u2", "u3", "rb0", "rb1", "ix0", "ix1"):
+for _k in ("u0", "u1", "u2", "u3", "u4", "u5", "ix0", "ix1"):
     SCRATCH[_k] = ("psum", [128, 512], F32)
-LOADS = (["ls1_%d" % k for k in range(len(FIRSTV))] + ["ls0", "lg", "lc", "lr", "lja", "ljb"] + ["l%s%d" % (n, k) for n in ("wy", "wx") for k in range(2)] + ["lrs%d" % f for f in range(F)])
-SEMAPHORES = (["cv", "cs", "ct", "cg", "stored", "asked", "ask"] + LOADS
-              + ["%s%d_%d" % (n, f, k) for n in ("va", "sent") for f in range(F) for k in range(4)])
+LOADS = (["ls1_%d" % k for k in range(len(FIRSTV))] + ["ls0", "lg", "lc", "lr", "lja0", "ljb0", "lja1", "ljb1"]
+         + ["l%s%d" % (n, k) for n in ("wy", "wx") for k in range(3)] + ["lrs%d" % f for f in range(F)])
+SEMAPHORES = ["cv", "cs", "ct", "cg", "stored"] + LOADS + ["%s%d_%d" % (n, f, k) for n in ("va", "sent") for f in range(F) for k in range(3)]
 
 
 def rank_program(g, core, T, topo):
@@ -63,9 +54,7 @@ def rank_program(g, core, T, topo):
         return
     nxt = T.cores[(rank + 1) % len(T.cores)]
     prv = T.cores[(rank - 1) % len(T.cores)]
-
-    def engines(src, dst):
-        return len(topo.engines(src, dst))
+    nout, nin = len(topo.engines(core, nxt)), len(topo.engines(prv, core))
     Q = {"v": g.vector, "s": g.scalar, "t": g.tensor, "g": g, "y": g.sync}
     cnt = {"cv": 0, "cs": 0, "ct": 0, "cg": 0}
     known = {e: {} for e in Q}
@@ -102,7 +91,7 @@ def rank_program(g, core, T, topo):
                 for name, lo, hi in x[1]:
                     hist.setdefault(name, []).append((lo, hi, wr, e, tok))
 
-    calls, seen, line, soft, early = [], {}, {}, set(), [0.0]
+    calls, seen, line, soft = [], {}, {}, set()
 
     def width(x):
         return sum(hi - lo for _, lo, hi in x[1])
@@ -127,25 +116,48 @@ def rank_program(g, core, T, topo):
             for x in group:
                 for name, lo, hi in x[1]:
                     seen.setdefault(name, []).append((lo, hi, wr, len(calls)))
-        calls.append((e, cost, flight, before, emit, FIRST if line else early[0]))
+        calls.append((e, cost, flight, before, emit, line.get(e)))
         return len(calls) - 1
 
     def issue():
-        def gap(j, k):
-            e, cost, flight = calls[j][:3]
-            if (j, k) in soft or (e == calls[k][0] and e in "tgy"):
-                return max(cost, flight if calls[k][2] else 0.0)
-            return WAKE + (START + flight if flight else cost)
+        def links(once, far):
+            on, back = [[] for _ in calls], [[] for _ in calls]
+            for k, c in enumerate(calls):
+                for j in c[3]:
+                    e, cost, flight = calls[j][:3]
+                    if (j, k) in soft or (e == c[0] and e in "tgy"):
+                        gap = max(cost, flight if c[2] else 0.0)
+                    elif flight:
+                        gap = WAKE + (START + flight) * (far if e == "g" else 1.0) + (once if j == sends["sent0_0"] else 0.0)
+                    else:
+                        gap = WAKE + cost
+                    on[j].append((k, gap))
+                    back[k].append((j, gap + c[1] - cost))
+            return on, back
 
-        def plan(users, at, rank_):
+        def span(done, on):
+            at, free = [0.0] * n, {e: 0.0 for e in Q}
+            for k in done:
+                at[k] = max(at[k], free[calls[k][0]])
+                free[calls[k][0]] = at[k] + calls[k][1]
+                for j, lag in on[k]:
+                    at[j] = max(at[j], at[k] + lag)
+            return max(at[k] + calls[k][1] + tail[k] for k in range(n))
+
+        def plan(users, at, weight):
             left = [0] * n
-            for row_ in users:
-                for k, lag in row_:
+            for links in users:
+                for k, lag in links:
                     left[k] += 1
             ready, free, done = {e: [k for k in range(n) if not left[k] and calls[k][0] == e] for e in Q}, {e: 0.0 for e in Q}, []
+            busy = {e: 0 for e in Q}
             while len(done) < n:
-                end, e = min((max(at[k], free[e]) + calls[k][1], e) for e in Q for k in ready[e])
-                k = max((j for j in ready[e] if max(at[j], free[e]) < end), key=lambda j: (rank_[j], -j))
+                may = {e: [k for k in ready[e] if not busy[e] or calls[k][5] or calls[k][1] <= SHORT[e]] for e in Q}
+                may = may if any(may.values()) else ready
+                end, e = min((max(at[k], free[e]) + calls[k][1], e) for e in Q for k in may[e])
+                k = max((j for j in may[e] if max(at[j], free[e]) < end), key=lambda j: (weight[j], -j))
+                if calls[k][5]:
+                    busy[e] = (busy[e] or len(calls[k][5])) - 1
                 ready[e].remove(k)
                 at[k] = max(at[k], free[e])
                 free[e] = at[k] + calls[k][1]
@@ -157,18 +169,21 @@ def rank_program(g, core, T, topo):
                         ready[calls[j][0]].append(j)
             return done, [at[k] + calls[k][1] for k in range(n)]
         n = len(calls)
-        on, back = [[] for _ in calls], [[] for _ in calls]
-        for k, c in enumerate(calls):
-            for j in c[3]:
-                on[j].append((k, gap(j, k)))
-                back[k].append((j, gap(j, k) + c[1] - calls[j][1]))
         tail = [START + c[2] - c[1] if c[2] else 0.0 for c in calls]
-        chain = [0.0] * n
-        for j in reversed(range(n)):
-            chain[j] = max([tail[j] + calls[j][1]] + [lag + chain[k] for k, lag in on[j]])
-        for _ in range(ROUNDS):
-            chain = plan(back, list(tail), plan(on, [0.0] * n, [x + c[5] for x, c in zip(chain, calls)])[1])[1]
-        for k in plan(on, [0.0] * n, [x + c[5] for x, c in zip(chain, calls)])[0]:
+        if ORDER.get("n") != n:
+            cases, best = [links(*c) for c in CASES], None
+            for on, back in cases:
+                chain = [0.0] * n
+                for j in reversed(range(n)):
+                    chain[j] = max([tail[j] + calls[j][1]] + [lag + chain[k] for k, lag in on[j]])
+                for _ in range(ROUNDS):
+                    done, ends = plan(on, [0.0] * n, chain)
+                    length = sum(span(done, c[0]) for c in cases)
+                    if best is None or length < best[0]:
+                        best = (length, done)
+                    chain = plan(back, list(tail), ends)[1]
+            ORDER.update(n=n, done=best[1])
+        for k in ORDER["done"]:
             calls[k][4]()
 
     def run(e, outs, ins, call, rate=1.0, fixed=0.0):
@@ -232,7 +247,7 @@ def rank_program(g, core, T, topo):
             run("s", [o, acc], [i, bias, scale], lambda: g.scalar.activation(o[0], i[0], func, bias=u(bias), scale=u(scale), accum_out=acc[0]))
 
     def mm(o, l, r, start=False, stop=False):
-        run("t", [o], [l, r], lambda: g.tensor.matmul(o[0], l[0], r[0], start, stop), 2.0 if SCRATCH[l[1][0][0]][2] == F32 else 0.5)
+        run("t", [o], [l, r], lambda: g.tensor.matmul(o[0], l[0], r[0], start, stop), 0.5, PEFIX)
 
     def mms(terms):
         for k, (o, l, r) in enumerate(terms):
@@ -275,23 +290,24 @@ def rank_program(g, core, T, topo):
 
     sends = {}
 
-    def send(dst, src, rsem, lsem, to=nxt, frm=prv):
+    def send(f, k, dst, src):
+        rsem, lsem = "va%d_%d" % (f, k), "sent%d_%d" % (f, k)
+
         def emit():
             order("g", [], [src])
-            g.remote_dma(out_ap=dst[0], in_ap=src[0], remote_sem=T.sem[rsem], local_sem=T.sem[lsem], pid=topo.addr(to)[1], routing_id=topo.addr(to)[0],
-                         dma_engine_mask=topo.mask(core, to))
-        n = engines(core, to)
-        note("r", [dst], [], (rsem, engines(frm, core), {}))
-        sends[lsem] = (n, add("g", [dst], [src], CALL, emit, 128 // n * (FAR + REMOTE * row(src)) + (0.0 if sends else ONCE)))
+            g.remote_dma(out_ap=dst[0], in_ap=src[0], remote_sem=T.sem[rsem], local_sem=T.sem[lsem], pid=topo.addr(nxt)[1], routing_id=topo.addr(nxt)[0],
+                         dma_engine_mask=topo.mask(core, nxt))
+        note("r", [dst], [], (rsem, nin, {}))
+        sends[lsem] = add("g", [dst], [src], CALL, emit, 128 // nout * (FAR + REMOTE * row(src)))
 
     def slot(k, lo=0, hi=P):
-        return a("win", U + (k - 1 + B) * P + lo, U + (k - 1 + B) * P + hi)
+        return a("win", k * P + lo, k * P + hi)
 
     def blank(n):
-        return slot(1, 0, n)
+        return slot(0, 0, n)
 
     def made(f, lo, hi):
-        return a("sb", f * SB + 16 + lo, f * SB + 16 + hi)
+        return a("sb", f * P + lo, f * P + hi)
 
     def vectors(k, lo, hi):
         load("y", a("wy", lo, hi), T.vy[:, lo:hi], "lwy%d" % k)
@@ -304,128 +320,100 @@ def rank_program(g, core, T, topo):
     load("y", a("ctl", 10, 25, parts=8), T.rel[:], "lr")
     load("s", a("ctl", 5, 10, parts=8), T.cmd[:], "lc")
     for k, (lo, hi) in enumerate(FIRSTV):
-        load("y", slot(3, lo, hi), T.pic0[:, P + lo:P + hi], "ls1_%d" % k)
-    load("y", a("ja", 0, 320), T.ia[:], "lja")
-    load("y", a("jb", 0, 320), T.ib[:], "ljb")
+        load("y", slot(2, lo, hi), T.pic0[:, P + lo:P + hi], "ls1_%d" % k)
+    load("y", a("ja", 0, 128), T.ia[:, 0:128], "lja0")
+    load("y", a("jb", 0, 128), T.ib[:, 0:128], "ljb0")
     vectors(0, 0, 128)
-    load("y", slot(2), T.pic0[:, 0:P], "ls0")
     residual(0)
-    vectors(1, 128, 640)
+    load("y", slot(1), T.pic0[:, 0:P], "ls0")
+    vectors(1, 128, 256)
 
     def later(f):
-        n, k = sends["sent%d_3" % f]
-        gate.append((("sent%d_3" % f, n, {}), k))
+        sem = [s for s in sends if s.startswith("sent%d" % f)][-1]
+        gate.append(((sem, nout, {}), sends[sem]))
         if f < F - 1:
             residual(f + 1)
+        if f == 0:
+            load("y", a("ja", 128, 320), T.ia[:, 128:320], "lja1")
+            load("y", a("jb", 128, 320), T.ib[:, 128:320], "ljb1")
+            vectors(2, 256, 640)
         if f > 0:
-            store((f - 1) * P, f * P, slot(3 + f))
+            store((f - 1) * P, f * P, slot(2 + f))
 
-    nf, n1, nb0, nb1, cl, c01, gz, cz, ee, sm, ek, lf, b4, b16, et, hn, h0 = [one("col", k) for k in range(17)]
-    alls, ge, a18, a7, an7, a8, i32, i8, ni, n8k, n16, quar, unit, mup, mdn, nalls, nge, nge4, n4, nbig, i64k, i2k, n32 = [a(n, 0, 128) for n in MATS]
-    wide, ident, i16 = a("wide", 0, 256), a("wide", 0, 128), a("i16", 0, 16)
+    nf, n1, nb0, nb1, cl, c01, gz, cz, ee, sm, s1, hn, h0, hp = [one("col", k) for k in range(14)]
+    alls, ge, a18, a7, an7, a8, i32, i8, ni, n8k, n16, quar, unit, mup, mdn, i6 = [a(n, 0, 128) for n in MATS]
+    wide, ident, i16, rep = a("wide", 0, 256), a("wide", 0, 128), a("i16", 0, 16), a("rep", 0, 128, parts=8)
     iota(one("pcol", 0), [[0, 1]], 0, 1, False)
     iota(a("repi", 0, 128, parts=8), [[1, 8], [0, 16]], 0, -1)
-    iota(a("ci", 0, 16), [[1, 16]], 0, 0)
     iota(a("dif", 0, 128), [[1, 128]], 0, -1)
-    rep = a("rep", 0, 128, parts=8)
+    iota(a("ci", 0, 16), [[1, 16]], 0, 0)
+    for k, (lo, hi) in enumerate(FIRSTV):
+        send(0, k, slot(3, lo, hi), slot(2, lo, hi))
+    iota(slot(0, 512, P), [[0, P - 512]], 128, 0)
+    ms(blank(128), 128.0)
+    ms(slot(0, 128, 512), 128.0)
     ms(a("c", 120, 128), 0.0)
     act(a("one", 0, 8), a("c", 120, 128), AF.Exp, fixed=1600.0)
-    ts(one("ncol", 0), one("pcol", 0), 15, None, OP.bitwise_and)
     ms(quar, 2.0 ** -16)
-    cp(nf, one("ncol", 0))
     ms(unit, 2.0 ** -14)
     ms(mup, 768.0)
     ms(mdn, -768.0)
+    ms(a("mst", 0, 192), 0.0)
+    ms(a3("arow", 0, 5, 0, F), 0.0)
+    ts(one("ncol", 0), one("pcol", 0), 15, None, OP.bitwise_and)
+    cp(nf, one("ncol", 0))
+    ts(n1, nf, -1.0, 1.0, OP.mult, OP.add)
+    act(nb0, nf, bias=K, scale=K)
+    act(nb1, nf, bias=-239.0)
+    act(cl, nf, bias=255.0, scale=-2.0)
+    ts(hn, nf, 0.5, None, OP.mult)
+    ts(c01, nf, 2.0, nb0, OP.is_lt, OP.mult)
+    ts(i16, a("ci", 0, 16), nf, None, OP.is_equal)
     ts(rep, a("repi", 0, 128, parts=8), 0.0, None, OP.is_equal)
     mm(a("u1", 0, 128), rep, rep, True, True)
-    ts(n1, nf, -1.0, 1.0, OP.mult, OP.add)
-    ts(nb0, nf, K, K, OP.mult, OP.add)
-    ts(nb1, nf, -239.0, None, OP.add)
     cp(alls, a("u1", 0, 128))
-    ts(cl, nf, -2.0, 255.0, OP.mult, OP.add)
-    ts(i16, a("ci", 0, 16), nf, None, OP.is_equal)
-    ts(c01, nf, 2.0, nb0, OP.is_lt, OP.mult)
-    ts(ident, a("dif", 0, 128), 0.0, None, OP.is_equal)
-    ms(a("arow", 0, 25), 0.0)
-    ms(blank(128), 128.0)
-    cp(a("ctlb", 0, 25, parts=8), a("ctl", 0, 25, parts=8))
-    mm(a("u3", 0, 25), rep, a("ctlb", 0, 25, parts=8), True, True)
-    ts(a("wide", 128, 256), a("dif", 0, 128), 0.0, None, OP.is_equal)
-
-    def select(o, i, pat):
-        run("g", [o], [i], lambda: g.affine_select(o[0], i[0], pat, OP.is_ge, 0.0, 0, 1), 2.0, 200.0)
-    ts(hn, nf, 0.5, None, OP.mult)
+    for h in range(2):
+        ts(a("wide", 128 * h, 128 * h + 128), a("dif", 0, 128), 0.0, None, OP.is_equal)
     act(ge, a("dif", 0, 128), AF.Abs, bias=hn)
     ts(ge, ge, hn, None, OP.is_le)
-    iota(a("base", 0, 128), [[0, 2], [1, 32], [0, 2]], -192, 0)
-    for k, (lo, hi) in enumerate(FIRSTV):
-        send(slot(4, lo, hi), slot(3, lo, hi), "va0_%d" % k, "sent0_%d" % (3 if hi == P else k))
+    ts(hp, one("pcol", 0), 0.5, -192.25, OP.mult, OP.add)
     for k in range(2):
+        act(a("base", 64 * k, 64 * k + 64), a("dif", 0, 64), bias=hp, scale=0.5)
         act((T.base[:, 128 + k:256:2], [("base", 128 + 64 * k, 192 + 64 * k)]), blank(64), bias=nf, scale=(16.0 * k - 192.0) / 128)
     act(a("mio", 0, 12), a("ci", 0, 12), bias=nf, scale=16.0)
-    ms(a("mst", 0, 192), 0.0)
-    if NL:
-        act(nalls, alls, scale=-1.0)
-        select(nge, nalls, [[-1, 128]])
-        select(nge4, nalls, [[-16, 8], [0, 4], [-4, 4]])
-        iota(a("e4", 0, 128, parts=32), [[1, 32], [0, 4]], 0, -1)
-        iota(a("e4", 128, 256, parts=32), [[16, 8], [1, 4], [4, 4]], 0, -4)
-        iota(a("thr", 0, 16 * NL), [[0, NL], [16, 16]], 16, 0)
-        iota(slot(0), [[0, P]], 255, 0)
-        ms(slot(1, 128, P), 128.0)
-    else:
-        iota(slot(1, 128, P), [[0, P - 128]], 128, 0)
-    act(a18, alls, scale=2.0 ** 18)
-    act(a7, alls, scale=7.0)
-    act(an7, alls, scale=-7.0)
-    act(n16, ident, scale=-16.0)
-    act(ni, ident, scale=-1.0)
-    act(i32, ident, scale=32.0)
+    for k, (m, src, x) in enumerate(((n16, ident, -16.0), (ni, ident, -1.0), (a18, alls, 2.0 ** 18), (a7, alls, 7.0), (an7, alls, -7.0), (i32, ident, 32.0),
+                                     (a("half", 0, 256), wide, 0.5), (a8, alls, 8.0), (i8, ident, 8.0), (n8k, ident, -8.0 * K))):
+        if k < ONV:
+            ts(m, src, x, None, OP.mult)
+        else:
+            act(m, src, scale=x)
+    for k in range(2):
+        act(a3("arow", k, k + 1, 0, F), a("ci", 3, 8), scale=2.0 ** 25)
+    act(a3("arow", 3, 4, 0, F), a("ci", 0, 5), scale=-8.0 * K)
 
-    def ev(f, lo, hi):
-        return a("ev", 256 * f + lo, 256 * f + hi)
-
-    def dg(f, k):
-        return a("dg", 192 * f + 64 * k, 192 * f + 64 * k + 64)
-
-    def explicit(f, nd=a("ix0", 384, 512)):
-        mms([(nd, unit, blank(128)), (nd, ni, a3("d3", f, f + 1, 0, 128))])
+    def places(lo, hi, bank):
+        ja = a3("jf", lo, hi, 0, 64)
+        cp(ja, a("ja", 64 * lo, 64 * hi))
+        for j in range(3 if lo else 1):
+            act(a3("d3", lo, hi, 64 * j, 64 * j + 64), ja, AF.Relu, bias=-5.0)
+        for f in range(lo, hi):
+            o, d = a(bank[0], bank[1] + 64 * (f - lo), bank[1] + 64 * (f - lo + 1)), a3("d3", f, f + 1, 0, 64)
+            mm(o, i6, d, True, True)
+        tt(a3("jf", F + lo, F + hi, 0, 64), a("jb", 64 * lo, 64 * hi), a(bank[0], bank[1], bank[1] + 64 * (hi - lo)), OP.max)
         for k in range(2):
-            tt(ev(f, 128 * k, 128 * k + 128), a(("wy", "wx")[k], 128 * f, 128 * f + 128), nd, OP.mult)
-
-    def clamp(lo=0.0):
-        ts(a("cb", 0, 256), a("ix0", 0, 256), lo, lo + 31.0, OP.max, OP.min)
-
-    def preacc(f):
-        s, CH = (f + 1) % F, (CA if f >= L0 else CW)
-        for k in range(len(CH) - 1):
-            n = CH[k + 1] - CH[k]
-            mm(a("u%d" % k, 0, n), a("wide", 16 * s, 16 * s + 128), a("rs", f * P + CH[k], f * P + CH[k + 1]), True)
-            mm(a("u%d" % k, 0, n), quar, blank(n))
-
-    def look(f):
-        for k in range(3 if f < F - 1 else 2):
-            p = 320 * (k & 1) + 64 * f
-            ts(a("ti", 64 * k, 64 * k + 64), a("pw", p, p + 64), one("tt", 5 * k + f), None, OP.mult)
-
-    def digits(f):
-        n = 192 if f < F - 1 else 128
-        ts(a("ta", 0, n), a("ti", 0, n), 7 * 1024, None, OP.bitwise_and)
-
-    def keep(f):
-        n = 192 if f < F - 1 else 128
-        cp(a("dg", 192 * f, 192 * f + n), a("ta", 0, n))
-
-    def mplace(f):
-        ts(a("moff", 12 * (f - 1), 12 * f), a("mio", 0, 12), one("tt", 20 + f), None, OP.add)
+            act(a("pw", 320 * k + 64 * lo, 320 * k + 64 * hi), a3("jf", F * k + lo, F * k + hi, 0, 64), AF.Exp, scale=-LN8)
+    ts(i6, ident, 6.0, None, OP.mult)
+    places(0, 1, ("u0", 0))
+    places(1, SPLIT, ("u0", 64))
 
     def c5(k, lo=0, hi=5):
         return a("c", 8 * k + lo, 8 * k + hi)
-    cn_, tx, tc, lt, m0, m1, kb, isf, sl_, hs, he, ka, ths, thl, k2 = range(15)
+    cn_, tx, tc, lt, m0, m1, kb, isf, sl_, hk, ka, ths, thl, k2 = range(14)
+    slc = c5(sl_, 3, 4)
 
-    def tv(k, lo=0, hi=5):
+    def tv(k, lo, hi):
         return a("tv", 8 * k + lo, 8 * k + hi)
-    ex, vs, v0, v1, ve, v0e, v1m = range(7)
+    ex, eh, s14, vs, v0, v1, ve, v0e, v1m = range(9)
 
     def short(f):
         return one("st", f)
@@ -433,378 +421,217 @@ def rank_program(g, core, T, topo):
     def long_(f):
         return one("st", 5 + f)
 
+    def table(k, f):
+        return a3("tt", k, k + 1, f, f + 1)
+
     def place(bank, lo, hi):
+        for f in range(lo, hi):
+            act(c5(ka, f, f + 1), long_(f), bias=c5(kb, f, f + 1), scale=cl)
+            act(one("key", f), short(f), bias=c5(ka, f, f + 1), scale=256.0)
+            act(a("dd", 16 * f, 16 * f + 16), i16, scale=one("key", f))
         keys = a(bank, 64 + 16 * lo, 64 + 16 * hi)
         mms([(keys, quar, blank(16 * (hi - lo))), (keys, alls, a("dd", 16 * lo, 16 * hi))])
         for f in range(lo, hi):
             act(a("junk", 16 * f, 16 * f + 16), a(bank, 64 + 16 * f, 80 + 16 * f), AF.Sign, bias=one("key", f), scale=-1.0, acc=one("sg", f))
+        act(tv(ex, lo, hi), a("sg", lo, hi), AF.Exp, bias=7.0 * LN8, scale=-LN8 / 2)
 
-    def control():
-        tt(c5(tx), c5(cn_), a("u3", 10, 25, 3), OP.is_equal)
-        ts(c5(lt), c5(cn_), 0.0, None, OP.is_gt)
-        ts(cz, one("u3", 5), gz, one("u3", 5), OP.is_le, OP.mult)
-        yield
-        ts(c5(tc, 0, 1), c5(tx, 0, 1), cz, None, OP.mult)
-        tt(c5(tc, 1, 5), c5(tx, 1, 5), a("u3", 6, 10), OP.mult)
-        tt(a("cq", 1, 5), c5(lt, 1, 5), c5(lt, 0, 4), OP.subtract)
-        yield
-        ts(short(0), c5(tc, 0, 1), 0.0, c5(lt, 0, 1), OP.is_equal, OP.mult)
-        ts(long_(0), c5(tc, 0, 1), 1.0, None, OP.is_equal)
-        ts(c5(k2), c5(tc), 2.0, None, OP.not_equal)
-        act(c5(thl), c5(tc), AF.Abs, bias=-100.0, scale=100.0)
-        act(c5(ths), c5(tc), bias=-11.0, scale=-100.0)
-        act(c5(thl), c5(thl), bias=-11.0, scale=-1.0)
-        for f in range(1, F):
-            cum, lk = one("u1", f), one("sm", f)
-            mms([(cum, ge, one("cq", f)), (cum, n16, one("cq", f)), (cum, alls, long_(f - 1)), (cum, ge, short(f - 1)), (cum, n16, short(f - 1))])
-            ts(lk, long_(f - 1), c5(k2, f, f + 1), None, OP.mult)
-            yield
-            act(c5(ka, f - 1, f), long_(f - 1), bias=c5(kb, f - 1, f), scale=cl)
-            act(one("key", f - 1), short(f - 1), bias=c5(ka, f - 1, f), scale=256.0)
-            act(a("dd", 16 * f - 16, 16 * f), i16, scale=one("key", f - 1))
-            if f == 1:
-                place("u2", 0, 1)
-                act(tv(ex, 0, 1), one("sg", 0), AF.Exp, bias=7.0 * LN8, scale=-LN8 / 2)
-                f0, f1, fs = [one("f0", k) for k in range(3)]
-                ts(h0, one("key", 0), 0.0, c01, OP.is_gt, OP.mult)
-                ts(f0, one("sg", 0), 14.0, c01, OP.is_equal, OP.mult)
-                ts(f1, one("sg", 0), 12.0, c01, OP.is_equal, OP.mult)
-                act(fs, tv(ex, 0, 1), scale=h0)
-                mms([(one("u2", 0), a18, f0), (one("u2", 0), alls, fs)])
-                mms([(one("u2", 1), a7, f0), (one("u2", 1), a18, f1), (one("u2", 1), an7, f1), (one("u2", 1), alls, fs)])
-                act(a("t0", 0, 2), a("u2", 0, 2), bias=K * (B * (8 ** 6 + sum(8 ** k for k in range(5))) + (3 + B) * 8 ** 5))
-            yield
-            ts(short(f), cum, c5(ths, f, f + 1), None, OP.is_le)
-            ts(long_(f), cum, c5(thl, f, f + 1), lk, OP.is_le, OP.add)
-        place("ix1", 1, 4)
-        yield
-        ts(c5(ka, 4, 5), long_(4), cl, c5(kb, 4, 5), OP.mult, OP.add)
-        total(ee, a("st", 0, 11))
-        yield
-        ts(one("key", 4), short(4), 256.0, c5(ka, 4, 5), OP.mult, OP.add)
-        act(ek, ee, scale=K)
-        yield
-        ts(a("dd", 64, 80), i16, one("key", 4), None, OP.mult)
-        place("ix1", 4, 5)
-        act(tv(ex, 1, 5), a("sg", 1, 5), AF.Exp, bias=7.0 * LN8, scale=-LN8 / 2)
-        slc = c5(sl_, 3, 4)
-        ts(c5(hs), a("key", 0, 5), 0.0, slc, OP.is_gt, OP.mult)
-        ts(c5(he), a("key", 0, 5), 0.0, ek, OP.is_gt, OP.mult)
-        yield
-        yield
-        ts(tv(v0), a("sg", 0, 5), 14.0, slc, OP.is_equal, OP.mult)
-        ts(tv(v1), a("sg", 0, 5), 12.0, slc, OP.is_equal, OP.mult)
-        ts(tv(v0e), a("sg", 0, 5), 14.0, ek, OP.is_equal, OP.mult)
-        ts(tv(v1m), a("sg", 0, 5), 12.0, sm, OP.is_equal, OP.mult)
-        tt(tv(vs), tv(ex), c5(hs), OP.mult)
-        tt(tv(ve), tv(ex), c5(he), OP.mult)
-        b = [a("ix1", 192 + 5 * k, 197 + 5 * k) for k in range(5)]
-        mms([(b[3], alls, tv(v0)), (b[3], a8, tv(v0e))])
-        mms([(b[4], alls, tv(v1m))])
-        mms([(b[0], a18, tv(v0)), (b[0], alls, tv(vs))])
-        mms([(b[1], a7, tv(v0)), (b[1], a18, tv(v1)), (b[1], an7, tv(v1)), (b[1], alls, tv(vs))])
-        mms([(b[2], a18, tv(v0e)), (b[2], alls, tv(ve))])
-        yield
-        tt(a("tt", 0, 25), a("ix1", 192, 217), a("arow", 0, 25), OP.add)
+    def tables(bank, lo, hi):
+        w, sg = hi - lo, a("sg", lo, hi)
+        ts(c5(hk, lo, hi), a("key", lo, hi), 0.0, K, OP.is_gt, OP.mult)
+        tt(tv(eh, lo, hi), tv(ex, lo, hi), c5(hk, lo, hi), OP.mult)
+        ts(tv(s14, lo, hi), sg, 14.0, K, OP.is_equal, OP.mult)
+        ts(tv(v1, lo, hi), sg, 12.0, slc, OP.is_equal, OP.mult)
+        ts(tv(v1m, lo, hi), sg, 12.0, sm, OP.is_equal, OP.mult)
+        for o, i, x in ((vs, eh, s1), (v0, s14, s1), (ve, eh, ee), (v0e, s14, ee)):
+            act(tv(o, lo, hi), tv(i, lo, hi), scale=x)
+        b = [a(bank, 192 + w * k, 192 + w * k + w) for k in range(5)]
+        mms([(a(bank, 192, 192 + 5 * w), alls, a("mst", 0, 5 * w))]
+            + [(b[k], m, tv(x, lo, hi)) for k, m, x in ((1, a18, v1), (1, an7, v1), (4, alls, v1m), (0, a18, v0), (1, a7, v0), (3, alls, v0), (0, alls, vs),
+                                                        (1, alls, vs), (2, a18, v0e), (3, a8, v0e), (2, alls, ve))])
+        tt(a3("tt", 0, 5, lo, hi), a(bank, 192, 192 + 5 * w), a3("arow", 0, 5, lo, hi), OP.add)
 
-    def lists():
-        for _ in range(LAG):
-            yield
-        ja = a3("jf", 0, F, 0, 64)
-        cp(ja, a("ja", 0, 320))
-        act(a("r6", 0, 320), ja, AF.Relu, bias=-30.0, scale=6.0)
-        mm(a("u0", 0, 320), ident, a("r6", 0, 320), True, True)
-        for j in range(2):
-            act(a3("d3", 0, F, 64 * j, 64 * j + 64), ja, AF.Relu, bias=-5.0)
-        yield
-        yield
-        tt(a3("jf", F, 2 * F, 0, 64), a("jb", 0, 320), a("u0", 0, 320), OP.max)
-        yield
-        yield
+    cp(a("ctlb", 0, 25, parts=8), a("ctl", 0, 25, parts=8))
+    mm(a("u3", 0, 25), rep, a("ctlb", 0, 25, parts=8), True, True)
+    scan(c5(cn_), a("u3", 0, 5), a("one", 0, 5), n1, OP.add, OP.add)
+    ts(gz, one("u3", 0), 1.0, 1.0, OP.min, OP.add)
+    tt(c5(tx), c5(cn_), a("u3", 10, 25, 3), OP.is_equal)
+    ts(c5(lt), c5(cn_), 0.0, None, OP.is_gt)
+    ts(cz, one("u3", 5), gz, one("u3", 5), OP.is_le, OP.mult)
+    ts(c5(tc, 0, 1), c5(tx, 0, 1), cz, None, OP.mult)
+    tt(c5(tc, 1, 5), c5(tx, 1, 5), a("u3", 6, 10), OP.mult)
+    tt(a("cq", 1, 5), c5(lt, 1, 5), c5(lt, 0, 4), OP.subtract)
+    ts(short(0), c5(tc, 0, 1), 0.0, c5(lt, 0, 1), OP.is_equal, OP.mult)
+    ts(long_(0), c5(tc, 0, 1), 1.0, None, OP.is_equal)
+    ts(c5(k2), c5(tc), 2.0, None, OP.not_equal)
+    act(c5(thl), c5(tc), AF.Abs, bias=-100.0, scale=100.0)
+    act(c5(ths), c5(tc), bias=-11.0, scale=-100.0)
+    act(c5(thl), c5(thl), bias=-11.0, scale=-1.0)
+    tt(c5(m0), c5(cn_), a("u3", 11, 25, 3), OP.is_equal)
+    tt(c5(m1), c5(cn_), a("u3", 12, 25, 3), OP.is_equal)
+    act(c5(m0), c5(m0), bias=nb1, scale=32.0)
+    act(c5(m1), c5(m1), scale=64.0)
+    tt(c5(kb), c5(m0), c5(m1), OP.add)
+    ts(c5(isf, 0, 4), c5(cn_, 0, 4), 0.0, K, OP.is_equal, OP.mult)
+    tt(c5(isf, 4, 8), c5(isf, 0, 4), a("ci", 3, 7), OP.mult)
+    act(c5(sl_), c5(lt), bias=1.0, scale=-1.0, acc=ee)
+    act(one("st", 10), ee, bias=-1.0)
+    scan(c5(sl_, 0, 4), c5(isf, 4, 8), c5(isf, 4, 8), c01, OP.max, OP.max)
+    act(sm, slc, AF.Relu, bias=-384.0, scale=192.0 / K)
+    act(s1, slc, scale=1.0 / K)
+    for f in range(1, F):
+        cum, lk = one(("u5", "u1")[f & 1], 256 + f), one("sm", f)
+        mms([(cum, ge, one("cq", f)), (cum, n16, one("cq", f)), (cum, alls, long_(f - 1)), (cum, ge, short(f - 1)), (cum, n16, short(f - 1))])
+        act(lk, long_(f - 1), scale=c5(k2, f, f + 1))
+        ts(short(f), cum, c5(ths, f, f + 1), None, OP.is_le)
+        ts(long_(f), cum, c5(thl, f, f + 1), lk, OP.is_le, OP.add)
+    total(ee, a("st", 0, 11))
+    place("u2", 0, 1)
+    f0, f1, fs = [one("f0", k) for k in range(3)]
+    ts(h0, one("key", 0), 0.0, c01, OP.is_gt, OP.mult)
+    ts(f0, one("sg", 0), 14.0, c01, OP.is_equal, OP.mult)
+    ts(f1, one("sg", 0), 12.0, c01, OP.is_equal, OP.mult)
+    act(fs, tv(ex, 0, 1), scale=h0)
+    ms(a("f0", 4, 6), K)
+    ta0, tb0 = one("u2", 0), one("u2", 1)
+    mms([(a("u2", 0, 2), mup, a("f0", 4, 6)), (ta0, a18, f0), (tb0, a7, f0), (tb0, a18, f1), (tb0, an7, f1), (ta0, alls, fs), (tb0, alls, fs)])
+    place("u4", 1, GROUPS[0][1])
+    tables("ix1", *GROUPS[0])
+
+    def ev(f, lo, hi):
+        return a("ev", 256 * f + lo, 256 * f + hi)
+
+    def dg(f, k):
+        return a("dg", 192 * f + 64 * k, 192 * f + 64 * k + 64)
+
+    def explicit(f):
+        nd = a("ix0", 384, 512)
+        mms([(nd, unit, blank(128))] + [(a("ix0", 384 + 64 * k, 448 + 64 * k), ni, a3("d3", f, f + 1, 0, 64)) for k in range(2)])
+        for k in range(2):
+            tt(ev(f, 128 * k, 128 * k + 128), a(("wy", "wx")[k], 128 * f, 128 * f + 128), nd, OP.mult)
+
+    def clamp(lo=0.0):
+        ts(a("cb", 0, 256), a("ix0", 0, 256), lo, lo + 31.0, OP.max, OP.min)
+
+    def look(o, f, k, x):
+        ts(o, a("pw", 320 * k + 64 * f, 320 * k + 64 * f + 64), x, None, OP.mult)
+
+    def digits(f):
+        n = 192 if f < F - 1 else 128
+        for k in range(n // 64):
+            look(a("ti", 64 * k, 64 * k + 64), f, k & 1, table(k, f))
+        ts(a("ta", 0, n), a("ti", 0, n), 7 * 1024, None, OP.bitwise_and)
+        cp(a("dg", 192 * f, 192 * f + n), a("ta", 0, n))
+        ts(a("moff", 12 * (f - 1), 12 * f), a("mio", 0, 12), table(4, f), None, OP.add)
+
+    def first():
         explicit(0)
         mms([(a("ix0", 0, 256), ident, a("base", 0, 256)), (a("ix0", 0, 256), ident, ev(0, 0, 256))])
-        yield
-        act(a8, alls, scale=8.0)
-        yield
         clamp(-192.0)
-        ones = B * K * (8 ** 6 + sum(8 ** k for k in range(5)))
-        for k in (0, 5):
-            act(a("arow", k, k + L0), a("ci", 3 + B, 3 + B + L0), bias=ones, scale=2.0 ** 25)
-            if NL:
-                act(a("arow", k + L0, k + 5), a("ci", 0, NL), bias=ones, scale=0.0)
-        act(a("arow", 15, 20), a("ci", 0, 5), bias=B * K, scale=-8.0 * K)
-        yield
-        yield
-        yield
+        mms([(a("ix0", 256, 384), i32, a("cb", 0, 128)), (a("ix0", 256, 384), ident, a("cb", 128, 256))])
+        for k, x in enumerate((ta0, tb0, table(2, 0))):
+            look(a("ta0", 64 * k, 64 * k + 64), 0, k & 1, x)
+        for lo, hi in ((0, 128), (128, 192)):
+            ts(a("ta0", lo, hi), a("ta0", lo, hi), 7 * 1024, None, OP.bitwise_and)
+        tt(a("o0", 0, 128), a("ta0", 0, 128), a("ix0", 256, 384), OP.add)
+        ts(a("off", 0, 128), a("o0", 0, 128), 33.0 * 192, None, OP.add)
+        ts(dg(0, 2), a("ta0", 128, 192), 8.0, None, OP.mult)
+        tt(a("mst", 192, 256), a("ta0", 0, 64), dg(0, 2), OP.add)
         for k in range(2):
-            act(a("pw", 320 * k, 320 * k + 64), a3("jf", F * k, F * k + 1, 0, 64), AF.Exp, scale=-LN8)
-            act(a("pw", 320 * k + 64, 320 * k + 320), a3("jf", F * k + 1, F * k + F, 0, 64), AF.Exp, scale=-LN8)
-
-    def extras():
-        yield
-        tt(c5(m0), c5(cn_), a("u3", 11, 25, 3), OP.is_equal)
-        tt(c5(m1), c5(cn_), a("u3", 12, 25, 3), OP.is_equal)
-        act(c5(m0), c5(m0), bias=nb1, scale=32.0)
-        act(c5(m1), c5(m1), scale=64.0)
-        yield
-        tt(c5(kb), c5(m0), c5(m1), OP.add)
-        yield
-        ts(c5(isf, 0, 4), c5(cn_, 0, 4), 0.0, K, OP.is_equal, OP.mult)
-        act(c5(sl_), c5(lt), bias=1.0, scale=-1.0, acc=ee)
-        yield
-        tt(c5(isf, 4, 8), c5(isf, 0, 4), a("ci", 3, 7), OP.mult)
-        act(one("st", 10), ee, bias=-1.0)
-        yield
-        scan(c5(sl_, 0, 4), c5(isf, 4, 8), c5(isf, 4, 8), c01, OP.max, OP.max)
-        yield
-        act(sm, c5(sl_, 3, 4), AF.Relu, bias=-384.0, scale=192.0 / K)
-
-    def weave(*threads):
-        live = list(threads)
-        while live:
-            live = [t for t in live if next(t, live) is not live]
-
-    def start(f):
-        m = 192 * (f + 1)
-        tt(a("xb", 0, 192), gi(a("mst", 0, m), a("moff", 12 * (f - 1), 12 * f)), a3("d3", f, f + 1, 0, 192), OP.mult)
-        act(a("hv", 0, 128), a("xb", 64, 192), bias=191.75, scale=0.5)
-        act(a("zz", 0, 64), a("xb", 0, 64), AF.Relu, bias=-8.0 * K * f)
-        ts(a("zz", 64, 128), a("xb", 0, 64), 8.0 * K * f, one("tt", 15 + f), OP.is_ge, OP.mult)
-
-    def ask():
-        x0, x1, y0, y1 = a("rb0", 0, N), a("rb0", N, 2 * N), a("rb1", 0, N), a("rb1", N, 2 * N)
-        e = [a("eq", 128 * k, 128 * (k + 1), parts=32) for k in range(6)]
-        ts(e[4], a("e4", 0, 128, parts=32), 0.0, None, OP.is_equal)
-        ts(e[5], a("e4", 0, 128, parts=32), 0.0, -1.0, OP.is_equal, OP.mult)
-        for v in range(4):
-            ts(e[v], a("e4", 128, 256, parts=32), float(v), None, OP.is_equal)
-        for v in range(4):
-            o = a("rb1", 128 * v, 128 * v + 128)
-            mms([(o, e[4], e[v]), (o, e[5 if v else 4], e[v - 1 if v else 3])])
-        act(a("w1", 0, 512), a("rb1", 0, 512), scale=0.5)
-        fa, fb, vf, inc = a("fab", 0, N), a("fab", N, 2 * N), a("vf", 0, N), a("inc", 0, N)
-        q0, q1, q2 = [a("qq", k * N, k * N + N) for k in range(3)]
-        ts(fa, a3("jf", L0, F, 0, 64), 5.0, None, OP.is_equal)
-        ts(fb, a3("jf", F + L0, 2 * F, 0, 64), 5.0, None, OP.is_equal)
-        tt(vf, fa, fb, OP.max)
-        ms(a("fm", 0, N), 1.0)
-        ms(a("fm", 0, N, 64), 0.0)
-        ts(one("lcol", 0), one("pcol", 0), 2, 3, OP.arith_shift_right, OP.bitwise_and)
-        cp(lf, one("lcol", 0))
-        act(b4, lf, bias=160.375, scale=-0.25)
-        act(b16, lf, bias=160.0 + 3.0 / 16 - 15.0 / 32, scale=-1.0 / 16)
-        act(et, nf, bias=15.5, scale=16.0)
-        act(n4, ident, scale=-4.0)
-        act(nbig, ident, scale=-16384.0)
-        mm(x0, alls, vf, True, True)
-        scan(inc, a("fm", 0, N), x0, 0.0, OP.mult, OP.add)
-        mms([(x0, ident, inc), (x0, nge, vf)])
-        mms([(x1, ident, inc), (x1, nge4, vf)])
-        mms([(y0, ident, inc), (y0, nalls, vf)])
-        mms([(y1, ident, inc), (y1, nge, vf), (y1, nbig, vf)])
-        act(q0, x0, bias=159.625, scale=0.25)
-        act(q1, x1, bias=b4, scale=0.25)
-        act(q2, x1, bias=b16, scale=1.0 / 16)
-        mms([(x0, ident, inc), (x0, nge, vf), (x0, n4, q0)])
-        mms([(x1, ident, q1), (x1, n4, q2)])
-        for v in range(1, 4):
-            act(a("sgn", (v - 1) * N, v * N), x0, AF.Sign, bias=640.5 - v)
-        for v in range(1, 4):
-            act(a("sgn", (v + 2) * N, (v + 3) * N), x1, AF.Sign, bias=480.5 - v)
-        act(a("sx", 0, N), y0)
-        for j in range(NL):
-            part = a("rb1", 64 * j, 64 * j + 64)
-            act(a("k0", 64 * j, 64 * j + 64), part, bias=130.0 + 32 * j - 15.0 / 32, scale=1.0 / 16)
-            act(a("kp", 64 * j, 64 * j + 64), part, AF.Sign, bias=et, scale=-1.0, acc=one("ec", j))
-            act(a("zq", 64 * j, 64 * j + 64), a("rb1", N + 64 * j, N + 64 * j + 64), bias=16384.0 - 256 * (j + 1))
-        tt(a("kp", 1, N), a("k0", 1, N), a("k0", 0, N - 1), OP.is_equal)
-        act(a("ec", 8, 8 + NL), a("ci", 0, NL), bias=62.0, scale=128.0)
-        tt(a("ec", 4, 4 + NL), a("ec", 0, NL), a("ec", 8, 8 + NL), OP.add)
-        ts(a("eo", 0, NL), a("ec", 4, 4 + NL), 0.5, None, OP.mult)
-        act(a("be", 0, 128), a("base", 0, 128), bias=192.0)
-        act(a("be", 128, 256), a("base", 128, 256), bias=208.0)
-        act(i64k, ident, scale=65536.0)
-        act(i2k, ident, scale=2048.0)
-        for j in range(NL):
-            explicit(L0 + j, a("rb1", 128 * j, 128 * j + 128))
-        for k, bank in enumerate(("rb1", "rb0")):
-            for j in range(NL):
-                o = a(bank, 128 * j, 128 * j + 128)
-                mms([(o, ident, a("be", 128 * k, 128 * k + 128)), (o, ident, ev(L0 + j, 128 * k, 128 * k + 128))])
-            ts(a("cbe", 2 * N * k, 2 * N * (k + 1)), a(bank, 0, 2 * N), 16.0 * k, 16.0 * k + 31, OP.max, OP.min)
-        for i, (my, mx) in enumerate(((i32, ident), (i64k, i2k))):
-            for j in range(NL):
-                o, c = a("rb1", i * N + 64 * j, i * N + 64 * j + 64), 128 * j + 64 * i
-                mms([(o, my, a("cbe", c, c + 64)), (o, mx, a("cbe", 2 * N + c, 2 * N + c + 64))])
-        tt(a("pa", 0, N), fa, y0, OP.mult)
-        tt(x0, fb, y1, OP.mult)
-        tt(x0, a("pa", 0, N), x0, OP.add)
-        for s, (src, dst, w) in enumerate(((x0, y0, "w1"), (y0, x0, "w1"))):
-            for v in range(3):
-                tt(a("pv", v * N, v * N + N), a("sgn", (3 * s + v) * N, (3 * s + v + 1) * N), src, OP.mult)
-            act(a("pf", 0, N), src)
-            mms([(dst, a(w, 128 * v, 128 * v + 128), a("pv", (v - 1) * N, v * N)) for v in range(1, 4)] + [(dst, a(w, 0, 128), a("pf", 0, N))])
-        n, xs, ys, eo = 16 * NL, a("xs", 0, N), a("ys", 0, N), a("eo", 0, NL)
-        act(xs, x0)
-        scan(ys, a("kp", 0, N), xs, 0.0, OP.mult, OP.add)
-        act(a("thr", n, 2 * n), a("thr", 0, n), bias=-16.5)
-        act(a("thr", 0, n), a("thr", 0, n), bias=nf)
-        ms(a("hs", 0, 8), 0.0)
-        tt(a("wm", 0, n), gi(inc, eo), a("thr", 0, n), OP.is_gt)
-        tt(a("wm", n, 2 * n), gi(a("sx", 0, N), eo), a("thr", n, 2 * n), OP.is_gt)
-        tt(a("hs", 8, 8 + n), gi(xs, eo), a("wm", 0, n), OP.mult)
-        tt(a("y1", 0, n), gi(ys, eo), a("hs", 8, 8 + n), OP.subtract)
-        tt(a("y1", n, 2 * n), a("y1", 0, n), a("wm", n, 2 * n), OP.mult)
-        tt(a("ri", 2 * n, 3 * n), a("y1", n, 2 * n), a("hs", 7, 7 + n), OP.add)
-        ts(a("ri", 0, n), a("ri", 2 * n, 3 * n), 2047, None, OP.bitwise_and)
-        ts(a("ri", n, 2 * n), a("ri", 2 * n, 3 * n), 11, None, OP.arith_shift_right)
-        cp(a("rqo", 0, 2 * n), a("ri", 0, 2 * n))
-        for f in range(L0 - 1, F - 1):
-            ms(a("sb", f * SB, f * SB + 16), 255.0)
-        act(n32, ident, scale=-32.0)
-
-    def answer(f):
-        j, win = f - L0, a("sb", (f - 1) * SB, f * SB)
-        for h in range(2):
-            c = 16 * j + 8 * h
-            act(a("ob", 128 * h, 128 * h + 128), gi(win, a("rq", c, c + 8)), bias=-255.0)
-        for h in range(2):
-            c = 16 * (NL + j) + 8 * h
-            tt(a("uo", 256 * j + 128 * h, 256 * j + 128 * h + 128), gi(win, a("rq", c, c + 8)), a("ob", 128 * h, 128 * h + 128), OP.add)
-        send(a("win", 256 * (F - 1 - f), 256 * (F - f)), a("uo", 256 * j, 256 * j + 256), "va%d_3" % f, "sent%d_3" % f)
+            act(a("mst", 256 + 64 * k, 320 + 64 * k), ev(0, 128 * k, 128 * k + 64))
 
     def index(f):
         more, m = f < F - 1, 192 * (f + 1)
-        turn_back(f - 1)
+        explicit(f)
+        digits(f)
+        tt(a("xb", 0, 192), gi(a("mst", 0, m), a("moff", 12 * (f - 1), 12 * f)), a3("d3", f, f + 1, 0, 192), OP.mult)
+        act(a("hv", 0, 128), a("xb", 64, 192), bias=191.75, scale=0.5)
+        act(a("zz", 0, 64), a("xb", 0, 64), AF.Relu, bias=-8.0 * K * f)
+        ts(a("zz", 64, 128), a("xb", 0, 64), 8.0 * K * f, table(3, f), OP.is_ge, OP.mult)
         code = a("ix1", 0, 64)
-        terms = [(code, ident, dg(f, 0)), (code, ident, a("zz", 0, 64)), (code, ni, a("zz", 64, 128))]
-        if more:
-            terms.insert(1, (code, i8, dg(f, 2)))
-        mms(terms)
+        mms([(code, ident, dg(f, 0))] + [(code, i8, dg(f, 2))] * more + [(code, ident, a("zz", 0, 64)), (code, ni, a("zz", 64, 128))])
         y0, y1, x0, x1 = [a("ix0", 64 * k, 64 * k + 64) for k in range(4)]
         hy, hx = a("hv", 0, 64), a("hv", 64, 128)
-        mms([(a("ix0", 0, 256), ident, a("base", 0, 256)), (y1, ni, a("xb", 64, 128)), (x1, ni, a("xb", 128, 192)),
-             (y0, ident, hy), (y1, ident, hy), (x0, ident, hx), (x1, ident, hx), (a("ix0", 0, 256), ident, ev(f, 0, 256))])
+        mms([(a("ix0", 0, 256), ident, a("base", 0, 256)), (a("ix0", 0, 256), ident, ev(f, 0, 256)), (y1, ni, a("xb", 64, 128)), (x1, ni, a("xb", 128, 192)),
+             (y0, ident, hy), (y1, ident, hy), (x0, ident, hx), (x1, ident, hx)])
         act(a("mst", m, m + 64), code)
         act(a("ef", 0, 64), code, bias=192.0 - 7.0 / 16, scale=1.0 / (8 * K))
-        if more:
-            look(f + 1)
         clamp()
-        if more:
-            digits(f + 1)
         op, oq = a("ix0", 256, 320), a("ix0", 320, 384)
         mms([(a("ix0", 256, 384), i32, a("cb", 0, 128)), (a("ix0", 256, 384), ident, a("cb", 128, 256)), (oq, ident, dg(f, 1)),
              (op, ident, a("mst", m, m + 64)), (op, n8k, a("ef", 0, 64))])
-        if f >= L0:
-            j, od = f - L0, a("ix0", 384, 448)
-            y0, y1, x0, x1 = [a("cb", 64 * k, 64 * k + 64) for k in range(4)]
-            mms([(od, i32, y1), (od, n32, y0), (od, ident, x1), (od, ni, x0), (od, ident, dg(f, 1))])
-            tt(a("of", 0, 64), a("fab", 64 * j, 64 * j + 64), od, OP.mult)
-            tt(a("of", 128, 192), a("zq", 64 * j, 64 * j + 64), oq, OP.min)
-            tt(a("of", 64, 128), a("of", 0, 64), op, OP.add)
-            op, oq = a("of", 64, 128), a("of", 128, 192)
         if more:
-            mplace(f + 1)
             mms([(a("ix1", 64, 192), ident, a("hv", 0, 128)), (a("ix1", 64, 128), ident, ev(f, 0, 64)), (a("ix1", 128, 192), ident, ev(f, 128, 192))])
             act(a("mst", m + 64, m + 192), a("ix1", 64, 192), bias=-192.0)
         ts(a("off", 128 * f, 128 * f + 64), op, 192.0 * 8 * K, None, OP.add)
-        ts(a("off", 128 * f + 64, 128 * f + 128), oq, 256.0 * max(0, f - L0 + 1), None, OP.add)
-        if more:
-            keep(f + 1)
-        preacc(f)
-        later(f)
+        cp(a("off", 128 * f + 64, 128 * f + 128), oq)
+
+    def preacc(f):
+        s, ch = (f + 1) % F, (HAND if f < F - 1 else LAST)["CH"]
+        for k in range(len(ch) - 1):
+            n = ch[k + 1] - ch[k]
+            mm(a("u%d" % k, 0, n), a("wide", 16 * s, 16 * s + 128), a("rs", f * P + ch[k], f * P + ch[k + 1]), True)
+            mm(a("u%d" % k, 0, n), quar, blank(n))
 
     def turn_back(f):
-        s, CH = f + 1, (CA if f >= L0 else CW)
-        for k in range(len(CH) - 1):
-            bank = a("u%d" % k, 0, CH[k + 1] - CH[k])
-            mm(bank, a("wide", 128 - 16 * s, 256 - 16 * s), made(f, CH[k], CH[k + 1]), True, True)
-            act(slot(4 + f, CH[k], CH[k + 1]), bank)
+        s = f + 1
+        for k, lo, hi in BACK:
+            bank = a("u%d" % k, 0, hi - lo)
+            mm(bank, a("wide", 128 - 16 * s, 256 - 16 * s), made(f, lo, hi), True, True)
+            act(slot(3 + f, lo, hi), bank)
 
     def pixels(f):
-        s, asked = (f + 1) % F, f >= L0
-        CH = CA if asked else CW
-        end = U + (4 + B + f - asked) * P
-        wins = [a("win", U, end), a("win", 256 * (F - 1 - f) if asked else U, end)]
+        s, how = (f + 1) % F, (HAND if f < F - 1 else LAST)
+        ch, win, summed = how["CH"], a("win", 0, (4 + f) * P), []
 
-        def gather(i, lo, hi):
+        def gather(x):
+            i, k = "pq".index(x[0]), int(x[1])
             o = 128 * f + 64 * i
-            return a("pq", P * i + lo, P * i + hi), gi(wins[i], a("off", o + lo // 16, o + hi // 16))
+            return a("pq", P * i + ch[k], P * i + ch[k + 1]), gi(win, a("off", o + ch[k] // 16, o + ch[k + 1] // 16))
 
-        def half(i, k):
-            mm(a("u%d" % k, 0, CH[k + 1] - CH[k]), a("half", 16 * s, 16 * s + 128), a("pq", P * i + CH[k], P * i + CH[k + 1]))
-
-        def finish(k):
-            n = CH[k + 1] - CH[k]
-            acc = a("u%d" % k, 0, n)
-            for i in range(asked, 2):
-                half(i, k)
-            mm(acc, mup, blank(n))
-            mm(acc, mdn, blank(n), False, True)
-            ts(made(f, CH[k], CH[k + 1]), acc, 0.0, 255.0, OP.max, OP.min)
-            if f < L0 - 1 and k in SENDS:
-                send(slot(5 + f, *SENDS[k]), made(f, *SENDS[k]), "va%d_%d" % (f + 1, k), "sent%d_%d" % (f + 1, k))
-            if f == F - 1 and k in STORES:
-                lo, hi = STORES[k]
-                store(f * P + lo, f * P + hi, made(f, lo, hi))
-        if asked:
-            for x in SPRE:
-                act(*gather(*x))
-            for x in VPRE:
-                cp(*gather(*x))
-            for k in range(len(CH) - 1):
-                half(0, k)
+        def add_up(k):
+            n = ch[k + 1] - ch[k]
+            terms = [(a("half", 16 * s, 16 * s + 128), gather(x)[0]) for x in (how["V"] + " " + how["S"]).split() if x in ("p%d" % k, "q%d" % k)]
+            if "c%d" % k in how["V"]:
+                terms += [(mup, blank(n)), (mdn, blank(n))]
+            for j, (l, r) in enumerate(terms):
+                mm(a("u%d" % k, 0, n), l, r, False, j == len(terms) - 1)
+            summed.append(k)
         line.update(v=[], s=[], t=[])
-        for x in SPOST if asked else SWORK:
-            act(*gather(*x))
-        for x in VPOST if asked else VWORK:
-            if isinstance(x, tuple):
-                cp(*gather(*x))
-            else:
-                finish(x)
-        if L0 - 1 <= f < F - 1:
-            answer(f + 1)
+        for x in how["S"].split():
+            act(*gather(x))
+        for x in how["V"].split():
+            k = int(x[1])
+            acc, near = a("u%d" % k, 0, ch[k + 1] - ch[k]), a("cr", ch[k], ch[k + 1])
+            if x[0] in "pq":
+                cp(*gather(x))
+                continue
+            for j in range(len(summed), k + 1):
+                add_up(j)
+            if x[0] == "r":
+                ts(near, acc, MAGIC, MAGIC, OP.add, OP.subtract)
+                continue
+            ts(made(f, ch[k], ch[k + 1]), near if x[0] == "m" else acc, 0.0, 255.0, OP.max, OP.min)
+            if x in how["OUT"]:
+                lo, hi = how["OUT"][x]
+                if f < F - 1:
+                    send(f + 1, int(hi == P), slot(4 + f, lo, hi), made(f, lo, hi))
+                else:
+                    store(f * P + lo, f * P + hi, made(f, lo, hi))
         line.clear()
 
-    scan(c5(cn_), a("u3", 0, 5), a("one", 0, 5), n1, OP.add, OP.add)
-    ts(gz, one("u3", 0), 1.0, 1.0, OP.min, OP.add)
-    weave(control(), lists(), extras())
+    first()
     later(0)
-    act(a("half", 0, 256), wide, scale=0.5)
-    act(i8, ident, scale=8.0)
-    preacc(0)
-    mms([(a("ix0", 256, 384), i32, a("cb", 0, 128)), (a("ix0", 256, 384), ident, a("cb", 128, 256))])
-    for k, table in enumerate((one("t0", 0), one("t0", 1), one("tt", 10))):
-        ts(a("ta0", 64 * k, 64 * k + 64), a("pw", 320 * (k & 1), 320 * (k & 1) + 64), table, None, OP.mult)
-    for lo, hi in ((0, 128), (128, 192)):
-        ts(a("ta0", lo, hi), a("ta0", lo, hi), 7 * 1024, None, OP.bitwise_and)
-    tt(a("o0", 0, 128), a("ta0", 0, 128), a("ix0", 256, 384), OP.add)
-    ts(a("off", 0, 128), a("o0", 0, 128), 33.0 * 192, None, OP.add)
-    ts(dg(0, 2), a("ta0", 128, 192), 8.0, None, OP.mult)
-    tt(a("mst", 192, 256), a("ta0", 0, 64), dg(0, 2), OP.add)
-    look(1)
-    for f in range(1, L0):
-        explicit(f)
-    early[0] = EARLY
-    if NL:
-        ask()
-    early[0] = 0.0
     for f in range(F):
+        preacc(f)
         pixels(f)
-        if NL and f == ASK:
-            send(a("rq", 0, 32 * NL), a("rqo", 0, 32 * NL), "asked", "ask", prv, nxt)
-        if f == 0:
-            act(a("mst", 192 + 64, 192 + 128), ev(0, 0, 64))
-            act(a("mst", 192 + 128, 192 + 192), ev(0, 128, 192))
-            act(a3("d3", 1, F, 128, 192), a3("jf", 1, F, 0, 64), AF.Relu, bias=-5.0)
-            act(n8k, ident, scale=-8.0 * K)
-            mplace(1)
-            digits(1)
-            start(1)
-            keep(1)
         if f < F - 1:
-            if f > 0:
-                start(f + 1)
+            turn_back(f)
+            later(f + 1)
+            if f + 1 == SPLIT < F:
+                places(SPLIT, F, ("ix1", 256))
+            if f + 1 == GROUPS[1][0] - 1:
+                place("ix1", *GROUPS[1])
+                tables("ix1", *GROUPS[1])
             index(f + 1)
 
     issue()
@@ -813,5 +640,5 @@ def rank_program(g, core, T, topo):
     for sem in LOADS:
         need("y", (sem, 16, {}))
     for sem in sends:
-        need("y", (sem, sends[sem][0], {}))
+        need("y", (sem, nout, {}))
     need("y", ("stored", stores[0], {}))

import math
from concourse.mybir import AluOpType as OP, ActivationFunctionType as AF, AxisListType as AX

F, P = 5, 1024
BF, F32, I32, U16 = "bfloat16", "float32", "int32", "uint16"
HAND = dict(CH=[0, 160, 352, 448, 768, 928, 1024], V="p0 p1 p2 p3 c0 c1 c2 p5 c3 c4 c5", S="q0 q1 q2 q3 p4 q4 q5", OUT={"c2": (0, 448), "c5": (448, 1024)})
LAST = dict(CH=[0, 128, 320, 544, 768, 960, 1024], V="p0 p1 p2 p3 c0 p4 c1 c2 c3 c4 c5", S="q0 q1 q2 q3 q4 p5 q5",
            OUT={"c2": (0, 544), "c4": (544, 960), "c5": (960, 1024)})
BACK = [(0, 0, 448), (3, 448, 768), (4, 768, 1024)]
MAGIC = 1.5 * 2.0 ** 23
ONV, PEFIX = 7, 10.0
SPLIT = 2
FIRSTV = [(0, 1024)]
GROUPS = [(0, 3), (3, 5)]
WAKE, GATHER, START, ROW, LOCAL, FAR, REMOTE, CALL = 230.0, 1.7, 1300.0, 30.0, 0.03, 6.0, 0.06, 1200.0
CASES = [(0.0, 0.9), (300.0, 1.0)]
ORDER = {}
ROUNDS, SHORT = 4, {"v": 130.0, "s": 130.0, "t": 50.0}
LN8 = math.log(8.0)
K = 1024.0


def _sb(n, d):
    return ("sbuf", [128, n] if isinstance(n, int) else [128] + n, d)


SCRATCH = {
    "win": _sb(8 * P, BF), "rs": _sb(F * P, BF), "sb": _sb(F * P, BF), "pq": _sb(2 * P, BF), "cr": _sb(P, BF),
    "ctl": _sb(26, I32), "ctlb": _sb(26, BF),
    "ja": _sb(320, I32), "jb": _sb(320, I32), "wy": _sb(640, I32), "wx": _sb(640, I32),
    "jf": _sb([2 * F, 64], BF), "r6": _sb(320, BF), "d3": _sb([F, 192], BF), "pw": _sb(640, BF), "ev": _sb(F * 256, BF),
    "pcol": _sb(4, I32), "ncol": _sb(4, I32), "col": _sb(16, F32), "ci": _sb(16, F32), "one": _sb(8, BF),
    "repi": _sb(128, BF), "rep": _sb(128, BF), "i16": _sb(16, BF), "dif": _sb(128, BF), "wide": _sb(256, BF), "half": _sb(256, BF),
    "base": _sb(256, BF), "mio": _sb(12, F32), "moff": _sb(48, U16), "mst": _sb(6 * 192, BF),
    "c": _sb(128, F32), "cq": _sb(8, BF), "st": _sb(16, BF), "sm": _sb(8, F32), "key": _sb(8, F32), "sg": _sb(8, F32),
    "dd": _sb(80, BF), "junk": _sb(80, BF), "tv": _sb(80, BF), "arow": _sb([5, F], F32), "tt": _sb([5, F], F32),
    "f0": _sb(6, BF), "o0": _sb(128, F32), "ta0": _sb(192, I32),
    "ti": _sb(192, I32), "ta": _sb(192, I32), "dg": _sb(F * 192, BF),
    "xb": _sb(192, BF), "hv": _sb(128, BF), "zz": _sb(128, BF), "ef": _sb(64, BF), "cb": _sb(256, BF), "off": _sb(F * 128, U16),
}
MATS = ("alls", "ge", "a18", "a7", "an7", "a8", "i32", "i8", "ni", "n8k", "n16", "quar", "unit", "mup", "mdn", "i6")
for _k in MATS:
    SCRATCH[_k] = _sb(128, BF)
for _k in ("u0", "u1", "u2", "u3", "u4", "u5", "ix0", "ix1"):
    SCRATCH[_k] = ("psum", [128, 512], F32)
LOADS = (["ls1_%d" % k for k in range(len(FIRSTV))] + ["ls0", "lg", "lc", "lr", "lja0", "ljb0", "lja1", "ljb1"]
         + ["l%s%d" % (n, k) for n in ("wy", "wx") for k in range(3)] + ["lrs%d" % f for f in range(F)])
SEMAPHORES = ["cv", "cs", "ct", "cg", "stored"] + LOADS + ["%s%d_%d" % (n, f, k) for n in ("va", "sent") for f in range(F) for k in range(3)]


def rank_program(g, core, T, topo):
    rank = T.rank_of(core)
    if rank is None:
        return
    nxt = T.cores[(rank + 1) % len(T.cores)]
    prv = T.cores[(rank - 1) % len(T.cores)]
    nout, nin = len(topo.engines(core, nxt)), len(topo.engines(prv, core))
    Q = {"v": g.vector, "s": g.scalar, "t": g.tensor, "g": g, "y": g.sync}
    cnt = {"cv": 0, "cs": 0, "ct": 0, "cg": 0}
    known = {e: {} for e in Q}
    hist = {}

    def need(e, tok):
        sem, val, snap = tok
        if known[e].get(sem, 0) >= val:
            return
        Q[e].wait_ge(T.sem[sem], val)
        known[e][sem] = val
        for k, v in snap.items():
            if known[e].get(k, 0) < v:
                known[e][k] = v

    def order(e, outs, ins):
        toks = {}
        for wr, group in ((True, outs), (False, ins)):
            for x in group:
                for name, lo, hi in x[1]:
                    ps = SCRATCH[name][0] == "psum"
                    for l2, h2, w2, e2, tok in hist.get(name, []):
                        if ps and e2 == e == "t":
                            continue
                        if (ps and e2 != e) or ((wr or w2) and lo < h2 and l2 < hi):
                            if tok[0] not in toks or toks[tok[0]][1] < tok[1]:
                                toks[tok[0]] = tok
        for tok in sorted(toks.values(), key=lambda t: -len(t[2])):
            need(e, tok)

    def note(e, outs, ins, tok):
        for wr, group in ((True, outs), (False, ins)):
            for x in group:
                for name, lo, hi in x[1]:
                    hist.setdefault(name, []).append((lo, hi, wr, e, tok))

    calls, seen, line, soft = [], {}, {}, set()

    def width(x):
        return sum(hi - lo for _, lo, hi in x[1])

    def add(e, outs, ins, cost, emit, flight=0.0, after=()):
        before = set(after)
        for wr, group in ((True, outs), (False, ins)):
            for x in group:
                for name, lo, hi in x[1]:
                    ps = SCRATCH[name][0] == "psum"
                    for l2, h2, w2, k in seen.get(name, []):
                        if (ps and (calls[k][0] != e or e == "t")) or ((wr or w2) and lo < h2 and l2 < hi):
                            before.add(k)
        if e in "gy":
            before.update([k for k, c in enumerate(calls) if c[0] == e][-1:])
        in_line = set(line.get(e, [])[-1:]) - before
        before |= in_line
        if e in line:
            line[e].append(len(calls))
        soft.update((j, len(calls)) for j in in_line)
        for wr, group in ((True, outs), (False, ins)):
            for x in group:
                for name, lo, hi in x[1]:
                    seen.setdefault(name, []).append((lo, hi, wr, len(calls)))
        calls.append((e, cost, flight, before, emit, line.get(e)))
        return len(calls) - 1

    def issue():
        def links(once, far):
            on, back = [[] for _ in calls], [[] for _ in calls]
            for k, c in enumerate(calls):
                for j in c[3]:
                    e, cost, flight = calls[j][:3]
                    if (j, k) in soft or (e == c[0] and e in "tgy"):
                        gap = max(cost, flight if c[2] else 0.0)
                    elif flight:
                        gap = WAKE + (START + flight) * (far if e == "g" else 1.0) + (once if j == sends["sent0_0"] else 0.0)
                    else:
                        gap = WAKE + cost
                    on[j].append((k, gap))
                    back[k].append((j, gap + c[1] - cost))
            return on, back

        def span(done, on):
            at, free = [0.0] * n, {e: 0.0 for e in Q}
            for k in done:
                at[k] = max(at[k], free[calls[k][0]])
                free[calls[k][0]] = at[k] + calls[k][1]
                for j, lag in on[k]:
                    at[j] = max(at[j], at[k] + lag)
            return max(at[k] + calls[k][1] + tail[k] for k in range(n))

        def plan(users, at, weight):
            left = [0] * n
            for links in users:
                for k, lag in links:
                    left[k] += 1
            ready, free, done = {e: [k for k in range(n) if not left[k] and calls[k][0] == e] for e in Q}, {e: 0.0 for e in Q}, []
            busy = {e: 0 for e in Q}
            while len(done) < n:
                may = {e: [k for k in ready[e] if not busy[e] or calls[k][5] or calls[k][1] <= SHORT[e]] for e in Q}
                may = may if any(may.values()) else ready
                end, e = min((max(at[k], free[e]) + calls[k][1], e) for e in Q for k in may[e])
                k = max((j for j in may[e] if max(at[j], free[e]) < end), key=lambda j: (weight[j], -j))
                if calls[k][5]:
                    busy[e] = (busy[e] or len(calls[k][5])) - 1
                ready[e].remove(k)
                at[k] = max(at[k], free[e])
                free[e] = at[k] + calls[k][1]
                done.append(k)
                for j, lag in users[k]:
                    at[j] = max(at[j], at[k] + lag)
                    left[j] -= 1
                    if not left[j]:
                        ready[calls[j][0]].append(j)
            return done, [at[k] + calls[k][1] for k in range(n)]
        n = len(calls)
        tail = [START + c[2] - c[1] if c[2] else 0.0 for c in calls]
        if ORDER.get("n") != n:
            cases, best = [links(*c) for c in CASES], None
            for on, back in cases:
                chain = [0.0] * n
                for j in reversed(range(n)):
                    chain[j] = max([tail[j] + calls[j][1]] + [lag + chain[k] for k, lag in on[j]])
                for _ in range(ROUNDS):
                    done, ends = plan(on, [0.0] * n, chain)
                    length = sum(span(done, c[0]) for c in cases)
                    if best is None or length < best[0]:
                        best = (length, done)
                    chain = plan(back, list(tail), ends)[1]
            ORDER.update(n=n, done=best[1])
        for k in ORDER["done"]:
            calls[k][4]()

    def run(e, outs, ins, call, rate=1.0, fixed=0.0):
        ins = [x for x in ins if isinstance(x, tuple)]

        def emit():
            order(e, outs, ins)
            sem = "c" + e
            cnt[sem] += 1
            call().then_inc(T.sem[sem], 1)
            note(e, outs, ins, (sem, cnt[sem], dict(known[e])))
        if any(len(x) > 2 for x in ins):
            rate, fixed = GATHER, 70.0
        elif e == "v" and rate == 1.0 and all(SCRATCH[x[1][0][0]][2] in (BF, U16) for x in outs + ins[:1]):
            rate = 0.5
        add(e, outs, ins, fixed + max(64.0 * min(rate, 1.0) if e == "t" else 64.0, rate * width(outs[0])), emit)

    def a(name, lo, hi, step=1, parts=128):
        ap = T[name][0:parts, lo:hi] if step == 1 else T[name][0:parts, lo:hi:step]
        return (ap, [(name, lo, hi)])

    def a3(name, r0, r1, lo, hi):
        w = SCRATCH[name][1][2]
        return (T[name][:, r0, lo:hi] if r1 == r0 + 1 else T[name][:, r0:r1, lo:hi], [(name, r * w + lo, r * w + hi) for r in range(r0, r1)])

    def one(name, k):
        return a(name, k, k + 1)

    def gi(w, o):
        return (w[0].indirect(o[0]), w[1] + o[1], "gather")

    def u(x):
        return x[0] if isinstance(x, tuple) else x

    def ts(o, i, s1, s2, op0, op1=None):
        if op1 is None:
            run("v", [o], [i, s1], lambda: g.vector.tensor_scalar(o[0], i[0], u(s1), None, op0))
        else:
            run("v", [o], [i, s1, s2], lambda: g.vector.tensor_scalar(o[0], i[0], u(s1), u(s2), op0, op1))

    def tt(o, x, y, op):
        both = all(SCRATCH[z[1][0][0]][0] == "sbuf" for z in (x, y))
        run("v", [o], [x, y], lambda: g.vector.tensor_tensor(o[0], x[0], y[0], op), 2.0 if both else 1.0)

    def cp(o, i):
        run("v", [o], [i], lambda: g.vector.tensor_copy(o[0], i[0]))

    def ms(o, c):
        run("v", [o], [], lambda: g.vector.memset(o[0], c))

    def scan(o, d0, d1, init, op0, op1):
        run("v", [o], [d0, d1, init], lambda: g.vector.tensor_tensor_scan(o[0], d0[0], d1[0], u(init), op0, op1))

    def total(o, i):
        run("v", [o], [i], lambda: g.vector.tensor_reduce(o[0], i[0], AX.X, OP.add))

    def act(o, i, func=AF.Identity, bias=0.0, scale=1.0, acc=None, fixed=0.0):
        if acc is None:
            run("s", [o], [i, bias, scale], lambda: g.scalar.activation(o[0], i[0], func, bias=u(bias), scale=u(scale)), 1.0, fixed)
        else:
            run("s", [o, acc], [i, bias, scale], lambda: g.scalar.activation(o[0], i[0], func, bias=u(bias), scale=u(scale), accum_out=acc[0]))

    def mm(o, l, r, start=False, stop=False):
        run("t", [o], [l, r], lambda: g.tensor.matmul(o[0], l[0], r[0], start, stop), 0.5, PEFIX)

    def mms(terms):
        for k, (o, l, r) in enumerate(terms):
            mm(o, l, r, k == 0, k == len(terms) - 1)

    def iota(o, pat, base, cm, small=True):
        if small:
            run("g", [o], [], lambda: g.iota(o[0], pat, base, cm, allow_small_or_imprecise_dtypes=True), 2.0, 160.0)
        else:
            run("g", [o], [], lambda: g.iota(o[0], pat, base, cm), 2.0, 160.0)

    def row(x):
        return width(x) * (4 if SCRATCH[x[1][0][0]][2] == I32 else 2)

    gate = []

    def local(e, outs, ins, start):
        waits, after = [tok for tok, k in gate], [k for tok, k in gate]
        del gate[:]

        def emit():
            for tok in waits:
                need(e, tok)
            order(e, outs, ins)
            start()
        x = (outs + ins)[0]
        add(e, outs, ins, 64.0, emit, (8 if row(x) > 64 else 1) * (ROW + LOCAL * row(x)), after)

    def load(e, o, src, sem):
        def start():
            Q[e].dma_start(o[0], src).then_inc(T.sem[sem], 16)
            note(e, [o], [], (sem, 16, dict(known[e])))
        local(e, [o], [], start)

    stores = [0]

    def store(lo, hi, src):
        local("y", [], [src], lambda: g.sync.dma_start(T.y[:, lo:hi], src[0]).then_inc(T.sem.stored, 16))
        stores[0] += 16

    sends = {}

    def send(f, k, dst, src):
        rsem, lsem = "va%d_%d" % (f, k), "sent%d_%d" % (f, k)

        def emit():
            order("g", [], [src])
            g.remote_dma(out_ap=dst[0], in_ap=src[0], remote_sem=T.sem[rsem], local_sem=T.sem[lsem], pid=topo.addr(nxt)[1], routing_id=topo.addr(nxt)[0],
                         dma_engine_mask=topo.mask(core, nxt))
        note("r", [dst], [], (rsem, nin, {}))
        sends[lsem] = add("g", [dst], [src], CALL, emit, 128 // nout * (FAR + REMOTE * row(src)))

    def slot(k, lo=0, hi=P):
        return a("win", k * P + lo, k * P + hi)

    def blank(n):
        return slot(0, 0, n)

    def made(f, lo, hi):
        return a("sb", f * P + lo, f * P + hi)

    def vectors(k, lo, hi):
        load("y", a("wy", lo, hi), T.vy[:, lo:hi], "lwy%d" % k)
        load("y", a("wx", lo, hi), T.vx[:, lo:hi], "lwx%d" % k)

    def residual(f):
        load("y", a("rs", f * P, (f + 1) * P), T.res[:, f * P:(f + 1) * P], "lrs%d" % f)

    load("s", a("ctl", 0, 5, parts=8), T.gaps[:], "lg")
    load("y", a("ctl", 10, 25, parts=8), T.rel[:], "lr")
    load("s", a("ctl", 5, 10, parts=8), T.cmd[:], "lc")
    for k, (lo, hi) in enumerate(FIRSTV):
        load("y", slot(2, lo, hi), T.pic0[:, P + lo:P + hi], "ls1_%d" % k)
    load("y", a("ja", 0, 128), T.ia[:, 0:128], "lja0")
    load("y", a("jb", 0, 128), T.ib[:, 0:128], "ljb0")
    vectors(0, 0, 128)
    residual(0)
    load("y", slot(1), T.pic0[:, 0:P], "ls0")
    vectors(1, 128, 256)

    def later(f):
        sem = [s for s in sends if s.startswith("sent%d" % f)][-1]
        gate.append(((sem, nout, {}), sends[sem]))
        if f < F - 1:
            residual(f + 1)
        if f == 0:
            load("y", a("ja", 128, 320), T.ia[:, 128:320], "lja1")
            load("y", a("jb", 128, 320), T.ib[:, 128:320], "ljb1")
            vectors(2, 256, 640)
        if f > 0:
            store((f - 1) * P, f * P, slot(2 + f))

    nf, n1, nb0, nb1, cl, c01, gz, cz, ee, sm, s1, hn, h0, hp = [one("col", k) for k in range(14)]
    alls, ge, a18, a7, an7, a8, i32, i8, ni, n8k, n16, quar, unit, mup, mdn, i6 = [a(n, 0, 128) for n in MATS]
    wide, ident, i16, rep = a("wide", 0, 256), a("wide", 0, 128), a("i16", 0, 16), a("rep", 0, 128, parts=8)
    iota(one("pcol", 0), [[0, 1]], 0, 1, False)
    iota(a("repi", 0, 128, parts=8), [[1, 8], [0, 16]], 0, -1)
    iota(a("dif", 0, 128), [[1, 128]], 0, -1)
    iota(a("ci", 0, 16), [[1, 16]], 0, 0)
    for k, (lo, hi) in enumerate(FIRSTV):
        send(0, k, slot(3, lo, hi), slot(2, lo, hi))
    iota(slot(0, 512, P), [[0, P - 512]], 128, 0)
    ms(blank(128), 128.0)
    ms(slot(0, 128, 512), 128.0)
    ms(a("c", 120, 128), 0.0)
    act(a("one", 0, 8), a("c", 120, 128), AF.Exp, fixed=1600.0)
    ms(quar, 2.0 ** -16)
    ms(unit, 2.0 ** -14)
    ms(mup, 768.0)
    ms(mdn, -768.0)
    ms(a("mst", 0, 192), 0.0)
    ms(a3("arow", 0, 5, 0, F), 0.0)
    ts(one("ncol", 0), one("pcol", 0), 15, None, OP.bitwise_and)
    cp(nf, one("ncol", 0))
    ts(n1, nf, -1.0, 1.0, OP.mult, OP.add)
    act(nb0, nf, bias=K, scale=K)
    act(nb1, nf, bias=-239.0)
    act(cl, nf, bias=255.0, scale=-2.0)
    ts(hn, nf, 0.5, None, OP.mult)
    ts(c01, nf, 2.0, nb0, OP.is_lt, OP.mult)
    ts(i16, a("ci", 0, 16), nf, None, OP.is_equal)
    ts(rep, a("repi", 0, 128, parts=8), 0.0, None, OP.is_equal)
    mm(a("u1", 0, 128), rep, rep, True, True)
    cp(alls, a("u1", 0, 128))
    for h in range(2):
        ts(a("wide", 128 * h, 128 * h + 128), a("dif", 0, 128), 0.0, None, OP.is_equal)
    act(ge, a("dif", 0, 128), AF.Abs, bias=hn)
    ts(ge, ge, hn, None, OP.is_le)
    ts(hp, one("pcol", 0), 0.5, -192.25, OP.mult, OP.add)
    for k in range(2):
        act(a("base", 64 * k, 64 * k + 64), a("dif", 0, 64), bias=hp, scale=0.5)
        act((T.base[:, 128 + k:256:2], [("base", 128 + 64 * k, 192 + 64 * k)]), blank(64), bias=nf, scale=(16.0 * k - 192.0) / 128)
    act(a("mio", 0, 12), a("ci", 0, 12), bias=nf, scale=16.0)
    for k, (m, src, x) in enumerate(((n16, ident, -16.0), (ni, ident, -1.0), (a18, alls, 2.0 ** 18), (a7, alls, 7.0), (an7, alls, -7.0), (i32, ident, 32.0),
                                     (a("half", 0, 256), wide, 0.5), (a8, alls, 8.0), (i8, ident, 8.0), (n8k, ident, -8.0 * K))):
        if k < ONV:
            ts(m, src, x, None, OP.mult)
        else:
            act(m, src, scale=x)
    for k in range(2):
        act(a3("arow", k, k + 1, 0, F), a("ci", 3, 8), scale=2.0 ** 25)
    act(a3("arow", 3, 4, 0, F), a("ci", 0, 5), scale=-8.0 * K)

    def places(lo, hi, bank):
        ja = a3("jf", lo, hi, 0, 64)
        cp(ja, a("ja", 64 * lo, 64 * hi))
        for j in range(3 if lo else 1):
            act(a3("d3", lo, hi, 64 * j, 64 * j + 64), ja, AF.Relu, bias=-5.0)
        for f in range(lo, hi):
            o, d = a(bank[0], bank[1] + 64 * (f - lo), bank[1] + 64 * (f - lo + 1)), a3("d3", f, f + 1, 0, 64)
            mm(o, i6, d, True, True)
        tt(a3("jf", F + lo, F + hi, 0, 64), a("jb", 64 * lo, 64 * hi), a(bank[0], bank[1], bank[1] + 64 * (hi - lo)), OP.max)
        for k in range(2):
            act(a("pw", 320 * k + 64 * lo, 320 * k + 64 * hi), a3("jf", F * k + lo, F * k + hi, 0, 64), AF.Exp, scale=-LN8)
    ts(i6, ident, 6.0, None, OP.mult)
    places(0, 1, ("u0", 0))
    places(1, SPLIT, ("u0", 64))

    def c5(k, lo=0, hi=5):
        return a("c", 8 * k + lo, 8 * k + hi)
    cn_, tx, tc, lt, m0, m1, kb, isf, sl_, hk, ka, ths, thl, k2 = range(14)
    slc = c5(sl_, 3, 4)

    def tv(k, lo, hi):
        return a("tv", 8 * k + lo, 8 * k + hi)
    ex, eh, s14, vs, v0, v1, ve, v0e, v1m = range(9)

    def short(f):
        return one("st", f)

    def long_(f):
        return one("st", 5 + f)

    def table(k, f):
        return a3("tt", k, k + 1, f, f + 1)

    def place(bank, lo, hi):
        for f in range(lo, hi):
            act(c5(ka, f, f + 1), long_(f), bias=c5(kb, f, f + 1), scale=cl)
            act(one("key", f), short(f), bias=c5(ka, f, f + 1), scale=256.0)
            act(a("dd", 16 * f, 16 * f + 16), i16, scale=one("key", f))
        keys = a(bank, 64 + 16 * lo, 64 + 16 * hi)
        mms([(keys, quar, blank(16 * (hi - lo))), (keys, alls, a("dd", 16 * lo, 16 * hi))])
        for f in range(lo, hi):
            act(a("junk", 16 * f, 16 * f + 16), a(bank, 64 + 16 * f, 80 + 16 * f), AF.Sign, bias=one("key", f), scale=-1.0, acc=one("sg", f))
        act(tv(ex, lo, hi), a("sg", lo, hi), AF.Exp, bias=7.0 * LN8, scale=-LN8 / 2)

    def tables(bank, lo, hi):
        w, sg = hi - lo, a("sg", lo, hi)
        ts(c5(hk, lo, hi), a("key", lo, hi), 0.0, K, OP.is_gt, OP.mult)
        tt(tv(eh, lo, hi), tv(ex, lo, hi), c5(hk, lo, hi), OP.mult)
        ts(tv(s14, lo, hi), sg, 14.0, K, OP.is_equal, OP.mult)
        ts(tv(v1, lo, hi), sg, 12.0, slc, OP.is_equal, OP.mult)
        ts(tv(v1m, lo, hi), sg, 12.0, sm, OP.is_equal, OP.mult)
        for o, i, x in ((vs, eh, s1), (v0, s14, s1), (ve, eh, ee), (v0e, s14, ee)):
            act(tv(o, lo, hi), tv(i, lo, hi), scale=x)
        b = [a(bank, 192 + w * k, 192 + w * k + w) for k in range(5)]
        mms([(a(bank, 192, 192 + 5 * w), alls, a("mst", 0, 5 * w))]
            + [(b[k], m, tv(x, lo, hi)) for k, m, x in ((1, a18, v1), (1, an7, v1), (4, alls, v1m), (0, a18, v0), (1, a7, v0), (3, alls, v0), (0, alls, vs),
                                                        (1, alls, vs), (2, a18, v0e), (3, a8, v0e), (2, alls, ve))])
        tt(a3("tt", 0, 5, lo, hi), a(bank, 192, 192 + 5 * w), a3("arow", 0, 5, lo, hi), OP.add)

    cp(a("ctlb", 0, 25, parts=8), a("ctl", 0, 25, parts=8))
    mm(a("u3", 0, 25), rep, a("ctlb", 0, 25, parts=8), True, True)
    scan(c5(cn_), a("u3", 0, 5), a("one", 0, 5), n1, OP.add, OP.add)
    ts(gz, one("u3", 0), 1.0, 1.0, OP.min, OP.add)
    tt(c5(tx), c5(cn_), a("u3", 10, 25, 3), OP.is_equal)
    ts(c5(lt), c5(cn_), 0.0, None, OP.is_gt)
    ts(cz, one("u3", 5), gz, one("u3", 5), OP.is_le, OP.mult)
    ts(c5(tc, 0, 1), c5(tx, 0, 1), cz, None, OP.mult)
    tt(c5(tc, 1, 5), c5(tx, 1, 5), a("u3", 6, 10), OP.mult)
    tt(a("cq", 1, 5), c5(lt, 1, 5), c5(lt, 0, 4), OP.subtract)
    ts(short(0), c5(tc, 0, 1), 0.0, c5(lt, 0, 1), OP.is_equal, OP.mult)
    ts(long_(0), c5(tc, 0, 1), 1.0, None, OP.is_equal)
    ts(c5(k2), c5(tc), 2.0, None, OP.not_equal)
    act(c5(thl), c5(tc), AF.Abs, bias=-100.0, scale=100.0)
    act(c5(ths), c5(tc), bias=-11.0, scale=-100.0)
    act(c5(thl), c5(thl), bias=-11.0, scale=-1.0)
    tt(c5(m0), c5(cn_), a("u3", 11, 25, 3), OP.is_equal)
    tt(c5(m1), c5(cn_), a("u3", 12, 25, 3), OP.is_equal)
    act(c5(m0), c5(m0), bias=nb1, scale=32.0)
    act(c5(m1), c5(m1), scale=64.0)
    tt(c5(kb), c5(m0), c5(m1), OP.add)
    ts(c5(isf, 0, 4), c5(cn_, 0, 4), 0.0, K, OP.is_equal, OP.mult)
    tt(c5(isf, 4, 8), c5(isf, 0, 4), a("ci", 3, 7), OP.mult)
    act(c5(sl_), c5(lt), bias=1.0, scale=-1.0, acc=ee)
    act(one("st", 10), ee, bias=-1.0)
    scan(c5(sl_, 0, 4), c5(isf, 4, 8), c5(isf, 4, 8), c01, OP.max, OP.max)
    act(sm, slc, AF.Relu, bias=-384.0, scale=192.0 / K)
    act(s1, slc, scale=1.0 / K)
    for f in range(1, F):
        cum, lk = one(("u5", "u1")[f & 1], 256 + f), one("sm", f)
        mms([(cum, ge, one("cq", f)), (cum, n16, one("cq", f)), (cum, alls, long_(f - 1)), (cum, ge, short(f - 1)), (cum, n16, short(f - 1))])
        act(lk, long_(f - 1), scale=c5(k2, f, f + 1))
        ts(short(f), cum, c5(ths, f, f + 1), None, OP.is_le)
        ts(long_(f), cum, c5(thl, f, f + 1), lk, OP.is_le, OP.add)
    total(ee, a("st", 0, 11))
    place("u2", 0, 1)
    f0, f1, fs = [one("f0", k) for k in range(3)]
    ts(h0, one("key", 0), 0.0, c01, OP.is_gt, OP.mult)
    ts(f0, one("sg", 0), 14.0, c01, OP.is_equal, OP.mult)
    ts(f1, one("sg", 0), 12.0, c01, OP.is_equal, OP.mult)
    act(fs, tv(ex, 0, 1), scale=h0)
    ms(a("f0", 4, 6), K)
    ta0, tb0 = one("u2", 0), one("u2", 1)
    mms([(a("u2", 0, 2), mup, a("f0", 4, 6)), (ta0, a18, f0), (tb0, a7, f0), (tb0, a18, f1), (tb0, an7, f1), (ta0, alls, fs), (tb0, alls, fs)])
    place("u4", 1, GROUPS[0][1])
    tables("ix1", *GROUPS[0])

    def ev(f, lo, hi):
        return a("ev", 256 * f + lo, 256 * f + hi)

    def dg(f, k):
        return a("dg", 192 * f + 64 * k, 192 * f + 64 * k + 64)

    def explicit(f):
        nd = a("ix0", 384, 512)
        mms([(nd, unit, blank(128))] + [(a("ix0", 384 + 64 * k, 448 + 64 * k), ni, a3("d3", f, f + 1, 0, 64)) for k in range(2)])
        for k in range(2):
            tt(ev(f, 128 * k, 128 * k + 128), a(("wy", "wx")[k], 128 * f, 128 * f + 128), nd, OP.mult)

    def clamp(lo=0.0):
        ts(a("cb", 0, 256), a("ix0", 0, 256), lo, lo + 31.0, OP.max, OP.min)

    def look(o, f, k, x):
        ts(o, a("pw", 320 * k + 64 * f, 320 * k + 64 * f + 64), x, None, OP.mult)

    def digits(f):
        n = 192 if f < F - 1 else 128
        for k in range(n // 64):
            look(a("ti", 64 * k, 64 * k + 64), f, k & 1, table(k, f))
        ts(a("ta", 0, n), a("ti", 0, n), 7 * 1024, None, OP.bitwise_and)
        cp(a("dg", 192 * f, 192 * f + n), a("ta", 0, n))
        ts(a("moff", 12 * (f - 1), 12 * f), a("mio", 0, 12), table(4, f), None, OP.add)

    def first():
        explicit(0)
        mms([(a("ix0", 0, 256), ident, a("base", 0, 256)), (a("ix0", 0, 256), ident, ev(0, 0, 256))])
        clamp(-192.0)
        mms([(a("ix0", 256, 384), i32, a("cb", 0, 128)), (a("ix0", 256, 384), ident, a("cb", 128, 256))])
        for k, x in enumerate((ta0, tb0, table(2, 0))):
            look(a("ta0", 64 * k, 64 * k + 64), 0, k & 1, x)
        for lo, hi in ((0, 128), (128, 192)):
            ts(a("ta0", lo, hi), a("ta0", lo, hi), 7 * 1024, None, OP.bitwise_and)
        tt(a("o0", 0, 128), a("ta0", 0, 128), a("ix0", 256, 384), OP.add)
        ts(a("off", 0, 128), a("o0", 0, 128), 33.0 * 192, None, OP.add)
        ts(dg(0, 2), a("ta0", 128, 192), 8.0, None, OP.mult)
        tt(a("mst", 192, 256), a("ta0", 0, 64), dg(0, 2), OP.add)
        for k in range(2):
            act(a("mst", 256 + 64 * k, 320 + 64 * k), ev(0, 128 * k, 128 * k + 64))

    def index(f):
        more, m = f < F - 1, 192 * (f + 1)
        explicit(f)
        digits(f)
        tt(a("xb", 0, 192), gi(a("mst", 0, m), a("moff", 12 * (f - 1), 12 * f)), a3("d3", f, f + 1, 0, 192), OP.mult)
        act(a("hv", 0, 128), a("xb", 64, 192), bias=191.75, scale=0.5)
        act(a("zz", 0, 64), a("xb", 0, 64), AF.Relu, bias=-8.0 * K * f)
        ts(a("zz", 64, 128), a("xb", 0, 64), 8.0 * K * f, table(3, f), OP.is_ge, OP.mult)
        code = a("ix1", 0, 64)
        mms([(code, ident, dg(f, 0))] + [(code, i8, dg(f, 2))] * more + [(code, ident, a("zz", 0, 64)), (code, ni, a("zz", 64, 128))])
        y0, y1, x0, x1 = [a("ix0", 64 * k, 64 * k + 64) for k in range(4)]
        hy, hx = a("hv", 0, 64), a("hv", 64, 128)
        mms([(a("ix0", 0, 256), ident, a("base", 0, 256)), (a("ix0", 0, 256), ident, ev(f, 0, 256)), (y1, ni, a("xb", 64, 128)), (x1, ni, a("xb", 128, 192)),
             (y0, ident, hy), (y1, ident, hy), (x0, ident, hx), (x1, ident, hx)])
        act(a("mst", m, m + 64), code)
        act(a("ef", 0, 64), code, bias=192.0 - 7.0 / 16, scale=1.0 / (8 * K))
        clamp()
        op, oq = a("ix0", 256, 320), a("ix0", 320, 384)
        mms([(a("ix0", 256, 384), i32, a("cb", 0, 128)), (a("ix0", 256, 384), ident, a("cb", 128, 256)), (oq, ident, dg(f, 1)),
             (op, ident, a("mst", m, m + 64)), (op, n8k, a("ef", 0, 64))])
        if more:
            mms([(a("ix1", 64, 192), ident, a("hv", 0, 128)), (a("ix1", 64, 128), ident, ev(f, 0, 64)), (a("ix1", 128, 192), ident, ev(f, 128, 192))])
            act(a("mst", m + 64, m + 192), a("ix1", 64, 192), bias=-192.0)
        ts(a("off", 128 * f, 128 * f + 64), op, 192.0 * 8 * K, None, OP.add)
        cp(a("off", 128 * f + 64, 128 * f + 128), oq)

    def preacc(f):
        s, ch = (f + 1) % F, (HAND if f < F - 1 else LAST)["CH"]
        for k in range(len(ch) - 1):
            n = ch[k + 1] - ch[k]
            mm(a("u%d" % k, 0, n), a("wide", 16 * s, 16 * s + 128), a("rs", f * P + ch[k], f * P + ch[k + 1]), True)
            mm(a("u%d" % k, 0, n), quar, blank(n))

    def turn_back(f):
        s = f + 1
        for k, lo, hi in BACK:
            bank = a("u%d" % k, 0, hi - lo)
            mm(bank, a("wide", 128 - 16 * s, 256 - 16 * s), made(f, lo, hi), True, True)
            act(slot(3 + f, lo, hi), bank)

    def pixels(f):
        s, how = (f + 1) % F, (HAND if f < F - 1 else LAST)
        ch, win, summed = how["CH"], a("win", 0, (4 + f) * P), []

        def gather(x):
            i, k = "pq".index(x[0]), int(x[1])
            o = 128 * f + 64 * i
            return a("pq", P * i + ch[k], P * i + ch[k + 1]), gi(win, a("off", o + ch[k] // 16, o + ch[k + 1] // 16))

        def add_up(k):
            n = ch[k + 1] - ch[k]
            terms = [(a("half", 16 * s, 16 * s + 128), gather(x)[0]) for x in (how["V"] + " " + how["S"]).split() if x in ("p%d" % k, "q%d" % k)]
            if "c%d" % k in how["V"]:
                terms += [(mup, blank(n)), (mdn, blank(n))]
            for j, (l, r) in enumerate(terms):
                mm(a("u%d" % k, 0, n), l, r, False, j == len(terms) - 1)
            summed.append(k)
        line.update(v=[], s=[], t=[])
        for x in how["S"].split():
            act(*gather(x))
        for x in how["V"].split():
            k = int(x[1])
            acc, near = a("u%d" % k, 0, ch[k + 1] - ch[k]), a("cr", ch[k], ch[k + 1])
            if x[0] in "pq":
                cp(*gather(x))
                continue
            for j in range(len(summed), k + 1):
                add_up(j)
            if x[0] == "r":
                ts(near, acc, MAGIC, MAGIC, OP.add, OP.subtract)
                continue
            ts(made(f, ch[k], ch[k + 1]), near if x[0] == "m" else acc, 0.0, 255.0, OP.max, OP.min)
            if x in how["OUT"]:
                lo, hi = how["OUT"][x]
                if f < F - 1:
                    send(f + 1, int(hi == P), slot(4 + f, lo, hi), made(f, lo, hi))
                else:
                    store(f * P + lo, f * P + hi, made(f, lo, hi))
        line.clear()

    first()
    later(0)
    for f in range(F):
        preacc(f)
        pixels(f)
        if f < F - 1:
            turn_back(f)
            later(f + 1)
            if f + 1 == SPLIT < F:
                places(SPLIT, F, ("ix1", 256))
            if f + 1 == GROUPS[1][0] - 1:
                place("ix1", *GROUPS[1])
                tables("ix1", *GROUPS[1])
            index(f + 1)

    issue()
    for sem in cnt:
        need("y", (sem, cnt[sem], {}))
    for sem in LOADS:
        need("y", (sem, 16, {}))
    for sem in sends:
        need("y", (sem, nout, {}))
    need("y", ("stored", stores[0], {}))
